import numpy as np
import ml_dtypes


def mxq(x, axis, fmt="e4m3"):
    dtype, down = {"e4m3": (ml_dtypes.float8_e4m3fn, 7), "e5m2": (ml_dtypes.float8_e5m2, 14)}[fmt]
    v = np.moveaxis(np.asarray(x, np.float32).astype(ml_dtypes.bfloat16).astype(np.float64), axis, -1)
    blocks = v.reshape(v.shape[:-1] + (-1, 32))
    amax = np.abs(blocks).max(-1, keepdims=True)
    byte = np.maximum(np.where(amax > 0, np.frexp(amax)[1] - 1 + 127, 0) - down, 1)
    scale = np.exp2(byte - 127.0)
    codes = (blocks / scale).astype(np.float32).astype(dtype).astype(np.float64)
    return np.moveaxis((codes * scale).reshape(v.shape), -1, axis)


WIDE = False


def mx_kscale(k):
    if not WIDE:
        return np.ones(k)
    levels = np.array([10, -10, 5, -5, 0])
    if k % 512:
        return np.exp2(np.random.permutation(np.resize(levels, k // 32))).repeat(32)
    a = np.empty((k // 512, 16))
    for p in range(k // 512):
        a[p, :8] = np.random.permutation(np.resize(levels, 8))
        for g in range(8):
            far = levels[np.abs(levels - a[p, g]) >= 10]
            a[p, g + 8] = far[np.random.randint(len(far))]
    return np.exp2(a.ravel()).repeat(32)


def f64(x):
    return np.asarray(x).astype(np.float64)


def striped(idx):
    return np.tile(np.asarray(idx).reshape(-1, 16).T, (8, 1)).astype(np.uint16)


def unstriped(offs):
    return offs[:16].T.reshape(-1).astype(np.int64)


E2M1 = np.array([0.0, 0.5, 1.0, 1.5, 2.0, 3.0, 4.0, 6.0, -0.0, -0.5, -1.0, -1.5, -2.0, -3.0, -4.0, -6.0])


def pack_weight(w, fmt):
    k, n = w.shape
    w = f64(np.asarray(w, np.float32).astype(ml_dtypes.bfloat16)).reshape(k // 32, 32, n)
    amax = np.abs(w).max(1)
    if fmt == "e4m3":
        byte = np.frexp(amax)[1] - 1 + 127 - 7
    else:
        mant, ex = np.frexp(amax / 6.0)
        byte = np.where(mant > 0.5, ex, ex - 1) + 127
    byte = np.clip(np.where(amax > 0, byte, 1), 1, 254)
    scaled = (w * np.exp2(127.0 - byte)[:, None, :]).reshape(k, n).astype(np.float32)
    by_word = np.ascontiguousarray(scaled.reshape(k // 512, 128, 4, n).transpose(0, 1, 3, 2))
    if fmt == "e4m3":
        words = by_word.astype(ml_dtypes.float8_e4m3fn).view(np.uint8)
    else:
        c = by_word.astype(ml_dtypes.float4_e2m1fn).view(np.uint8) & 0xF
        words = (c[..., 0::2] | (c[..., 1::2] << 4)).reshape(k // 512, 128, 2 * n)
    return np.ascontiguousarray(words), np.ascontiguousarray(byte.astype(np.uint8).reshape(k // 512, 16, n))


def unpack_weight(words, scales, fmt):
    g, _, n = scales.shape
    words = np.ascontiguousarray(words).reshape(g, 128, n, -1)
    if fmt == "e4m3":
        vals = words.view(ml_dtypes.float8_e4m3fn).astype(np.float64)
    else:
        nib = np.empty((g, 128, n, 4), np.uint8)
        nib[..., 0::2] = words & 0xF
        nib[..., 1::2] = words >> 4
        vals = E2M1[nib]
    vals = vals * np.repeat(np.exp2(scales.astype(np.float64) - 127.0), 8, axis=1)[..., None]
    return vals.transpose(0, 1, 3, 2).reshape(g * 512, n)


def sigmoid(v):
    return 1.0 / (1.0 + np.exp(-v))


B, N, T, D, NQ = 1, 512, 2048, 512, 512
DV = 512


def sgn(shape):
    return np.random.uniform(0.5, 2.0, shape) * np.where(np.random.standard_normal(shape) < 0, -1.0, 1.0)


def setup_inputs():
    n = np.random.standard_normal
    idx = np.random.permutation(T)[:B * N]
    s = mx_kscale(D)[:, None]
    u = mx_kscale(N)
    ut = np.ones(T)
    ut[idx] = u
    kp = pack_weight(n((D, T)) / s, "e4m3")
    cp = pack_weight(n((D, T)) / s / 12, "e4m3")
    return {
        "qT": (n((B, D, NQ)) * s * (1.00 / np.sqrt(D))).astype(np.float32),
        "k_words": kp[0],
        "k_scales": kp[1],
        "c_words": cp[0],
        "c_scales": cp[1],
        "vT": (n((DV, T)) / ut).astype(np.float32),
        "th": (n((B, 1, NQ)) + 1).astype(np.float32),
        "us": (sgn((B, N, 1)) * u[:, None]).astype(np.float32),
        "offs": striped(idx),
    }


def reference(qT, k_words, k_scales, c_words, c_scales, vT, th, us, offs):
    idx = unstriped(offs)
    pick = lambda x, which: x[:, which].reshape(x.shape[0], B, -1).transpose(1, 0, 2)
    k = unpack_weight(k_words, k_scales, "e4m3")
    kg = pick(k, idx)
    c = unpack_weight(c_words, c_scales, "e4m3")
    cg = pick(c, idx)
    qq = mxq(f64(qT), 1, "e4m3")
    a = (kg.transpose(0, 2, 1) @ qq) + (cg.transpose(0, 2, 1) @ qq)
    y = sigmoid(a - f64(th)) * f64(us)
    wq = mxq(y, 1, "e4m3")
    o = wq.transpose(0, 2, 1) @ mxq(pick(f64(vT), idx).transpose(0, 2, 1), 1, "e4m3")
    ms = np.mean(np.square(o), axis=-1, keepdims=True)
    r_ = o / np.sqrt(ms + 1e-05)
    return r_

@@ -1,0 +1,193 @@
+import math
+from contextlib import ExitStack
+
+import concourse.mybir as mybir
+from concourse.masks import make_identity
+
+F32 = mybir.dt.float32
+BF16 = mybir.dt.bfloat16
+I32 = mybir.dt.int32
+U32 = mybir.dt.uint32
+U16 = mybir.dt.uint16
+U8 = mybir.dt.uint8
+FP8X4 = mybir.dt.float8_e4m3fn_x4
+ACT = mybir.ActivationFunctionType
+ALU = mybir.AluOpType
+
+P = 128
+PACK = 4
+SLOTS = 512
+TOKENS = 2048
+QUERIES = 512
+DV = 512
+Q_TILES = QUERIES // P
+V_TILES = DV // P
+EPS = 1e-05
+C_ROW = 4
+Q_SPLIT = 80
+
+FLOPS = 3 * 2 * 512 * 512 * 512
+
+
+def tile_attend_at_residsig_topk_kernel(tc, qT, k_words, k_scales, c_words, c_scales, vT, th, us, offs, out):
+    nc = tc.nc
+    with ExitStack() as ctx:
+        keep = ctx.enter_context(tc.tile_pool(name="keep", bufs=1))
+        psum = ctx.enter_context(tc.psum_pool(name="psum", bufs=1))
+        turn = ctx.enter_context(tc.psum_pool(name="turn", bufs=2))
+
+        offsets = keep.tile([P, SLOTS // 16], U16, name="offsets")
+        k_scale_pool = keep.tile([P, TOKENS], U8, name="k_scale_pool")
+        c_scale_pool = keep.tile([P, TOKENS], U8, name="c_scale_pool")
+        nc.gpsimd.memset(k_scale_pool[:].bitcast(I32), 0)
+        nc.gpsimd.memset(c_scale_pool[:].bitcast(I32), 0)
+
+        q_raw = keep.tile([P, PACK, QUERIES], F32, name="q_raw")
+        k_pool = keep.tile([P, TOKENS], I32, name="k_pool")
+        c_pool = keep.tile([P, TOKENS], I32, name="c_pool")
+        v_pool = [keep.tile([P, TOKENS], F32, name="v_pool%d" % e) for e in range(V_TILES)]
+        th_col = keep.tile([P, Q_TILES], F32, name="th_col")
+        us_col = keep.tile([P, PACK], F32, name="us_col")
+
+        nc.sync.dma_start(k_pool[:], k_words[0].rearrange("p n t -> p (n t)").bitcast(I32))
+        nc.sync.dma_start(offsets[:], offs)
+        nc.sync.dma_start(th_col[:], th[0, 0].rearrange("(m j) -> m j", j=Q_TILES))
+        nc.sync.dma_start(us_col[:], us[0].rearrange("(p t) o -> p (t o)", t=PACK))
+        k_rows = k_scales[0].bitcast(I32).rearrange("(g r) n -> r g n", r=4)
+        c_rows = c_scales[0].bitcast(I32).rearrange("(g r) n -> r g n", r=4)
+        for r in range(4):
+            nc.scalar.dma_start(k_scale_pool[r:P:32, :].bitcast(I32), k_rows[r])
+        for r in range(4):
+            nc.scalar.dma_start(c_scale_pool[C_ROW + r:P:32, :].bitcast(I32), c_rows[r])
+        nc.gpsimd.dma_start(q_raw[:], qT[0].rearrange("(p t) q -> p t q", t=PACK))
+        ident = keep.tile([P, P], F32, name="ident")
+        make_identity(nc, ident[:])
+        nc.gpsimd.dma_start(c_pool[:], c_words[0].rearrange("p n t -> p (n t)").bitcast(I32))
+        for e in range(V_TILES):
+            nc.gpsimd.dma_start(v_pool[e][:], vT[e * P:(e + 1) * P, :])
+
+        warm = keep.tile([P, 8], F32, name="warm")
+        warm_out = keep.tile([P, 8], F32, name="warm_out")
+        nc.vector.memset(warm[:], 0.0)
+        nc.scalar.activation(warm_out[:, 0:1], warm[:, 0:1], ACT.Sigmoid)
+
+        neg_th = keep.tile([P, Q_TILES], F32, name="neg_th")
+        nc.vector.tensor_scalar(neg_th[:], th_col[:], -1.0, None, ALU.mult)
+
+        q_bf = keep.tile([P, Q_TILES, P, PACK], BF16, name="q_bf", align_bytes=64)
+        q_dst = q_bf[:].rearrange("p j m t -> p m j t")
+        q_src = q_raw[:].rearrange("p t (m j) -> p m j t", j=Q_TILES)
+        nc.scalar.copy(q_dst[:, :Q_SPLIT], q_src[:, :Q_SPLIT])
+
+        k_codes = keep.tile([P, SLOTS], U32, name="k_codes", align_bytes=64)
+        k_bytes = keep.tile([P, SLOTS], U8, name="k_bytes", align_bytes=64)
+        c_codes = keep.tile([P, SLOTS], U32, name="c_codes", align_bytes=64)
+        c_bytes = keep.tile([P, SLOTS], U8, name="c_bytes", align_bytes=64)
+        q_codes = keep.tile([P, QUERIES], U32, name="q_codes", align_bytes=64)
+        q_bytes = keep.tile([P, QUERIES], U8, name="q_bytes", align_bytes=64)
+        nc.vector.tensor_copy(k_codes[:], k_pool[:].bitcast(U32).indirect(offsets[:]))
+        nc.vector.tensor_copy(k_bytes[:], k_scale_pool[:].indirect(offsets[:]))
+        nc.vector.tensor_copy(c_bytes[:], c_scale_pool[:].indirect(offsets[:]))
+        nc.vector.tensor_copy(q_dst[:, Q_SPLIT:], q_src[:, Q_SPLIT:])
+        nc.vector.quantize_mx(out=q_codes[:].bitcast(FP8X4), scales=q_bytes[:], in_=q_bf[:].rearrange("p j m t -> p (j m t)"))
+        nc.vector.tensor_copy(c_codes[:], c_pool[:].bitcast(U32).indirect(offsets[:]))
+
+        scores = []
+        for j in range(Q_TILES):
+            score = psum.tile([P, SLOTS], F32, name="score%d" % j, tag="rows%d" % j)
+            cols = slice(j * P, (j + 1) * P)
+            nc.tensor.matmul_mx(out=score[:], lhsT=q_codes[:, cols].bitcast(FP8X4), lhsT_scale=q_bytes[:, cols],
+                                rhs=k_codes[:].bitcast(FP8X4), rhs_scale=k_bytes[:], start=True, stop=False)
+            scores.append(score)
+        for j in range(Q_TILES):
+            cols = slice(j * P, (j + 1) * P)
+            nc.tensor.matmul_mx(out=scores[j][:], lhsT=q_codes[:, cols].bitcast(FP8X4), lhsT_scale=q_bytes[:, cols],
+                                rhs=c_codes[:].bitcast(FP8X4), rhs_scale=c_bytes[C_ROW:P, :], start=False, stop=True)
+
+        v_codes = keep.tile([P, DV], U32, name="v_codes", align_bytes=64)
+        v_bytes = keep.tile([P, DV], U8, name="v_bytes", align_bytes=64)
+        v_bf = keep.tile([P, DV, PACK], BF16, name="v_bf", align_bytes=64)
+
+        def turn_values(e):
+            picked = keep.tile([P, 2, P, 2], BF16, name="picked%d" % e)
+            nc.vector.tensor_copy(picked[:].rearrange("e u p b -> e p u b"), v_pool[e][:].indirect(offsets[:]))
+            words = picked[:].rearrange("e u p b -> e (u p b)").bitcast(F32)
+            turned = turn.tile([P, 2, P], F32, name="v_turned", tag="v_turned")
+            for u in range(2):
+                nc.tensor.transpose(turned[:, u, :], words[:, u * P:(u + 1) * P], ident[:])
+            dst = v_bf[:, e * P:(e + 1) * P, :].rearrange("p e t -> p (e t)").bitcast(F32)
+            nc.scalar.copy(dst.rearrange("p (e u) -> p e u", u=2), turned[:].rearrange("p u e -> p e u"))
+
+        def quantize_values(lo, hi):
+            nc.vector.quantize_mx(out=v_codes[:, lo:hi].bitcast(FP8X4), scales=v_bytes[:, lo:hi],
+                                  in_=v_bf[:, lo:hi, :].rearrange("p e t -> p (e t)"))
+
+        y_bf = keep.tile([P, QUERIES, PACK], BF16, name="y_bf", align_bytes=64)
+        y_codes = keep.tile([P, QUERIES], U32, name="y_codes", align_bytes=64)
+        y_bytes = keep.tile([P, QUERIES], U8, name="y_bytes", align_bytes=64)
+        sigs = []
+
+        def weigh(j):
+            sig = keep.tile([P, PACK, P], F32, name="sig%d" % j)
+            nc.scalar.activation(sig[:], scores[j][:].rearrange("q (p t) -> q t p", t=PACK), ACT.Sigmoid, bias=neg_th[:, j:j + 1])
+            turned = turn.tile([P, PACK, P], F32, name="y_turned", tag="y_turned")
+            for t in range(PACK):
+                nc.tensor.transpose(turned[:, t, :], sig[:, t, :], ident[:])
+            nc.vector.tensor_tensor(y_bf[:, j * P:(j + 1) * P, :], turned[:].rearrange("p t q -> p q t"),
+                                    us_col[:].unsqueeze(1).to_broadcast([P, P, PACK]), ALU.mult)
+            sigs.append(sig)
+
+        def quantize_weights(lo, hi):
+            nc.vector.quantize_mx(out=y_codes[:, lo:hi].bitcast(FP8X4), scales=y_bytes[:, lo:hi],
+                                  in_=y_bf[:, lo:hi, :].rearrange("p q t -> p (q t)"))
+
+        weigh(0)
+        weigh(1)
+        turn_values(0)
+        weigh(2)
+        quantize_weights(0, 2 * P)
+        weigh(3)
+        nc.scalar.activation(warm_out[:, 1:2], sigs[3][:, 0, 0:1], ACT.Abs_reciprocal_sqrt, bias=1.0)
+        turn_values(1)
+        quantize_weights(2 * P, 4 * P)
+
+        sums = [psum.tile([P, DV], F32, name="sum%d" % j, tag="rows%d" % j) for j in range(Q_TILES)]
+        squares = keep.tile([P, 2 * P], F32, name="squares")
+        parts = [keep.tile([P, Q_TILES], F32, name="part%d" % i) for i in range(3)]
+
+        def multiply(lo, hi):
+            for j in range(Q_TILES):
+                cols = slice(j * P, (j + 1) * P)
+                nc.tensor.matmul_mx(out=sums[j][:, lo:hi], lhsT=y_codes[:, cols].bitcast(FP8X4), lhsT_scale=y_bytes[:, cols],
+                                    rhs=v_codes[:, lo:hi].bitcast(FP8X4), rhs_scale=v_bytes[:, lo:hi], start=True, stop=True)
+
+        def mean_square(j, lo, hi, part):
+            nc.scalar.activation(squares[:, 0:hi - lo], sums[j][:, lo:hi], ACT.Square, scale=1.0 / math.sqrt(DV),
+                                 accum_out=part[:, j:j + 1])
+
+        quantize_values(0, 2 * P)
+        multiply(0, 2 * P)
+        for j in range(Q_TILES):
+            mean_square(j, 0, 2 * P, parts[0])
+        turn_values(2)
+        quantize_values(2 * P, 3 * P)
+        multiply(2 * P, 3 * P)
+        for j in range(Q_TILES):
+            mean_square(j, 2 * P, 3 * P, parts[1])
+        early = keep.tile([P, Q_TILES], F32, name="early")
+        nc.vector.scalar_tensor_tensor(early[:], parts[0][:], EPS, parts[1][:], ALU.add, ALU.add)
+        turn_values(3)
+        quantize_values(3 * P, 4 * P)
+        multiply(3 * P, 4 * P)
+
+        rows = out[0].rearrange("(m j) e -> j m e", j=Q_TILES)
+        for j in range(Q_TILES):
+            mean_square(j, 3 * P, 4 * P, parts[2])
+            gain = keep.tile([P, 1], F32, name="gain%d" % j)
+            nc.scalar.activation(gain[:], parts[2][:, j:j + 1], ACT.Abs_reciprocal_sqrt, bias=early[:, j:j + 1])
+            result = keep.tile([P, DV], F32, name="result%d" % j)
+            if j < 3:
+                nc.vector.tensor_scalar(result[:], sums[j][:], gain[:], None, ALU.mult)
+            else:
+                nc.scalar.activation(result[:], sums[j][:], ACT.Copy, scale=gain[:])
+            nc.sync.dma_start(rows[j], result[:])

@@ -37,51 +37,47 @@ def tile_attend_at_residsig_topk_kernel(tc, qT, k_words, k_scales, c_words, c_sc
         turn = ctx.enter_context(tc.psum_pool(name="turn", bufs=2))
 
         offsets = keep.tile([P, SLOTS // 16], U16, name="offsets")
-        k_scale_pool = keep.tile([P, TOKENS], U8, name="k_scale_pool")
-        c_scale_pool = keep.tile([P, TOKENS], U8, name="c_scale_pool")
+        k_scale_pool = keep.tile([P, TOKENS], U8, name="k_scale_pool", tag="stage1")
+        c_scale_pool = keep.tile([P, TOKENS], U8, name="c_scale_pool", tag="stage2")
         nc.gpsimd.memset(k_scale_pool[:].bitcast(I32), 0)
-        nc.gpsimd.memset(c_scale_pool[:].bitcast(I32), 0)
+        nc.vector.memset(c_scale_pool[:].bitcast(I32), 0)
 
-        q_raw = keep.tile([P, PACK, QUERIES], F32, name="q_raw")
-        k_pool = keep.tile([P, TOKENS], I32, name="k_pool")
-        c_pool = keep.tile([P, TOKENS], I32, name="c_pool")
-        v_pool = [keep.tile([P, TOKENS], F32, name="v_pool%d" % e) for e in range(V_TILES)]
+        q_raw = keep.tile([P, PACK, QUERIES], F32, name="q_raw", tag="stage3")
+        k_pool = keep.tile([P, TOKENS], I32, name="k_pool", tag="stage0")
+        c_pool = keep.tile([P, TOKENS], I32, name="c_pool", tag="after_c", align_bytes=64)
         th_col = keep.tile([P, Q_TILES], F32, name="th_col")
         us_col = keep.tile([P, PACK], F32, name="us_col")
 
         nc.sync.dma_start(k_pool[:], k_words[0].rearrange("p n t -> p (n t)").bitcast(I32))
         nc.sync.dma_start(offsets[:], offs)
-        nc.sync.dma_start(th_col[:], th[0, 0].rearrange("(m j) -> m j", j=Q_TILES))
-        nc.sync.dma_start(us_col[:], us[0].rearrange("(p t) o -> p (t o)", t=PACK))
+        nc.sync.dma_start(q_raw[:], qT[0].rearrange("(p t) q -> p t q", t=PACK))
+        nc.sync.dma_start(c_pool[:], c_words[0].rearrange("p n t -> p (n t)").bitcast(I32))
         k_rows = k_scales[0].bitcast(I32).rearrange("(g r) n -> r g n", r=4)
         c_rows = c_scales[0].bitcast(I32).rearrange("(g r) n -> r g n", r=4)
         for r in range(4):
             nc.scalar.dma_start(k_scale_pool[r:P:32, :].bitcast(I32), k_rows[r])
         for r in range(4):
-            nc.scalar.dma_start(c_scale_pool[C_ROW + r:P:32, :].bitcast(I32), c_rows[r])
-        nc.gpsimd.dma_start(q_raw[:], qT[0].rearrange("(p t) q -> p t q", t=PACK))
+            queue = nc.scalar if r < 2 else nc.gpsimd
+            queue.dma_start(c_scale_pool[C_ROW + r:P:32, :].bitcast(I32), c_rows[r])
+        nc.gpsimd.dma_start(th_col[:], th[0, 0].rearrange("(m j) -> m j", j=Q_TILES))
+        nc.gpsimd.dma_start(us_col[:], us[0].rearrange("(p t) o -> p (t o)", t=PACK))
         ident = keep.tile([P, P], F32, name="ident")
         make_identity(nc, ident[:])
-        nc.gpsimd.dma_start(c_pool[:], c_words[0].rearrange("p n t -> p (n t)").bitcast(I32))
-        for e in range(V_TILES):
-            nc.gpsimd.dma_start(v_pool[e][:], vT[e * P:(e + 1) * P, :])
 
         warm = keep.tile([P, 8], F32, name="warm")
         warm_out = keep.tile([P, 8], F32, name="warm_out")
         nc.vector.memset(warm[:], 0.0)
         nc.scalar.activation(warm_out[:, 0:1], warm[:, 0:1], ACT.Sigmoid)
 
-        neg_th = keep.tile([P, Q_TILES], F32, name="neg_th")
-        nc.vector.tensor_scalar(neg_th[:], th_col[:], -1.0, None, ALU.mult)
-
-        q_bf = keep.tile([P, Q_TILES, P, PACK], BF16, name="q_bf", align_bytes=64)
+        q_bf = keep.tile([P, Q_TILES, P, PACK], BF16, name="q_bf", tag="after_q", align_bytes=64)
         q_dst = q_bf[:].rearrange("p j m t -> p m j t")
         q_src = q_raw[:].rearrange("p t (m j) -> p m j t", j=Q_TILES)
         nc.scalar.copy(q_dst[:, :Q_SPLIT], q_src[:, :Q_SPLIT])
+        neg_th = keep.tile([P, Q_TILES], F32, name="neg_th")
+        nc.scalar.mul(neg_th[:], th_col[:], -1.0)
 
         k_codes = keep.tile([P, SLOTS], U32, name="k_codes", align_bytes=64)
         k_bytes = keep.tile([P, SLOTS], U8, name="k_bytes", align_bytes=64)
-        c_codes = keep.tile([P, SLOTS], U32, name="c_codes", align_bytes=64)
         c_bytes = keep.tile([P, SLOTS], U8, name="c_bytes", align_bytes=64)
         q_codes = keep.tile([P, QUERIES], U32, name="q_codes", align_bytes=64)
         q_bytes = keep.tile([P, QUERIES], U8, name="q_bytes", align_bytes=64)
@@ -90,7 +86,14 @@ def tile_attend_at_residsig_topk_kernel(tc, qT, k_words, k_scales, c_words, c_sc
         nc.vector.tensor_copy(c_bytes[:], c_scale_pool[:].indirect(offsets[:]))
         nc.vector.tensor_copy(q_dst[:, Q_SPLIT:], q_src[:, Q_SPLIT:])
         nc.vector.quantize_mx(out=q_codes[:].bitcast(FP8X4), scales=q_bytes[:], in_=q_bf[:].rearrange("p j m t -> p (j m t)"))
+        c_codes = keep.tile([P, SLOTS], U32, name="c_codes", tag="after_q", align_bytes=64)
         nc.vector.tensor_copy(c_codes[:], c_pool[:].bitcast(U32).indirect(offsets[:]))
+
+        v_pool = []
+        for e in range(V_TILES):
+            rows_in = keep.tile([P, TOKENS], F32, name="v_pool%d" % e, tag="stage%d" % e)
+            nc.sync.dma_start(rows_in[:], vT[e * P:(e + 1) * P, :])
+            v_pool.append(rows_in)
 
         scores = []
         for j in range(Q_TILES):
@@ -106,26 +109,26 @@ def tile_attend_at_residsig_topk_kernel(tc, qT, k_words, k_scales, c_words, c_sc
 
         v_codes = keep.tile([P, DV], U32, name="v_codes", align_bytes=64)
         v_bytes = keep.tile([P, DV], U8, name="v_bytes", align_bytes=64)
-        v_bf = keep.tile([P, DV, PACK], BF16, name="v_bf", align_bytes=64)
+        v_bf = [keep.tile([P, 2 * P, PACK], BF16, name="v_bf%d" % h, tag="v_bf%d" % h, align_bytes=64) for h in range(2)]
+        y_bf = [keep.tile([P, 2 * P, PACK], BF16, name="y_bf%d" % h, tag="y_bf%d" % h, align_bytes=64) for h in range(2)]
+        y_codes = keep.tile([P, QUERIES], U32, name="y_codes", align_bytes=64)
+        y_bytes = keep.tile([P, QUERIES], U8, name="y_bytes", align_bytes=64)
+        sigs = []
 
-        def turn_values(e):
-            picked = keep.tile([P, 2, P, 2], BF16, name="picked%d" % e)
+        def turn_values(e, tag, align):
+            picked = keep.tile([P, 2, P, 2], BF16, name="picked%d" % e, tag=tag, align_bytes=align)
             nc.vector.tensor_copy(picked[:].rearrange("e u p b -> e p u b"), v_pool[e][:].indirect(offsets[:]))
             words = picked[:].rearrange("e u p b -> e (u p b)").bitcast(F32)
             turned = turn.tile([P, 2, P], F32, name="v_turned", tag="v_turned")
             for u in range(2):
                 nc.tensor.transpose(turned[:, u, :], words[:, u * P:(u + 1) * P], ident[:])
-            dst = v_bf[:, e * P:(e + 1) * P, :].rearrange("p e t -> p (e t)").bitcast(F32)
+            dst = v_bf[e // 2][:, (e % 2) * P:(e % 2 + 1) * P, :].rearrange("p e t -> p (e t)").bitcast(F32)
             nc.scalar.copy(dst.rearrange("p (e u) -> p e u", u=2), turned[:].rearrange("p u e -> p e u"))
 
-        def quantize_values(lo, hi):
-            nc.vector.quantize_mx(out=v_codes[:, lo:hi].bitcast(FP8X4), scales=v_bytes[:, lo:hi],
-                                  in_=v_bf[:, lo:hi, :].rearrange("p e t -> p (e t)"))
-
-        y_bf = keep.tile([P, QUERIES, PACK], BF16, name="y_bf", align_bytes=64)
-        y_codes = keep.tile([P, QUERIES], U32, name="y_codes", align_bytes=64)
-        y_bytes = keep.tile([P, QUERIES], U8, name="y_bytes", align_bytes=64)
-        sigs = []
+        def quantize_half(codes, scale_bytes, halves, h):
+            cols = slice(2 * h * P, 2 * (h + 1) * P)
+            nc.vector.quantize_mx(out=codes[:, cols].bitcast(FP8X4), scales=scale_bytes[:, cols],
+                                  in_=halves[h][:].rearrange("p c t -> p (c t)"))
 
         def weigh(j):
             sig = keep.tile([P, PACK, P], F32, name="sig%d" % j)
@@ -133,61 +136,50 @@ def tile_attend_at_residsig_topk_kernel(tc, qT, k_words, k_scales, c_words, c_sc
             turned = turn.tile([P, PACK, P], F32, name="y_turned", tag="y_turned")
             for t in range(PACK):
                 nc.tensor.transpose(turned[:, t, :], sig[:, t, :], ident[:])
-            nc.vector.tensor_tensor(y_bf[:, j * P:(j + 1) * P, :], turned[:].rearrange("p t q -> p q t"),
+            nc.vector.tensor_tensor(y_bf[j // 2][:, (j % 2) * P:(j % 2 + 1) * P, :], turned[:].rearrange("p t q -> p q t"),
                                     us_col[:].unsqueeze(1).to_broadcast([P, P, PACK]), ALU.mult)
             sigs.append(sig)
 
-        def quantize_weights(lo, hi):
-            nc.vector.quantize_mx(out=y_codes[:, lo:hi].bitcast(FP8X4), scales=y_bytes[:, lo:hi],
-                                  in_=y_bf[:, lo:hi, :].rearrange("p q t -> p (q t)"))
+        squares = keep.tile([P, Q_TILES, 2 * P], F32, name="squares")
+        parts = [keep.tile([P, Q_TILES], F32, name="part%d" % h) for h in range(2)]
 
-        weigh(0)
-        weigh(1)
-        turn_values(0)
-        weigh(2)
-        quantize_weights(0, 2 * P)
-        weigh(3)
-        nc.scalar.activation(warm_out[:, 1:2], sigs[3][:, 0, 0:1], ACT.Abs_reciprocal_sqrt, bias=1.0)
-        turn_values(1)
-        quantize_weights(2 * P, 4 * P)
-
-        sums = [psum.tile([P, DV], F32, name="sum%d" % j, tag="rows%d" % j) for j in range(Q_TILES)]
-        squares = keep.tile([P, 2 * P], F32, name="squares")
-        parts = [keep.tile([P, Q_TILES], F32, name="part%d" % i) for i in range(3)]
-
-        def multiply(lo, hi):
+        def multiply(h):
+            half = slice(2 * h * P, 2 * (h + 1) * P)
             for j in range(Q_TILES):
                 cols = slice(j * P, (j + 1) * P)
-                nc.tensor.matmul_mx(out=sums[j][:, lo:hi], lhsT=y_codes[:, cols].bitcast(FP8X4), lhsT_scale=y_bytes[:, cols],
-                                    rhs=v_codes[:, lo:hi].bitcast(FP8X4), rhs_scale=v_bytes[:, lo:hi], start=True, stop=True)
+                nc.tensor.matmul_mx(out=sums[j][:, half], lhsT=y_codes[:, cols].bitcast(FP8X4), lhsT_scale=y_bytes[:, cols],
+                                    rhs=v_codes[:, half].bitcast(FP8X4), rhs_scale=v_bytes[:, half], start=True, stop=True)
 
-        def mean_square(j, lo, hi, part):
-            nc.scalar.activation(squares[:, 0:hi - lo], sums[j][:, lo:hi], ACT.Square, scale=1.0 / math.sqrt(DV),
-                                 accum_out=part[:, j:j + 1])
+        def mean_square(j, h):
+            nc.scalar.activation(squares[:, j, :], sums[j][:, 2 * h * P:2 * (h + 1) * P], ACT.Square, scale=1.0 / math.sqrt(DV),
+                                 accum_out=parts[h][:, j:j + 1])
 
-        quantize_values(0, 2 * P)
-        multiply(0, 2 * P)
+        turn_values(0, "after_c", 64)
+        weigh(0)
+        weigh(1)
+        quantize_half(y_codes, y_bytes, y_bf, 0)
+        turn_values(1, "y_bf0", 64)
+        weigh(2)
+        weigh(3)
+        nc.scalar.activation(warm_out[:, 1:2], sigs[3][:, 0, 0:1], ACT.Abs_reciprocal_sqrt, bias=1.0)
+        quantize_half(y_codes, y_bytes, y_bf, 1)
+        quantize_half(v_codes, v_bytes, v_bf, 0)
+        sums = [psum.tile([P, DV], F32, name="sum%d" % j, tag="rows%d" % j) for j in range(Q_TILES)]
+        multiply(0)
+        turn_values(2, "v_bf0", 64)
         for j in range(Q_TILES):
-            mean_square(j, 0, 2 * P, parts[0])
-        turn_values(2)
-        quantize_values(2 * P, 3 * P)
-        multiply(2 * P, 3 * P)
-        for j in range(Q_TILES):
-            mean_square(j, 2 * P, 3 * P, parts[1])
+            mean_square(j, 0)
         early = keep.tile([P, Q_TILES], F32, name="early")
-        nc.vector.scalar_tensor_tensor(early[:], parts[0][:], EPS, parts[1][:], ALU.add, ALU.add)
-        turn_values(3)
-        quantize_values(3 * P, 4 * P)
-        multiply(3 * P, 4 * P)
+        nc.gpsimd.tensor_scalar(early[:], parts[0][:], 1.0, EPS, ALU.mult, ALU.add)
+        turn_values(3, "y_bf1", 64)
+        quantize_half(v_codes, v_bytes, v_bf, 1)
+        multiply(1)
 
         rows = out[0].rearrange("(m j) e -> j m e", j=Q_TILES)
         for j in range(Q_TILES):
-            mean_square(j, 3 * P, 4 * P, parts[2])
+            mean_square(j, 1)
             gain = keep.tile([P, 1], F32, name="gain%d" % j)
-            nc.scalar.activation(gain[:], parts[2][:, j:j + 1], ACT.Abs_reciprocal_sqrt, bias=early[:, j:j + 1])
+            nc.scalar.activation(gain[:], parts[1][:, j:j + 1], ACT.Abs_reciprocal_sqrt, bias=early[:, j:j + 1])
             result = keep.tile([P, DV], F32, name="result%d" % j)
-            if j < 3:
-                nc.vector.tensor_scalar(result[:], sums[j][:], gain[:], None, ALU.mult)
-            else:
-                nc.scalar.activation(result[:], sums[j][:], ACT.Copy, scale=gain[:])
+            nc.vector.tensor_scalar(result[:], sums[j][:], gain[:], None, ALU.mult)
             nc.sync.dma_start(rows[j], result[:])

@@ -24,7 +24,6 @@ Q_TILES = QUERIES // P
 V_TILES = DV // P
 EPS = 1e-05
 C_ROW = 4
-Q_SPLIT = 80
 
 FLOPS = 3 * 2 * 512 * 512 * 512
 
@@ -34,45 +33,42 @@ def tile_attend_at_residsig_topk_kernel(tc, qT, k_words, k_scales, c_words, c_sc
     with ExitStack() as ctx:
         keep = ctx.enter_context(tc.tile_pool(name="keep", bufs=1))
         psum = ctx.enter_context(tc.psum_pool(name="psum", bufs=1))
-        turn = ctx.enter_context(tc.psum_pool(name="turn", bufs=2))
+        turn = ctx.enter_context(tc.psum_pool(name="turn", bufs=3))
 
         offsets = keep.tile([P, SLOTS // 16], U16, name="offsets")
-        k_scale_pool = keep.tile([P, TOKENS], U8, name="k_scale_pool", tag="stage1")
-        c_scale_pool = keep.tile([P, TOKENS], U8, name="c_scale_pool", tag="stage2")
+        k_scale_pool = keep.tile([P, TOKENS], U8, name="k_scale_pool", tag="stage0", align_bytes=64)
+        c_scale_pool = keep.tile([P, TOKENS], U8, name="c_scale_pool", tag="stage1", align_bytes=64)
         nc.gpsimd.memset(k_scale_pool[:].bitcast(I32), 0)
-        nc.vector.memset(c_scale_pool[:].bitcast(I32), 0)
+        nc.gpsimd.memset(c_scale_pool[:].bitcast(I32), 0)
+        warm = keep.tile([P, 8], F32, name="warm")
+        warm_out = keep.tile([P, 8], F32, name="warm_out")
+        nc.gpsimd.memset(warm[:], 0.0)
 
-        q_raw = keep.tile([P, PACK, QUERIES], F32, name="q_raw", tag="stage3")
-        k_pool = keep.tile([P, TOKENS], I32, name="k_pool", tag="stage0")
-        c_pool = keep.tile([P, TOKENS], I32, name="c_pool", tag="after_c", align_bytes=64)
+        q_raw = keep.tile([P, PACK, QUERIES], F32, name="q_raw", tag="stage2", align_bytes=64)
+        k_pool = keep.tile([P, TOKENS], I32, name="k_pool", tag="keys", align_bytes=64)
         th_col = keep.tile([P, Q_TILES], F32, name="th_col")
         us_col = keep.tile([P, PACK], F32, name="us_col")
 
-        nc.sync.dma_start(k_pool[:], k_words[0].rearrange("p n t -> p (n t)").bitcast(I32))
         nc.sync.dma_start(offsets[:], offs)
-        nc.sync.dma_start(q_raw[:], qT[0].rearrange("(p t) q -> p t q", t=PACK))
-        nc.sync.dma_start(c_pool[:], c_words[0].rearrange("p n t -> p (n t)").bitcast(I32))
+        nc.sync.dma_start(k_pool[:], k_words[0].rearrange("p n t -> p (n t)").bitcast(I32))
         k_rows = k_scales[0].bitcast(I32).rearrange("(g r) n -> r g n", r=4)
         c_rows = c_scales[0].bitcast(I32).rearrange("(g r) n -> r g n", r=4)
         for r in range(4):
             nc.scalar.dma_start(k_scale_pool[r:P:32, :].bitcast(I32), k_rows[r])
         for r in range(4):
-            queue = nc.scalar if r < 2 else nc.gpsimd
-            queue.dma_start(c_scale_pool[C_ROW + r:P:32, :].bitcast(I32), c_rows[r])
+            nc.scalar.dma_start(c_scale_pool[C_ROW + r:P:32, :].bitcast(I32), c_rows[r])
+        nc.gpsimd.dma_start(q_raw[:], qT[0].rearrange("(p t) q -> p t q", t=PACK))
         nc.gpsimd.dma_start(th_col[:], th[0, 0].rearrange("(m j) -> m j", j=Q_TILES))
         nc.gpsimd.dma_start(us_col[:], us[0].rearrange("(p t) o -> p (t o)", t=PACK))
         ident = keep.tile([P, P], F32, name="ident")
         make_identity(nc, ident[:])
 
-        warm = keep.tile([P, 8], F32, name="warm")
-        warm_out = keep.tile([P, 8], F32, name="warm_out")
-        nc.vector.memset(warm[:], 0.0)
         nc.scalar.activation(warm_out[:, 0:1], warm[:, 0:1], ACT.Sigmoid)
 
-        q_bf = keep.tile([P, Q_TILES, P, PACK], BF16, name="q_bf", tag="after_q", align_bytes=64)
-        q_dst = q_bf[:].rearrange("p j m t -> p m j t")
-        q_src = q_raw[:].rearrange("p t (m j) -> p m j t", j=Q_TILES)
-        nc.scalar.copy(q_dst[:, :Q_SPLIT], q_src[:, :Q_SPLIT])
+        q_bf = keep.tile([P, Q_TILES, P, PACK], BF16, name="q_bf", align_bytes=64)
+        q_dst = q_bf[:].rearrange("p j m t -> p m t j")
+        q_src = q_raw[:].rearrange("p t (m j) -> p m t j", j=Q_TILES)
+        nc.scalar.copy(q_dst[:, :, :, 2:], q_src[:, :, :, 2:])
         neg_th = keep.tile([P, Q_TILES], F32, name="neg_th")
         nc.scalar.mul(neg_th[:], th_col[:], -1.0)
 
@@ -82,30 +78,37 @@ def tile_attend_at_residsig_topk_kernel(tc, qT, k_words, k_scales, c_words, c_sc
         q_codes = keep.tile([P, QUERIES], U32, name="q_codes", align_bytes=64)
         q_bytes = keep.tile([P, QUERIES], U8, name="q_bytes", align_bytes=64)
         nc.vector.tensor_copy(k_codes[:], k_pool[:].bitcast(U32).indirect(offsets[:]))
+        c_pool = keep.tile([P, TOKENS], I32, name="c_pool", tag="keys", align_bytes=64)
+        nc.sync.dma_start(c_pool[:], c_words[0].rearrange("p n t -> p (n t)").bitcast(I32))
         nc.vector.tensor_copy(k_bytes[:], k_scale_pool[:].indirect(offsets[:]))
+        nc.vector.tensor_copy(q_dst[:, :, :, :2], q_src[:, :, :, :2])
+        nc.vector.quantize_mx(out=q_codes[:, :2 * P].bitcast(FP8X4), scales=q_bytes[:, :2 * P],
+                              in_=q_bf[:, :2].rearrange("p j m t -> p (j m t)"))
         nc.vector.tensor_copy(c_bytes[:], c_scale_pool[:].indirect(offsets[:]))
-        nc.vector.tensor_copy(q_dst[:, Q_SPLIT:], q_src[:, Q_SPLIT:])
-        nc.vector.quantize_mx(out=q_codes[:].bitcast(FP8X4), scales=q_bytes[:], in_=q_bf[:].rearrange("p j m t -> p (j m t)"))
-        c_codes = keep.tile([P, SLOTS], U32, name="c_codes", tag="after_q", align_bytes=64)
+        nc.vector.quantize_mx(out=q_codes[:, 2 * P:].bitcast(FP8X4), scales=q_bytes[:, 2 * P:],
+                              in_=q_bf[:, 2:].rearrange("p j m t -> p (j m t)"))
+        c_codes = keep.tile([P, SLOTS], U32, name="c_codes", align_bytes=64)
         nc.vector.tensor_copy(c_codes[:], c_pool[:].bitcast(U32).indirect(offsets[:]))
 
         v_pool = []
-        for e in range(V_TILES):
-            rows_in = keep.tile([P, TOKENS], F32, name="v_pool%d" % e, tag="stage%d" % e)
+
+        def load_values(e):
+            rows_in = keep.tile([P, TOKENS], F32, name="v_pool%d" % e, tag="stage%d" % (e % 3), align_bytes=64)
             nc.sync.dma_start(rows_in[:], vT[e * P:(e + 1) * P, :])
             v_pool.append(rows_in)
 
-        scores = []
-        for j in range(Q_TILES):
-            score = psum.tile([P, SLOTS], F32, name="score%d" % j, tag="rows%d" % j)
-            cols = slice(j * P, (j + 1) * P)
-            nc.tensor.matmul_mx(out=score[:], lhsT=q_codes[:, cols].bitcast(FP8X4), lhsT_scale=q_bytes[:, cols],
-                                rhs=k_codes[:].bitcast(FP8X4), rhs_scale=k_bytes[:], start=True, stop=False)
-            scores.append(score)
-        for j in range(Q_TILES):
+        for e in range(3):
+            load_values(e)
+
+        scores = [psum.tile([P, SLOTS], F32, name="score%d" % j, tag="rows%d" % j) for j in range(Q_TILES)]
+
+        def score_pass(j, codes, scale_rows, first):
             cols = slice(j * P, (j + 1) * P)
             nc.tensor.matmul_mx(out=scores[j][:], lhsT=q_codes[:, cols].bitcast(FP8X4), lhsT_scale=q_bytes[:, cols],
-                                rhs=c_codes[:].bitcast(FP8X4), rhs_scale=c_bytes[C_ROW:P, :], start=False, stop=True)
+                                rhs=codes[:].bitcast(FP8X4), rhs_scale=scale_rows, start=first, stop=not first)
+
+        for j in range(Q_TILES):
+            score_pass(j, k_codes, k_bytes[:], True)
 
         v_codes = keep.tile([P, DV], U32, name="v_codes", align_bytes=64)
         v_bytes = keep.tile([P, DV], U8, name="v_bytes", align_bytes=64)
@@ -113,17 +116,23 @@ def tile_attend_at_residsig_topk_kernel(tc, qT, k_words, k_scales, c_words, c_sc
         y_bf = [keep.tile([P, 2 * P, PACK], BF16, name="y_bf%d" % h, tag="y_bf%d" % h, align_bytes=64) for h in range(2)]
         y_codes = keep.tile([P, QUERIES], U32, name="y_codes", align_bytes=64)
         y_bytes = keep.tile([P, QUERIES], U8, name="y_bytes", align_bytes=64)
-        sigs = []
 
-        def turn_values(e, tag, align):
-            picked = keep.tile([P, 2, P, 2], BF16, name="picked%d" % e, tag=tag, align_bytes=align)
-            nc.vector.tensor_copy(picked[:].rearrange("e u p b -> e p u b"), v_pool[e][:].indirect(offsets[:]))
-            words = picked[:].rearrange("e u p b -> e (u p b)").bitcast(F32)
-            turned = turn.tile([P, 2, P], F32, name="v_turned", tag="v_turned")
+        us_rows = psum.tile([P, PACK, P], F32, name="us_rows")
+        for t in range(PACK):
+            nc.tensor.transpose(us_rows[:, t, :], us_col[:, t:t + 1].to_broadcast([P, P]), ident[:])
+
+        def turn_pairs(pairs, halves, i, copy=nc.scalar.copy):
+            words = pairs[:].rearrange("c u p b -> c (u p b)").bitcast(F32)
+            turned = turn.tile([P, 2, P], F32, name="turned")
             for u in range(2):
                 nc.tensor.transpose(turned[:, u, :], words[:, u * P:(u + 1) * P], ident[:])
-            dst = v_bf[e // 2][:, (e % 2) * P:(e % 2 + 1) * P, :].rearrange("p e t -> p (e t)").bitcast(F32)
-            nc.scalar.copy(dst.rearrange("p (e u) -> p e u", u=2), turned[:].rearrange("p u e -> p e u"))
+            dst = halves[i // 2][:, (i % 2) * P:(i % 2 + 1) * P, :].rearrange("p c t -> p (c t)").bitcast(F32)
+            copy(dst.rearrange("p (c u) -> p c u", u=2), turned[:].rearrange("p u c -> p c u"))
+
+        def pick_values(e):
+            picked = keep.tile([P, 2, P, 2], BF16, name="picked%d" % e)
+            nc.vector.tensor_copy(picked[:].rearrange("e u p b -> e p u b"), v_pool[e][:].indirect(offsets[:]))
+            return picked
 
         def quantize_half(codes, scale_bytes, halves, h):
             cols = slice(2 * h * P, 2 * (h + 1) * P)
@@ -131,14 +140,12 @@ def tile_attend_at_residsig_topk_kernel(tc, qT, k_words, k_scales, c_words, c_sc
                                   in_=halves[h][:].rearrange("p c t -> p (c t)"))
 
         def weigh(j):
-            sig = keep.tile([P, PACK, P], F32, name="sig%d" % j)
-            nc.scalar.activation(sig[:], scores[j][:].rearrange("q (p t) -> q t p", t=PACK), ACT.Sigmoid, bias=neg_th[:, j:j + 1])
-            turned = turn.tile([P, PACK, P], F32, name="y_turned", tag="y_turned")
-            for t in range(PACK):
-                nc.tensor.transpose(turned[:, t, :], sig[:, t, :], ident[:])
-            nc.vector.tensor_tensor(y_bf[j // 2][:, (j % 2) * P:(j % 2 + 1) * P, :], turned[:].rearrange("p t q -> p q t"),
-                                    us_col[:].unsqueeze(1).to_broadcast([P, P, PACK]), ALU.mult)
-            sigs.append(sig)
+            sig = keep.tile([P, 2, P, 2], F32, name="sig%d" % j)
+            nc.scalar.activation(sig[:], scores[j][:].rearrange("q (p u b) -> q u p b", u=2, b=2), ACT.Sigmoid,
+                                 bias=neg_th[:, j:j + 1])
+            weights = keep.tile([P, 2, P, 2], BF16, name="weights%d" % j)
+            nc.vector.tensor_tensor(weights[:], sig[:], us_rows[:].rearrange("q (u b) p -> q u p b", u=2), ALU.mult)
+            return weights
 
         squares = keep.tile([P, Q_TILES, 2 * P], F32, name="squares")
         parts = [keep.tile([P, Q_TILES], F32, name="part%d" % h) for h in range(2)]
@@ -154,24 +161,31 @@ def tile_attend_at_residsig_topk_kernel(tc, qT, k_words, k_scales, c_words, c_sc
             nc.scalar.activation(squares[:, j, :], sums[j][:, 2 * h * P:2 * (h + 1) * P], ACT.Square, scale=1.0 / math.sqrt(DV),
                                  accum_out=parts[h][:, j:j + 1])
 
-        turn_values(0, "after_c", 64)
-        weigh(0)
-        weigh(1)
+        for j in range(Q_TILES):
+            score_pass(j, c_codes, c_bytes[C_ROW:P, :], False)
+        picked = pick_values(0)
+        load_values(3)
+        weights = [weigh(j) for j in range(2)]
+        turn_pairs(picked, v_bf, 0)
+        picked = pick_values(1)
+        weights += [weigh(j) for j in range(2, 4)]
+        turn_pairs(weights[0], y_bf, 0)
+        turn_pairs(weights[1], y_bf, 1)
+        turn_pairs(picked, v_bf, 1)
+        turn_pairs(weights[2], y_bf, 2)
+        turn_pairs(weights[3], y_bf, 3)
+        nc.scalar.activation(warm_out[:, 1:2], y_bf[1][:, 2 * P - 1, 0:1], ACT.Abs_reciprocal_sqrt, bias=1.0, scale=0.0)
         quantize_half(y_codes, y_bytes, y_bf, 0)
-        turn_values(1, "y_bf0", 64)
-        weigh(2)
-        weigh(3)
-        nc.scalar.activation(warm_out[:, 1:2], sigs[3][:, 0, 0:1], ACT.Abs_reciprocal_sqrt, bias=1.0)
-        quantize_half(y_codes, y_bytes, y_bf, 1)
         quantize_half(v_codes, v_bytes, v_bf, 0)
+        quantize_half(y_codes, y_bytes, y_bf, 1)
+        turn_pairs(pick_values(2), v_bf, 2)
         sums = [psum.tile([P, DV], F32, name="sum%d" % j, tag="rows%d" % j) for j in range(Q_TILES)]
         multiply(0)
-        turn_values(2, "v_bf0", 64)
         for j in range(Q_TILES):
             mean_square(j, 0)
         early = keep.tile([P, Q_TILES], F32, name="early")
-        nc.gpsimd.tensor_scalar(early[:], parts[0][:], 1.0, EPS, ALU.mult, ALU.add)
-        turn_values(3, "y_bf1", 64)
+        nc.scalar.add(early[:], parts[0][:], EPS)
+        turn_pairs(pick_values(3), v_bf, 3, nc.vector.tensor_copy)
         quantize_half(v_codes, v_bytes, v_bf, 1)
         multiply(1)
 
@@ -181,5 +195,8 @@ def tile_attend_at_residsig_topk_kernel(tc, qT, k_words, k_scales, c_words, c_sc
             gain = keep.tile([P, 1], F32, name="gain%d" % j)
             nc.scalar.activation(gain[:], parts[1][:, j:j + 1], ACT.Abs_reciprocal_sqrt, bias=early[:, j:j + 1])
             result = keep.tile([P, DV], F32, name="result%d" % j)
-            nc.vector.tensor_scalar(result[:], sums[j][:], gain[:], None, ALU.mult)
+            if j < Q_TILES - 1:
+                nc.vector.tensor_scalar(result[:], sums[j][:], gain[:], None, ALU.mult)
+            else:
+                nc.scalar.activation(result[:], sums[j][:], ACT.Copy, scale=gain[:])
             nc.sync.dma_start(rows[j], result[:])

@@ -122,7 +122,7 @@ def tile_attend_at_residsig_topk_kernel(tc, qT, k_words, k_scales, c_words, c_sc
             nc.tensor.transpose(us_rows[:, t, :], us_col[:, t:t + 1].to_broadcast([P, P]), ident[:])
 
         def turn_pairs(pairs, halves, i, copy=nc.scalar.copy):
-            words = pairs[:].rearrange("c u p b -> c (u p b)").bitcast(F32)
+            words = pairs[:].rearrange("c u g r -> c (u g r)").bitcast(F32)
             turned = turn.tile([P, 2, P], F32, name="turned")
             for u in range(2):
                 nc.tensor.transpose(turned[:, u, :], words[:, u * P:(u + 1) * P], ident[:])
@@ -130,8 +130,8 @@ def tile_attend_at_residsig_topk_kernel(tc, qT, k_words, k_scales, c_words, c_sc
             copy(dst.rearrange("p (c u) -> p c u", u=2), turned[:].rearrange("p u c -> p c u"))
 
         def pick_values(e):
-            picked = keep.tile([P, 2, P, 2], BF16, name="picked%d" % e)
-            nc.vector.tensor_copy(picked[:].rearrange("e u p b -> e p u b"), v_pool[e][:].indirect(offsets[:]))
+            picked = keep.tile([P, 2, 16, 16], BF16, name="picked%d" % e)
+            nc.vector.tensor_copy(picked[:].rearrange("e u g r -> e g u r"), v_pool[e][:].indirect(offsets[:]))
             return picked
 
         def quantize_half(codes, scale_bytes, halves, h):
@@ -140,11 +140,12 @@ def tile_attend_at_residsig_topk_kernel(tc, qT, k_words, k_scales, c_words, c_sc
                                   in_=halves[h][:].rearrange("p c t -> p (c t)"))
 
         def weigh(j):
-            sig = keep.tile([P, 2, P, 2], F32, name="sig%d" % j)
-            nc.scalar.activation(sig[:], scores[j][:].rearrange("q (p u b) -> q u p b", u=2, b=2), ACT.Sigmoid,
-                                 bias=neg_th[:, j:j + 1])
-            weights = keep.tile([P, 2, P, 2], BF16, name="weights%d" % j)
-            nc.vector.tensor_tensor(weights[:], sig[:], us_rows[:].rearrange("q (u b) p -> q u p b", u=2), ALU.mult)
+            sig = keep.tile([P, SLOTS], F32, name="sig%d" % j)
+            nc.scalar.activation(sig[:], scores[j][:], ACT.Sigmoid, bias=neg_th[:, j:j + 1])
+            weights = keep.tile([P, 2, 16, 16], BF16, name="weights%d" % j)
+            nc.vector.tensor_tensor(weights[:].rearrange("q u g (a t) -> q g u a t", t=PACK),
+                                    sig[:].rearrange("q (g u a t) -> q g u a t", u=2, a=4, t=PACK),
+                                    us_rows[:].rearrange("q t (g u a) -> q g u a t", u=2, a=4), ALU.mult)
             return weights
 
         squares = keep.tile([P, Q_TILES, 2 * P], F32, name="squares")

@@ -22,6 +22,7 @@ QUERIES = 512
 DV = 512
 Q_TILES = QUERIES // P
 V_TILES = DV // P
+SPANS = (slice(0, 2 * P), slice(2 * P, 3 * P), slice(3 * P, 4 * P))
 EPS = 1e-05
 C_ROW = 4
 
@@ -139,6 +140,10 @@ def tile_attend_at_residsig_topk_kernel(tc, qT, k_words, k_scales, c_words, c_sc
             nc.vector.quantize_mx(out=codes[:, cols].bitcast(FP8X4), scales=scale_bytes[:, cols],
                                   in_=halves[h][:].rearrange("p c t -> p (c t)"))
 
+        def quantize_late_values(e, codes):
+            nc.vector.quantize_mx(out=codes.bitcast(FP8X4), scales=v_bytes[:, e * P:(e + 1) * P],
+                                  in_=v_bf[1][:, (e - 2) * P:(e - 1) * P, :].rearrange("p c t -> p (c t)"))
+
         def weigh(j):
             sig = keep.tile([P, SLOTS], F32, name="sig%d" % j)
             nc.scalar.activation(sig[:], scores[j][:], ACT.Sigmoid, bias=neg_th[:, j:j + 1])
@@ -148,18 +153,18 @@ def tile_attend_at_residsig_topk_kernel(tc, qT, k_words, k_scales, c_words, c_sc
                                     us_rows[:].rearrange("q t (g u a) -> q g u a t", u=2, a=4), ALU.mult)
             return weights
 
-        squares = keep.tile([P, Q_TILES, 2 * P], F32, name="squares")
-        parts = [keep.tile([P, Q_TILES], F32, name="part%d" % h) for h in range(2)]
+        squares = keep.tile([P, Q_TILES, DV], F32, name="squares")
+        parts = [keep.tile([P, Q_TILES], F32, name="part%d" % h) for h in range(3)]
 
-        def multiply(h):
-            half = slice(2 * h * P, 2 * (h + 1) * P)
+        def multiply(h, codes):
+            half = SPANS[h]
             for j in range(Q_TILES):
                 cols = slice(j * P, (j + 1) * P)
                 nc.tensor.matmul_mx(out=sums[j][:, half], lhsT=y_codes[:, cols].bitcast(FP8X4), lhsT_scale=y_bytes[:, cols],
-                                    rhs=v_codes[:, half].bitcast(FP8X4), rhs_scale=v_bytes[:, half], start=True, stop=True)
+                                    rhs=codes.bitcast(FP8X4), rhs_scale=v_bytes[:, half], start=True, stop=True)
 
         def mean_square(j, h):
-            nc.scalar.activation(squares[:, j, :], sums[j][:, 2 * h * P:2 * (h + 1) * P], ACT.Square, scale=1.0 / math.sqrt(DV),
+            nc.scalar.activation(squares[:, j, SPANS[h]], sums[j][:, SPANS[h]], ACT.Square, scale=1.0 / math.sqrt(DV),
                                  accum_out=parts[h][:, j:j + 1])
 
         for j in range(Q_TILES):
@@ -181,22 +186,34 @@ def tile_attend_at_residsig_topk_kernel(tc, qT, k_words, k_scales, c_words, c_sc
         quantize_half(y_codes, y_bytes, y_bf, 1)
         turn_pairs(pick_values(2), v_bf, 2)
         sums = [psum.tile([P, DV], F32, name="sum%d" % j, tag="rows%d" % j) for j in range(Q_TILES)]
-        multiply(0)
+        multiply(0, v_codes[:, SPANS[0]])
         for j in range(Q_TILES):
             mean_square(j, 0)
+        picked = pick_values(3)
+        third_codes = keep.tile([P, P], U32, name="third_codes", tag="stage0", align_bytes=64)
+        quantize_late_values(2, third_codes[:])
+        turn_pairs(picked, v_bf, 3, nc.vector.tensor_copy)
+        multiply(1, third_codes[:])
+        for j in range(Q_TILES):
+            mean_square(j, 1)
+        quantize_late_values(3, v_codes[:, SPANS[2]])
+        multiply(2, v_codes[:, SPANS[2]])
         early = keep.tile([P, Q_TILES], F32, name="early")
-        nc.scalar.add(early[:], parts[0][:], EPS)
-        turn_pairs(pick_values(3), v_bf, 3, nc.vector.tensor_copy)
-        quantize_half(v_codes, v_bytes, v_bf, 1)
-        multiply(1)
+        nc.vector.scalar_tensor_tensor(early[:], parts[0][:], EPS, parts[1][:], ALU.add, ALU.add)
 
         rows = out[0].rearrange("(m j) e -> j m e", j=Q_TILES)
         for j in range(Q_TILES):
-            mean_square(j, 1)
+            mean_square(j, 2)
             gain = keep.tile([P, 1], F32, name="gain%d" % j)
-            nc.scalar.activation(gain[:], parts[1][:, j:j + 1], ACT.Abs_reciprocal_sqrt, bias=early[:, j:j + 1])
+            nc.scalar.activation(gain[:], parts[2][:, j:j + 1], ACT.Abs_reciprocal_sqrt, bias=early[:, j:j + 1])
             result = keep.tile([P, DV], F32, name="result%d" % j)
-            if j < Q_TILES - 1:
+            if j == 0:
+                for h in range(2):
+                    cols = slice(h * DV // 2, (h + 1) * DV // 2)
+                    nc.vector.tensor_scalar(result[:, cols], sums[j][:, cols], gain[:], None, ALU.mult)
+                    nc.sync.dma_start(rows[j][:, cols], result[:, cols])
+                continue
+            if j % 2 == 0:
                 nc.vector.tensor_scalar(result[:], sums[j][:], gain[:], None, ALU.mult)
             else:
                 nc.scalar.activation(result[:], sums[j][:], ACT.Copy, scale=gain[:])

@@ -2,7 +2,6 @@ import math
 from contextlib import ExitStack
 
 import concourse.mybir as mybir
-from concourse.masks import make_identity
 
 F32 = mybir.dt.float32
 BF16 = mybir.dt.bfloat16
@@ -22,7 +21,13 @@ QUERIES = 512
 DV = 512
 Q_TILES = QUERIES // P
 V_TILES = DV // P
+HALF = QUERIES // 2
+ROW_BYTES = 4 * TOKENS
+C_AT = ROW_BYTES + 192
 SPANS = (slice(0, 2 * P), slice(2 * P, 3 * P), slice(3 * P, 4 * P))
+LATE = 51712
+V_AT = (16576, 40960, 28800, C_AT)
+WARM_PASSES = 3
 EPS = 1e-05
 C_ROW = 4
 
@@ -33,74 +38,85 @@ def tile_attend_at_residsig_topk_kernel(tc, qT, k_words, k_scales, c_words, c_sc
     nc = tc.nc
     with ExitStack() as ctx:
         keep = ctx.enter_context(tc.tile_pool(name="keep", bufs=1))
+        staged = ctx.enter_context(tc.tile_pool(name="staged", bufs=1))
         psum = ctx.enter_context(tc.psum_pool(name="psum", bufs=1))
         turn = ctx.enter_context(tc.psum_pool(name="turn", bufs=3))
 
         offsets = keep.tile([P, SLOTS // 16], U16, name="offsets")
-        k_scale_pool = keep.tile([P, TOKENS], U8, name="k_scale_pool", tag="stage0", align_bytes=64)
-        c_scale_pool = keep.tile([P, TOKENS], U8, name="c_scale_pool", tag="stage1", align_bytes=64)
-        nc.gpsimd.memset(k_scale_pool[:].bitcast(I32), 0)
-        nc.gpsimd.memset(c_scale_pool[:].bitcast(I32), 0)
-        warm = keep.tile([P, 8], F32, name="warm")
-        warm_out = keep.tile([P, 8], F32, name="warm_out")
-        nc.gpsimd.memset(warm[:], 0.0)
+        column = staged.tile([P, P], F32, name="column", offset=ROW_BYTES - 256, align_bytes=64)
+        row = staged.tile([P, 32], F32, name="row", offset=49152 + TOKENS - 64, align_bytes=64)
+        nc.gpsimd.iota(column[:], pattern=[[1, P]], base=0, channel_multiplier=0, allow_small_or_imprecise_dtypes=True)
+        nc.gpsimd.iota(row[:, 0:1], pattern=[[0, 1]], base=0, channel_multiplier=1, allow_small_or_imprecise_dtypes=True)
+        k_scale_pool = keep.tile([P, TOKENS], U8, name="k_scale_pool", tag="k_scales", align_bytes=64)
+        nc.vector.memset(k_scale_pool[:].bitcast(I32), 0)
+        ident = keep.tile([P, P], F32, name="ident")
+        nc.vector.tensor_scalar(ident[:], column[:], row[:, 0:1], None, ALU.is_equal)
+        c_scale_pool = staged.tile([P, TOKENS], U8, name="c_scale_pool", offset=49152, align_bytes=64)
+        nc.vector.memset(c_scale_pool[:].bitcast(I32), 0)
+        warm_in = staged.tile([P, 1], F32, name="warm_in", offset=C_AT, align_bytes=64)
+        warm_out = staged.tile([P, 1], F32, name="warm_out", offset=39616, align_bytes=64)
+        nc.vector.memset(warm_in[:], 0.0)
+        nc.scalar.activation(warm_out[:], warm_in[:], ACT.Sigmoid)
 
-        q_raw = keep.tile([P, PACK, QUERIES], F32, name="q_raw", tag="stage2", align_bytes=64)
-        k_pool = keep.tile([P, TOKENS], I32, name="k_pool", tag="keys", align_bytes=64)
-        th_col = keep.tile([P, Q_TILES], F32, name="th_col")
-        us_col = keep.tile([P, PACK], F32, name="us_col")
+        q_rows = qT[0].rearrange("(p t) q -> p t q", t=PACK)
+
+        def load_queries(h):
+            raw = staged.tile([P, PACK, HALF], F32, name="q_raw%d" % h, offset=(24704, 28736)[h], align_bytes=64)
+            nc.sync.dma_start(raw[:], q_rows[:, :, h * HALF:(h + 1) * HALF])
+            return raw
 
         nc.sync.dma_start(offsets[:], offs)
-        nc.sync.dma_start(k_pool[:], k_words[0].rearrange("p n t -> p (n t)").bitcast(I32))
+        q_first = load_queries(0)
         k_rows = k_scales[0].bitcast(I32).rearrange("(g r) n -> r g n", r=4)
         c_rows = c_scales[0].bitcast(I32).rearrange("(g r) n -> r g n", r=4)
         for r in range(4):
-            nc.scalar.dma_start(k_scale_pool[r:P:32, :].bitcast(I32), k_rows[r])
+            nc.sync.dma_start(k_scale_pool[r:P:32, :].bitcast(I32), k_rows[r])
+        k_pool = staged.tile([P, TOKENS], I32, name="k_pool", offset=0, align_bytes=64)
+        nc.sync.dma_start(k_pool[:], k_words[0].rearrange("p n t -> p (n t)").bitcast(I32))
         for r in range(4):
-            nc.scalar.dma_start(c_scale_pool[C_ROW + r:P:32, :].bitcast(I32), c_rows[r])
-        nc.gpsimd.dma_start(q_raw[:], qT[0].rearrange("(p t) q -> p t q", t=PACK))
-        nc.gpsimd.dma_start(th_col[:], th[0, 0].rearrange("(m j) -> m j", j=Q_TILES))
+            nc.sync.dma_start(c_scale_pool[C_ROW + r:P:32, :].bitcast(I32), c_rows[r])
+        c_pool = staged.tile([P, TOKENS], I32, name="c_pool", offset=C_AT, align_bytes=64)
+        nc.sync.dma_start(c_pool[:], c_words[0].rearrange("p n t -> p (n t)").bitcast(I32))
+        th_col = keep.tile([P, 2, 2], F32, name="th_col")
+        us_col = keep.tile([P, PACK], F32, name="us_col")
         nc.gpsimd.dma_start(us_col[:], us[0].rearrange("(p t) o -> p (t o)", t=PACK))
-        ident = keep.tile([P, P], F32, name="ident")
-        make_identity(nc, ident[:])
+        nc.gpsimd.dma_start(th_col[:], th[0, 0].rearrange("(h m j) -> m h j", h=2, j=2))
 
-        nc.scalar.activation(warm_out[:, 0:1], warm[:, 0:1], ACT.Sigmoid)
-
-        q_bf = keep.tile([P, Q_TILES, P, PACK], BF16, name="q_bf", align_bytes=64)
-        q_dst = q_bf[:].rearrange("p j m t -> p m t j")
-        q_src = q_raw[:].rearrange("p t (m j) -> p m t j", j=Q_TILES)
-        nc.scalar.copy(q_dst[:, :, :, 2:], q_src[:, :, :, 2:])
         neg_th = keep.tile([P, Q_TILES], F32, name="neg_th")
-        nc.scalar.mul(neg_th[:], th_col[:], -1.0)
-
-        k_codes = keep.tile([P, SLOTS], U32, name="k_codes", align_bytes=64)
-        k_bytes = keep.tile([P, SLOTS], U8, name="k_bytes", align_bytes=64)
-        c_bytes = keep.tile([P, SLOTS], U8, name="c_bytes", align_bytes=64)
+        nc.gpsimd.tensor_scalar(neg_th[:], th_col[:].rearrange("m h j -> m (h j)"), -1.0, None, ALU.mult)
+        q_bf = [staged.tile([P, 2 * P, PACK], BF16, name="q_bf%d" % h, offset=(38976, C_AT)[h], align_bytes=64) for h in range(2)]
         q_codes = keep.tile([P, QUERIES], U32, name="q_codes", align_bytes=64)
         q_bytes = keep.tile([P, QUERIES], U8, name="q_bytes", align_bytes=64)
-        nc.vector.tensor_copy(k_codes[:], k_pool[:].bitcast(U32).indirect(offsets[:]))
-        c_pool = keep.tile([P, TOKENS], I32, name="c_pool", tag="keys", align_bytes=64)
-        nc.sync.dma_start(c_pool[:], c_words[0].rearrange("p n t -> p (n t)").bitcast(I32))
+
+        def cast_queries(h, raw, copy):
+            copy(q_bf[h][:].rearrange("p (j m i) t -> p m t i j", j=2, i=2), raw[:].rearrange("p t (m i j) -> p m t i j", i=2, j=2))
+
+        def quantize_half(codes, scale_bytes, halves, h):
+            cols = slice(2 * h * P, 2 * (h + 1) * P)
+            nc.vector.quantize_mx(out=codes.bitcast(FP8X4), scales=scale_bytes[:, cols],
+                                  in_=halves[h][:].rearrange("p c t -> p (c t)"))
+
+        cast_queries(0, q_first, nc.scalar.copy)
+        q_second = load_queries(1)
+
+        k_codes = staged.tile([P, SLOTS], U32, name="k_codes", offset=36992, align_bytes=64)
+        k_bytes = staged.tile([P, SLOTS], U8, name="k_bytes", offset=49152 + TOKENS, align_bytes=64)
+        c_bytes = staged.tile([P, SLOTS], U8, name="c_bytes", offset=39040, align_bytes=64)
+        c_codes = staged.tile([P, SLOTS], U32, name="c_codes", offset=0, align_bytes=64)
         nc.vector.tensor_copy(k_bytes[:], k_scale_pool[:].indirect(offsets[:]))
-        nc.vector.tensor_copy(q_dst[:, :, :, :2], q_src[:, :, :, :2])
-        nc.vector.quantize_mx(out=q_codes[:, :2 * P].bitcast(FP8X4), scales=q_bytes[:, :2 * P],
-                              in_=q_bf[:, :2].rearrange("p j m t -> p (j m t)"))
+        quantize_half(q_codes[:, :HALF], q_bytes, q_bf, 0)
+        nc.vector.tensor_copy(k_codes[:], k_pool[:].bitcast(U32).indirect(offsets[:]))
         nc.vector.tensor_copy(c_bytes[:], c_scale_pool[:].indirect(offsets[:]))
-        nc.vector.quantize_mx(out=q_codes[:, 2 * P:].bitcast(FP8X4), scales=q_bytes[:, 2 * P:],
-                              in_=q_bf[:, 2:].rearrange("p j m t -> p (j m t)"))
-        c_codes = keep.tile([P, SLOTS], U32, name="c_codes", align_bytes=64)
         nc.vector.tensor_copy(c_codes[:], c_pool[:].bitcast(U32).indirect(offsets[:]))
+        cast_queries(1, q_second, nc.vector.tensor_copy)
+        quantize_half(q_codes[:, HALF:], q_bytes, q_bf, 1)
 
-        v_pool = []
+        v_pool = [staged.tile([P, TOKENS], F32, name="v_pool%d" % e, offset=V_AT[e], align_bytes=64)
+                  for e in range(V_TILES)]
+        for e in range(V_TILES):
+            nc.sync.dma_start(v_pool[e][:], vT[e * P:(e + 1) * P, :])
 
-        def load_values(e):
-            rows_in = keep.tile([P, TOKENS], F32, name="v_pool%d" % e, tag="stage%d" % (e % 3), align_bytes=64)
-            nc.sync.dma_start(rows_in[:], vT[e * P:(e + 1) * P, :])
-            v_pool.append(rows_in)
-
-        for e in range(3):
-            load_values(e)
-
+        us_rows = psum.tile([P, PACK, P], F32, name="us_rows")
         scores = [psum.tile([P, SLOTS], F32, name="score%d" % j, tag="rows%d" % j) for j in range(Q_TILES)]
 
         def score_pass(j, codes, scale_rows, first):
@@ -108,19 +124,24 @@ def tile_attend_at_residsig_topk_kernel(tc, qT, k_words, k_scales, c_words, c_sc
             nc.tensor.matmul_mx(out=scores[j][:], lhsT=q_codes[:, cols].bitcast(FP8X4), lhsT_scale=q_bytes[:, cols],
                                 rhs=codes[:].bitcast(FP8X4), rhs_scale=scale_rows, start=first, stop=not first)
 
-        for j in range(Q_TILES):
-            score_pass(j, k_codes, k_bytes[:], True)
-
-        v_codes = keep.tile([P, DV], U32, name="v_codes", align_bytes=64)
-        v_bytes = keep.tile([P, DV], U8, name="v_bytes", align_bytes=64)
-        v_bf = [keep.tile([P, 2 * P, PACK], BF16, name="v_bf%d" % h, tag="v_bf%d" % h, align_bytes=64) for h in range(2)]
-        y_bf = [keep.tile([P, 2 * P, PACK], BF16, name="y_bf%d" % h, tag="y_bf%d" % h, align_bytes=64) for h in range(2)]
-        y_codes = keep.tile([P, QUERIES], U32, name="y_codes", align_bytes=64)
-        y_bytes = keep.tile([P, QUERIES], U8, name="y_bytes", align_bytes=64)
-
-        us_rows = psum.tile([P, PACK, P], F32, name="us_rows")
         for t in range(PACK):
             nc.tensor.transpose(us_rows[:, t, :], us_col[:, t:t + 1].to_broadcast([P, P]), ident[:])
+        for j in range(2):
+            score_pass(j, k_codes, k_bytes[:], True)
+        for i in range(WARM_PASSES):
+            nc.tensor.matmul_mx(out=scores[2 + i % 2][:], lhsT=q_codes[:, :P].bitcast(FP8X4), lhsT_scale=q_bytes[:, :P],
+                                rhs=k_codes[:].bitcast(FP8X4), rhs_scale=k_bytes[:], start=True, stop=True)
+        for j in range(2):
+            score_pass(j, c_codes, c_bytes[C_ROW:P, :], False)
+        for j in range(2, Q_TILES):
+            score_pass(j, k_codes, k_bytes[:], True)
+            score_pass(j, c_codes, c_bytes[C_ROW:P, :], False)
+
+        last_codes = keep.tile([P, P], U32, name="last_codes", align_bytes=64)
+        v_bytes = keep.tile([P, DV], U8, name="v_bytes", align_bytes=64)
+        v_bf = [keep.tile([P, 2 * P, PACK], BF16, name="v_bf%d" % h, tag="v_bf%d" % h, align_bytes=64) for h in range(2)]
+        y_bf = [staged.tile([P, 2 * P, PACK], BF16, name="y_bf%d" % h, offset=LATE + (4 + h) * 2048, align_bytes=64) for h in range(2)]
+        y_bytes = keep.tile([P, QUERIES], U8, name="y_bytes", align_bytes=64)
 
         def turn_pairs(pairs, halves, i, copy=nc.scalar.copy):
             words = pairs[:].rearrange("c u g r -> c (u g r)").bitcast(F32)
@@ -131,23 +152,18 @@ def tile_attend_at_residsig_topk_kernel(tc, qT, k_words, k_scales, c_words, c_sc
             copy(dst.rearrange("p (c u) -> p c u", u=2), turned[:].rearrange("p u c -> p c u"))
 
         def pick_values(e):
-            picked = keep.tile([P, 2, 16, 16], BF16, name="picked%d" % e)
+            picked = staged.tile([P, 2, 16, 16], BF16, name="picked%d" % e, offset=LATE + (0, 6, 7, 5)[e] * 2048, align_bytes=64)
             nc.vector.tensor_copy(picked[:].rearrange("e u g r -> e g u r"), v_pool[e][:].indirect(offsets[:]))
             return picked
-
-        def quantize_half(codes, scale_bytes, halves, h):
-            cols = slice(2 * h * P, 2 * (h + 1) * P)
-            nc.vector.quantize_mx(out=codes[:, cols].bitcast(FP8X4), scales=scale_bytes[:, cols],
-                                  in_=halves[h][:].rearrange("p c t -> p (c t)"))
 
         def quantize_late_values(e, codes):
             nc.vector.quantize_mx(out=codes.bitcast(FP8X4), scales=v_bytes[:, e * P:(e + 1) * P],
                                   in_=v_bf[1][:, (e - 2) * P:(e - 1) * P, :].rearrange("p c t -> p (c t)"))
 
         def weigh(j):
-            sig = keep.tile([P, SLOTS], F32, name="sig%d" % j)
+            sig = staged.tile([P, SLOTS], F32, name="sig%d" % j, offset=LATE + j * 2048, align_bytes=64)
             nc.scalar.activation(sig[:], scores[j][:], ACT.Sigmoid, bias=neg_th[:, j:j + 1])
-            weights = keep.tile([P, 2, 16, 16], BF16, name="weights%d" % j)
+            weights = staged.tile([P, 2, 16, 16], BF16, name="weights%d" % j, offset=V_AT[0] if j == 2 else LATE + (8 + j) * 2048, align_bytes=64)
             nc.vector.tensor_tensor(weights[:].rearrange("q u g (a t) -> q g u a t", t=PACK),
                                     sig[:].rearrange("q (g u a t) -> q g u a t", u=2, a=4, t=PACK),
                                     us_rows[:].rearrange("q t (g u a) -> q g u a t", u=2, a=4), ALU.mult)
@@ -160,48 +176,50 @@ def tile_attend_at_residsig_topk_kernel(tc, qT, k_words, k_scales, c_words, c_sc
             half = SPANS[h]
             for j in range(Q_TILES):
                 cols = slice(j * P, (j + 1) * P)
-                nc.tensor.matmul_mx(out=sums[j][:, half], lhsT=y_codes[:, cols].bitcast(FP8X4), lhsT_scale=y_bytes[:, cols],
+                nc.tensor.matmul_mx(out=sums[j][:, half], lhsT=y_codes[j // 2][:, (j % 2) * P:(j % 2 + 1) * P].bitcast(FP8X4), lhsT_scale=y_bytes[:, cols],
                                     rhs=codes.bitcast(FP8X4), rhs_scale=v_bytes[:, half], start=True, stop=True)
 
         def mean_square(j, h):
             nc.scalar.activation(squares[:, j, SPANS[h]], sums[j][:, SPANS[h]], ACT.Square, scale=1.0 / math.sqrt(DV),
                                  accum_out=parts[h][:, j:j + 1])
 
-        for j in range(Q_TILES):
-            score_pass(j, c_codes, c_bytes[C_ROW:P, :], False)
-        picked = pick_values(0)
-        load_values(3)
         weights = [weigh(j) for j in range(2)]
-        turn_pairs(picked, v_bf, 0)
-        picked = pick_values(1)
-        weights += [weigh(j) for j in range(2, 4)]
+        picked = pick_values(0)
+        weights = weights + [weigh(j) for j in range(2, Q_TILES)]
         turn_pairs(weights[0], y_bf, 0)
         turn_pairs(weights[1], y_bf, 1)
-        turn_pairs(picked, v_bf, 1)
+        turn_pairs(picked, v_bf, 0)
         turn_pairs(weights[2], y_bf, 2)
         turn_pairs(weights[3], y_bf, 3)
-        nc.scalar.activation(warm_out[:, 1:2], y_bf[1][:, 2 * P - 1, 0:1], ACT.Abs_reciprocal_sqrt, bias=1.0, scale=0.0)
-        quantize_half(y_codes, y_bytes, y_bf, 0)
-        quantize_half(v_codes, v_bytes, v_bf, 0)
-        quantize_half(y_codes, y_bytes, y_bf, 1)
-        turn_pairs(pick_values(2), v_bf, 2)
+        turn_pairs(pick_values(1), v_bf, 1)
+        switch_out = keep.tile([P, 1], F32, name="switch_out")
+        nc.scalar.activation(switch_out[:], v_bf[0][:, 2 * P - 1, 0:1], ACT.Abs_reciprocal_sqrt, bias=1.0, scale=0.0)
+        y_codes = [keep.tile([P, HALF], U32, name="y_codes0", align_bytes=64)]
+        quantize_half(y_codes[0][:], y_bytes, y_bf, 0)
+        picked = pick_values(2)
+        y_codes.append(staged.tile([P, HALF], U32, name="y_codes1", offset=V_AT[2], align_bytes=64))
+        first_codes = staged.tile([P, HALF], U32, name="first_codes", offset=V_AT[2] + 1024, align_bytes=64)
+        quantize_half(y_codes[1][:], y_bytes, y_bf, 1)
+        quantize_half(first_codes[:], v_bytes, v_bf, 0)
+        turn_pairs(picked, v_bf, 2)
         sums = [psum.tile([P, DV], F32, name="sum%d" % j, tag="rows%d" % j) for j in range(Q_TILES)]
-        multiply(0, v_codes[:, SPANS[0]])
+        multiply(0, first_codes[:])
         for j in range(Q_TILES):
             mean_square(j, 0)
         picked = pick_values(3)
-        third_codes = keep.tile([P, P], U32, name="third_codes", tag="stage0", align_bytes=64)
+        third_codes = staged.tile([P, P], U32, name="third_codes", offset=V_AT[3], align_bytes=64)
         quantize_late_values(2, third_codes[:])
         turn_pairs(picked, v_bf, 3, nc.vector.tensor_copy)
         multiply(1, third_codes[:])
         for j in range(Q_TILES):
             mean_square(j, 1)
-        quantize_late_values(3, v_codes[:, SPANS[2]])
-        multiply(2, v_codes[:, SPANS[2]])
+        quantize_late_values(3, last_codes[:])
+        multiply(2, last_codes[:])
         early = keep.tile([P, Q_TILES], F32, name="early")
         nc.vector.scalar_tensor_tensor(early[:], parts[0][:], EPS, parts[1][:], ALU.add, ALU.add)
 
-        rows = out[0].rearrange("(m j) e -> j m e", j=Q_TILES)
+        by_half = out[0].rearrange("(h m j) e -> h j m e", h=2, j=2)
+        rows = [by_half[j // 2, j % 2] for j in range(Q_TILES)]
         for j in range(Q_TILES):
             mean_square(j, 2)
             gain = keep.tile([P, 1], F32, name="gain%d" % j)

@@ -82,9 +82,9 @@ def tile_attend_at_residsig_topk_kernel(tc, qT, k_words, k_scales, c_words, c_sc
         nc.gpsimd.dma_start(us_col[:], us[0].rearrange("(p t) o -> p (t o)", t=PACK))
         nc.gpsimd.dma_start(th_col[:], th[0, 0].rearrange("(h m j) -> m h j", h=2, j=2))
 
-        neg_th = keep.tile([P, Q_TILES], F32, name="neg_th")
-        nc.gpsimd.tensor_scalar(neg_th[:], th_col[:].rearrange("m h j -> m (h j)"), -1.0, None, ALU.mult)
-        q_bf = [staged.tile([P, 2 * P, PACK], BF16, name="q_bf%d" % h, offset=(38976, C_AT)[h], align_bytes=64) for h in range(2)]
+        neg_th = staged.tile([P, 32], F32, name="neg_th", offset=LATE + 13 * 2048 - 64, align_bytes=64)
+        nc.gpsimd.tensor_scalar(neg_th[:, :Q_TILES], th_col[:].rearrange("m h j -> m (h j)"), -1.0, None, ALU.mult)
+        q_bf = [staged.tile([P, 2 * P, PACK], BF16, name="q_bf%d" % h, offset=(38976, C_AT + 64 - 2048)[h], align_bytes=64) for h in range(2)]
         q_codes = keep.tile([P, QUERIES], U32, name="q_codes", align_bytes=64)
         q_bytes = keep.tile([P, QUERIES], U8, name="q_bytes", align_bytes=64)
 
@@ -126,6 +126,8 @@ def tile_attend_at_residsig_topk_kernel(tc, qT, k_words, k_scales, c_words, c_sc
 
         for t in range(PACK):
             nc.tensor.transpose(us_rows[:, t, :], us_col[:, t:t + 1].to_broadcast([P, P]), ident[:])
+        us_copy = keep.tile([P, SLOTS], F32, name="us_copy")
+        nc.scalar.copy(us_copy[:].rearrange("q (p t) -> q p t", t=PACK), us_rows[:].rearrange("q t p -> q p t"))
         for j in range(2):
             score_pass(j, k_codes, k_bytes[:], True)
         for i in range(WARM_PASSES):
@@ -139,8 +141,8 @@ def tile_attend_at_residsig_topk_kernel(tc, qT, k_words, k_scales, c_words, c_sc
 
         last_codes = keep.tile([P, P], U32, name="last_codes", align_bytes=64)
         v_bytes = keep.tile([P, DV], U8, name="v_bytes", align_bytes=64)
-        v_bf = [keep.tile([P, 2 * P, PACK], BF16, name="v_bf%d" % h, tag="v_bf%d" % h, align_bytes=64) for h in range(2)]
-        y_bf = [staged.tile([P, 2 * P, PACK], BF16, name="y_bf%d" % h, offset=LATE + (4 + h) * 2048, align_bytes=64) for h in range(2)]
+        v_bf = [staged.tile([P, 2 * P, PACK], BF16, name="v_bf%d" % h, offset=LATE + (12, 4)[h] * 2048, align_bytes=64) for h in range(2)]
+        y_bf = [staged.tile([P, 2 * P, PACK], BF16, name="y_bf%d" % h, offset=LATE + (13, 5)[h] * 2048, align_bytes=64) for h in range(2)]
         y_bytes = keep.tile([P, QUERIES], U8, name="y_bytes", align_bytes=64)
 
         def turn_pairs(pairs, halves, i, copy=nc.scalar.copy):
@@ -163,10 +165,14 @@ def tile_attend_at_residsig_topk_kernel(tc, qT, k_words, k_scales, c_words, c_sc
         def weigh(j):
             sig = staged.tile([P, SLOTS], F32, name="sig%d" % j, offset=LATE + j * 2048, align_bytes=64)
             nc.scalar.activation(sig[:], scores[j][:], ACT.Sigmoid, bias=neg_th[:, j:j + 1])
-            weights = staged.tile([P, 2, 16, 16], BF16, name="weights%d" % j, offset=V_AT[0] if j == 2 else LATE + (8 + j) * 2048, align_bytes=64)
-            nc.vector.tensor_tensor(weights[:].rearrange("q u g (a t) -> q g u a t", t=PACK),
-                                    sig[:].rearrange("q (g u a t) -> q g u a t", u=2, a=4, t=PACK),
-                                    us_rows[:].rearrange("q t (g u a) -> q g u a t", u=2, a=4), ALU.mult)
+            weights = staged.tile([P, 2, 16, 16], BF16, name="weights%d" % j, offset=(C_AT + 64 - 2048, LATE + 9 * 2048, V_AT[0], LATE + 11 * 2048)[j], align_bytes=64)
+            if j % 2 == 0:
+                nc.vector.tensor_tensor(weights[:].rearrange("q u g (a t) -> q g u a t", t=PACK),
+                                        sig[:].rearrange("q (g u a t) -> q g u a t", u=2, a=4, t=PACK),
+                                        us_rows[:].rearrange("q t (g u a) -> q g u a t", u=2, a=4), ALU.mult)
+            else:
+                nc.gpsimd.tensor_tensor(weights[:].rearrange("q u g r -> q g u r"), sig[:].rearrange("q (g u r) -> q g u r", u=2, r=16),
+                                        us_copy[:].rearrange("q (g u r) -> q g u r", u=2, r=16), ALU.mult)
             return weights
 
         squares = keep.tile([P, Q_TILES, DV], F32, name="squares")
@@ -192,9 +198,9 @@ def tile_attend_at_residsig_topk_kernel(tc, qT, k_words, k_scales, c_words, c_sc
         turn_pairs(weights[2], y_bf, 2)
         turn_pairs(weights[3], y_bf, 3)
         turn_pairs(pick_values(1), v_bf, 1)
-        switch_out = keep.tile([P, 1], F32, name="switch_out")
+        switch_out = staged.tile([P, 1], F32, name="switch_out", offset=LATE + 11 * 2048, align_bytes=64)
         nc.scalar.activation(switch_out[:], v_bf[0][:, 2 * P - 1, 0:1], ACT.Abs_reciprocal_sqrt, bias=1.0, scale=0.0)
-        y_codes = [keep.tile([P, HALF], U32, name="y_codes0", align_bytes=64)]
+        y_codes = [staged.tile([P, HALF], U32, name="y_codes0", offset=V_AT[1], align_bytes=64)]
         quantize_half(y_codes[0][:], y_bytes, y_bf, 0)
         picked = pick_values(2)
         y_codes.append(staged.tile([P, HALF], U32, name="y_codes1", offset=V_AT[2], align_bytes=64))

@@ -22,14 +22,41 @@ DV = 512
 Q_TILES = QUERIES // P
 V_TILES = DV // P
 HALF = QUERIES // 2
-ROW_BYTES = 4 * TOKENS
-C_AT = ROW_BYTES + 192
-SPANS = (slice(0, 2 * P), slice(2 * P, 3 * P), slice(3 * P, 4 * P))
-LATE = 51712
-V_AT = (16576, 40960, 28800, C_AT)
-WARM_PASSES = 3
+GROUPS = SLOTS // 32
+RUN = 16
 EPS = 1e-05
 C_ROW = 4
+WARM_PASSES = 3
+SPANS = (slice(0, 2 * P), slice(2 * P, 3 * P), slice(3 * P, 4 * P))
+
+LINK = 64
+ROW_BYTES = 4 * TOKENS
+CELL = 2048
+K_AT = 0
+COLUMN_AT = ROW_BYTES - 256
+C_AT = COLUMN_AT + 4 * P - LINK
+Q_BF1_AT = C_AT + LINK - CELL
+V0_AT = C_AT + ROW_BYTES
+Q_RAW0_AT = V0_AT + ROW_BYTES - LINK
+Q_RAW1_AT = Q_RAW0_AT + 2 * CELL - LINK
+V2_AT = Q_RAW0_AT + 2 * CELL
+K_CODES_AT = V2_AT + ROW_BYTES
+Q_BF0_AT = K_CODES_AT + CELL - LINK
+C_BYTES_AT = K_CODES_AT + CELL
+WARM_OUT_AT = C_BYTES_AT + SLOTS + LINK
+V1_AT = Q_BF0_AT + CELL - LINK
+C_SCALES_AT = V1_AT + ROW_BYTES
+K_BYTES_AT = C_SCALES_AT + TOKENS
+ROW_AT = K_BYTES_AT - LINK
+SIG_AT = K_BYTES_AT + SLOTS
+V_BF1_AT = SIG_AT + Q_TILES * CELL
+Y_BF1_AT = V_BF1_AT + CELL
+PICKED1_AT = Y_BF1_AT + CELL
+PICKED2_AT = PICKED1_AT + CELL
+WEIGHTS_AT = PICKED2_AT + CELL
+V_BF0_AT = WEIGHTS_AT + Q_TILES * CELL
+Y_BF0_AT = V_BF0_AT + CELL
+NEG_TH_AT = Y_BF0_AT - LINK
 
 FLOPS = 3 * 2 * 512 * 512 * 512
 
@@ -42,77 +69,77 @@ def tile_attend_at_residsig_topk_kernel(tc, qT, k_words, k_scales, c_words, c_sc
         psum = ctx.enter_context(tc.psum_pool(name="psum", bufs=1))
         turn = ctx.enter_context(tc.psum_pool(name="turn", bufs=3))
 
+        def place(shape, dtype, name, offset):
+            return staged.tile(shape, dtype, name=name, offset=offset, align_bytes=64)
+
         offsets = keep.tile([P, SLOTS // 16], U16, name="offsets")
-        column = staged.tile([P, P], F32, name="column", offset=ROW_BYTES - 256, align_bytes=64)
-        row = staged.tile([P, 32], F32, name="row", offset=49152 + TOKENS - 64, align_bytes=64)
+        column = place([P, P], F32, "column", COLUMN_AT)
+        row = place([P, 2 * LINK // 4], F32, "row", ROW_AT)
         nc.gpsimd.iota(column[:], pattern=[[1, P]], base=0, channel_multiplier=0, allow_small_or_imprecise_dtypes=True)
         nc.gpsimd.iota(row[:, 0:1], pattern=[[0, 1]], base=0, channel_multiplier=1, allow_small_or_imprecise_dtypes=True)
-        k_scale_pool = keep.tile([P, TOKENS], U8, name="k_scale_pool", tag="k_scales", align_bytes=64)
+        k_scale_pool = keep.tile([P, TOKENS], U8, name="k_scale_pool", align_bytes=64)
         nc.vector.memset(k_scale_pool[:].bitcast(I32), 0)
         ident = keep.tile([P, P], F32, name="ident")
         nc.vector.tensor_scalar(ident[:], column[:], row[:, 0:1], None, ALU.is_equal)
-        c_scale_pool = staged.tile([P, TOKENS], U8, name="c_scale_pool", offset=49152, align_bytes=64)
+        c_scale_pool = place([P, TOKENS], U8, "c_scale_pool", C_SCALES_AT)
         nc.vector.memset(c_scale_pool[:].bitcast(I32), 0)
-        warm_in = staged.tile([P, 1], F32, name="warm_in", offset=C_AT, align_bytes=64)
-        warm_out = staged.tile([P, 1], F32, name="warm_out", offset=39616, align_bytes=64)
+        warm_in = place([P, 1], F32, "warm_in", C_AT)
+        warm_out = place([P, 1], F32, "warm_out", WARM_OUT_AT)
         nc.vector.memset(warm_in[:], 0.0)
         nc.scalar.activation(warm_out[:], warm_in[:], ACT.Sigmoid)
 
         q_rows = qT[0].rearrange("(p t) q -> p t q", t=PACK)
 
         def load_queries(h):
-            raw = staged.tile([P, PACK, HALF], F32, name="q_raw%d" % h, offset=(24704, 28736)[h], align_bytes=64)
+            raw = place([P, PACK, HALF], F32, "q_raw%d" % h, (Q_RAW0_AT, Q_RAW1_AT)[h])
             nc.sync.dma_start(raw[:], q_rows[:, :, h * HALF:(h + 1) * HALF])
             return raw
 
-        nc.sync.dma_start(offsets[:], offs)
         q_first = load_queries(0)
+        nc.sync.dma_start(offsets[:], offs)
         k_rows = k_scales[0].bitcast(I32).rearrange("(g r) n -> r g n", r=4)
         c_rows = c_scales[0].bitcast(I32).rearrange("(g r) n -> r g n", r=4)
         for r in range(4):
             nc.sync.dma_start(k_scale_pool[r:P:32, :].bitcast(I32), k_rows[r])
-        k_pool = staged.tile([P, TOKENS], I32, name="k_pool", offset=0, align_bytes=64)
+        k_pool = place([P, TOKENS], I32, "k_pool", K_AT)
         nc.sync.dma_start(k_pool[:], k_words[0].rearrange("p n t -> p (n t)").bitcast(I32))
         for r in range(4):
             nc.sync.dma_start(c_scale_pool[C_ROW + r:P:32, :].bitcast(I32), c_rows[r])
-        c_pool = staged.tile([P, TOKENS], I32, name="c_pool", offset=C_AT, align_bytes=64)
+        c_pool = place([P, TOKENS], I32, "c_pool", C_AT)
         nc.sync.dma_start(c_pool[:], c_words[0].rearrange("p n t -> p (n t)").bitcast(I32))
         th_col = keep.tile([P, 2, 2], F32, name="th_col")
         us_col = keep.tile([P, PACK], F32, name="us_col")
         nc.gpsimd.dma_start(us_col[:], us[0].rearrange("(p t) o -> p (t o)", t=PACK))
-        nc.gpsimd.dma_start(th_col[:], th[0, 0].rearrange("(h m j) -> m h j", h=2, j=2))
+        nc.gpsimd.dma_start(th_col[:], th[0, 0].rearrange("(h m i) -> m h i", h=2, i=2))
+        neg_th = place([P, 2 * LINK // 4], F32, "neg_th", NEG_TH_AT)
+        nc.gpsimd.tensor_scalar(neg_th[:, :Q_TILES], th_col[:].rearrange("m h i -> m (h i)"), -1.0, None, ALU.mult)
 
-        neg_th = staged.tile([P, 32], F32, name="neg_th", offset=LATE + 13 * 2048 - 64, align_bytes=64)
-        nc.gpsimd.tensor_scalar(neg_th[:, :Q_TILES], th_col[:].rearrange("m h j -> m (h j)"), -1.0, None, ALU.mult)
-        q_bf = [staged.tile([P, 2 * P, PACK], BF16, name="q_bf%d" % h, offset=(38976, C_AT + 64 - 2048)[h], align_bytes=64) for h in range(2)]
+        q_bf = [place([P, HALF, PACK], BF16, "q_bf%d" % h, (Q_BF0_AT, Q_BF1_AT)[h]) for h in range(2)]
         q_codes = keep.tile([P, QUERIES], U32, name="q_codes", align_bytes=64)
         q_bytes = keep.tile([P, QUERIES], U8, name="q_bytes", align_bytes=64)
 
         def cast_queries(h, raw, copy):
-            copy(q_bf[h][:].rearrange("p (j m i) t -> p m t i j", j=2, i=2), raw[:].rearrange("p t (m i j) -> p m t i j", i=2, j=2))
+            copy(q_bf[h][:].rearrange("p (i m n) t -> p m t n i", i=2, n=2), raw[:].rearrange("p t (m n i) -> p m t n i", n=2, i=2))
 
-        def quantize_half(codes, scale_bytes, halves, h):
-            cols = slice(2 * h * P, 2 * (h + 1) * P)
-            nc.vector.quantize_mx(out=codes.bitcast(FP8X4), scales=scale_bytes[:, cols],
-                                  in_=halves[h][:].rearrange("p c t -> p (c t)"))
+        def quantize(codes, scale_bytes, values):
+            nc.vector.quantize_mx(out=codes.bitcast(FP8X4), scales=scale_bytes, in_=values.rearrange("p c t -> p (c t)"))
 
         cast_queries(0, q_first, nc.scalar.copy)
         q_second = load_queries(1)
 
-        k_codes = staged.tile([P, SLOTS], U32, name="k_codes", offset=36992, align_bytes=64)
-        k_bytes = staged.tile([P, SLOTS], U8, name="k_bytes", offset=49152 + TOKENS, align_bytes=64)
-        c_bytes = staged.tile([P, SLOTS], U8, name="c_bytes", offset=39040, align_bytes=64)
-        c_codes = staged.tile([P, SLOTS], U32, name="c_codes", offset=0, align_bytes=64)
+        k_codes = place([P, SLOTS], U32, "k_codes", K_CODES_AT)
+        k_bytes = place([P, SLOTS], U8, "k_bytes", K_BYTES_AT)
+        c_bytes = place([P, SLOTS], U8, "c_bytes", C_BYTES_AT)
+        c_codes = place([P, SLOTS], U32, "c_codes", K_AT)
         nc.vector.tensor_copy(k_bytes[:], k_scale_pool[:].indirect(offsets[:]))
-        quantize_half(q_codes[:, :HALF], q_bytes, q_bf, 0)
+        quantize(q_codes[:, :HALF], q_bytes[:, :HALF], q_bf[0][:])
         nc.vector.tensor_copy(k_codes[:], k_pool[:].bitcast(U32).indirect(offsets[:]))
         nc.vector.tensor_copy(c_bytes[:], c_scale_pool[:].indirect(offsets[:]))
         nc.vector.tensor_copy(c_codes[:], c_pool[:].bitcast(U32).indirect(offsets[:]))
         cast_queries(1, q_second, nc.vector.tensor_copy)
-        quantize_half(q_codes[:, HALF:], q_bytes, q_bf, 1)
+        quantize(q_codes[:, HALF:], q_bytes[:, HALF:], q_bf[1][:])
 
-        v_pool = [staged.tile([P, TOKENS], F32, name="v_pool%d" % e, offset=V_AT[e], align_bytes=64)
-                  for e in range(V_TILES)]
+        v_pool = [place([P, TOKENS], F32, "v_pool%d" % e, (V0_AT, V1_AT, V2_AT, C_AT)[e]) for e in range(V_TILES)]
         for e in range(V_TILES):
             nc.sync.dma_start(v_pool[e][:], vT[e * P:(e + 1) * P, :])
 
@@ -130,9 +157,6 @@ def tile_attend_at_residsig_topk_kernel(tc, qT, k_words, k_scales, c_words, c_sc
         nc.scalar.copy(us_copy[:].rearrange("q (p t) -> q p t", t=PACK), us_rows[:].rearrange("q t p -> q p t"))
         for j in range(2):
             score_pass(j, k_codes, k_bytes[:], True)
-        for i in range(WARM_PASSES):
-            nc.tensor.matmul_mx(out=scores[2 + i % 2][:], lhsT=q_codes[:, :P].bitcast(FP8X4), lhsT_scale=q_bytes[:, :P],
-                                rhs=k_codes[:].bitcast(FP8X4), rhs_scale=k_bytes[:], start=True, stop=True)
         for j in range(2):
             score_pass(j, c_codes, c_bytes[C_ROW:P, :], False)
         for j in range(2, Q_TILES):
@@ -141,8 +165,8 @@ def tile_attend_at_residsig_topk_kernel(tc, qT, k_words, k_scales, c_words, c_sc
 
         last_codes = keep.tile([P, P], U32, name="last_codes", align_bytes=64)
         v_bytes = keep.tile([P, DV], U8, name="v_bytes", align_bytes=64)
-        v_bf = [staged.tile([P, 2 * P, PACK], BF16, name="v_bf%d" % h, offset=LATE + (12, 4)[h] * 2048, align_bytes=64) for h in range(2)]
-        y_bf = [staged.tile([P, 2 * P, PACK], BF16, name="y_bf%d" % h, offset=LATE + (13, 5)[h] * 2048, align_bytes=64) for h in range(2)]
+        v_bf = [place([P, 2 * P, PACK], BF16, "v_bf%d" % h, (V_BF0_AT, V_BF1_AT)[h]) for h in range(2)]
+        y_bf = [place([P, 2 * P, PACK], BF16, "y_bf%d" % h, (Y_BF0_AT, Y_BF1_AT)[h]) for h in range(2)]
         y_bytes = keep.tile([P, QUERIES], U8, name="y_bytes", align_bytes=64)
 
         def turn_pairs(pairs, halves, i, copy=nc.scalar.copy):
@@ -154,91 +178,86 @@ def tile_attend_at_residsig_topk_kernel(tc, qT, k_words, k_scales, c_words, c_sc
             copy(dst.rearrange("p (c u) -> p c u", u=2), turned[:].rearrange("p u c -> p c u"))
 
         def pick_values(e):
-            picked = staged.tile([P, 2, 16, 16], BF16, name="picked%d" % e, offset=LATE + (0, 6, 7, 5)[e] * 2048, align_bytes=64)
+            picked = place([P, 2, GROUPS, RUN], BF16, "picked%d" % e, (SIG_AT, PICKED1_AT, PICKED2_AT, Y_BF1_AT)[e])
             nc.vector.tensor_copy(picked[:].rearrange("e u g r -> e g u r"), v_pool[e][:].indirect(offsets[:]))
             return picked
 
-        def quantize_late_values(e, codes):
-            nc.vector.quantize_mx(out=codes.bitcast(FP8X4), scales=v_bytes[:, e * P:(e + 1) * P],
-                                  in_=v_bf[1][:, (e - 2) * P:(e - 1) * P, :].rearrange("p c t -> p (c t)"))
-
         def weigh(j):
-            sig = staged.tile([P, SLOTS], F32, name="sig%d" % j, offset=LATE + j * 2048, align_bytes=64)
+            sig = place([P, SLOTS], F32, "sig%d" % j, SIG_AT + j * CELL)
             nc.scalar.activation(sig[:], scores[j][:], ACT.Sigmoid, bias=neg_th[:, j:j + 1])
-            weights = staged.tile([P, 2, 16, 16], BF16, name="weights%d" % j, offset=(C_AT + 64 - 2048, LATE + 9 * 2048, V_AT[0], LATE + 11 * 2048)[j], align_bytes=64)
+            y = place([P, 2, GROUPS, RUN], BF16, "weights%d" % j, (Q_BF1_AT, WEIGHTS_AT + CELL, V0_AT, WEIGHTS_AT + 3 * CELL)[j])
             if j % 2 == 0:
-                nc.vector.tensor_tensor(weights[:].rearrange("q u g (a t) -> q g u a t", t=PACK),
-                                        sig[:].rearrange("q (g u a t) -> q g u a t", u=2, a=4, t=PACK),
-                                        us_rows[:].rearrange("q t (g u a) -> q g u a t", u=2, a=4), ALU.mult)
+                nc.vector.tensor_tensor(y[:].rearrange("q u g (a t) -> q g u a t", t=PACK),
+                                        sig[:].rearrange("q (g u a t) -> q g u a t", u=2, a=RUN // PACK, t=PACK),
+                                        us_rows[:].rearrange("q t (g u a) -> q g u a t", u=2, a=RUN // PACK), ALU.mult)
             else:
-                nc.gpsimd.tensor_tensor(weights[:].rearrange("q u g r -> q g u r"), sig[:].rearrange("q (g u r) -> q g u r", u=2, r=16),
-                                        us_copy[:].rearrange("q (g u r) -> q g u r", u=2, r=16), ALU.mult)
-            return weights
+                nc.gpsimd.tensor_tensor(y[:].rearrange("q u g r -> q g u r"), sig[:].rearrange("q (g u r) -> q g u r", u=2, r=RUN),
+                                        us_copy[:].rearrange("q (g u r) -> q g u r", u=2, r=RUN), ALU.mult)
+            return y
 
         squares = keep.tile([P, Q_TILES, DV], F32, name="squares")
-        parts = [keep.tile([P, Q_TILES], F32, name="part%d" % h) for h in range(3)]
+        parts = [keep.tile([P, Q_TILES], F32, name="part%d" % s) for s in range(len(SPANS))]
 
-        def multiply(h, codes):
-            half = SPANS[h]
+        def multiply(s, v_codes):
             for j in range(Q_TILES):
-                cols = slice(j * P, (j + 1) * P)
-                nc.tensor.matmul_mx(out=sums[j][:, half], lhsT=y_codes[j // 2][:, (j % 2) * P:(j % 2 + 1) * P].bitcast(FP8X4), lhsT_scale=y_bytes[:, cols],
-                                    rhs=codes.bitcast(FP8X4), rhs_scale=v_bytes[:, half], start=True, stop=True)
+                nc.tensor.matmul_mx(out=sums[j][:, SPANS[s]], lhsT=y_codes[j // 2][:, (j % 2) * P:(j % 2 + 1) * P].bitcast(FP8X4),
+                                    lhsT_scale=y_bytes[:, j * P:(j + 1) * P], rhs=v_codes.bitcast(FP8X4),
+                                    rhs_scale=v_bytes[:, SPANS[s]], start=True, stop=True)
 
-        def mean_square(j, h):
-            nc.scalar.activation(squares[:, j, SPANS[h]], sums[j][:, SPANS[h]], ACT.Square, scale=1.0 / math.sqrt(DV),
-                                 accum_out=parts[h][:, j:j + 1])
+        def mean_square(j, s):
+            nc.scalar.activation(squares[:, j, SPANS[s]], sums[j][:, SPANS[s]], ACT.Square, scale=1.0 / math.sqrt(DV),
+                                 accum_out=parts[s][:, j:j + 1])
 
         weights = [weigh(j) for j in range(2)]
-        picked = pick_values(0)
+        picked0 = pick_values(0)
         weights = weights + [weigh(j) for j in range(2, Q_TILES)]
         turn_pairs(weights[0], y_bf, 0)
         turn_pairs(weights[1], y_bf, 1)
-        turn_pairs(picked, v_bf, 0)
+        turn_pairs(picked0, v_bf, 0)
         turn_pairs(weights[2], y_bf, 2)
         turn_pairs(weights[3], y_bf, 3)
         turn_pairs(pick_values(1), v_bf, 1)
-        switch_out = staged.tile([P, 1], F32, name="switch_out", offset=LATE + 11 * 2048, align_bytes=64)
+        switch_out = place([P, 1], F32, "switch_out", WEIGHTS_AT + 3 * CELL)
         nc.scalar.activation(switch_out[:], v_bf[0][:, 2 * P - 1, 0:1], ACT.Abs_reciprocal_sqrt, bias=1.0, scale=0.0)
-        y_codes = [staged.tile([P, HALF], U32, name="y_codes0", offset=V_AT[1], align_bytes=64)]
-        quantize_half(y_codes[0][:], y_bytes, y_bf, 0)
-        picked = pick_values(2)
-        y_codes.append(staged.tile([P, HALF], U32, name="y_codes1", offset=V_AT[2], align_bytes=64))
-        first_codes = staged.tile([P, HALF], U32, name="first_codes", offset=V_AT[2] + 1024, align_bytes=64)
-        quantize_half(y_codes[1][:], y_bytes, y_bf, 1)
-        quantize_half(first_codes[:], v_bytes, v_bf, 0)
-        turn_pairs(picked, v_bf, 2)
+        y_codes = [place([P, HALF], U32, "y_codes0", V1_AT)]
+        quantize(y_codes[0][:], y_bytes[:, :HALF], y_bf[0][:])
+        for i in range(WARM_PASSES):
+            nc.tensor.matmul_mx(out=us_rows[:].rearrange("q t p -> q (t p)"), lhsT=y_codes[0][:, :P].bitcast(FP8X4),
+                                lhsT_scale=y_bytes[:, :P], rhs=k_codes[:].bitcast(FP8X4), rhs_scale=k_bytes[:], start=True, stop=True)
+        picked2 = pick_values(2)
+        y_codes.append(place([P, HALF], U32, "y_codes1", V2_AT))
+        first_codes = place([P, 2 * P], U32, "first_codes", V2_AT + 4 * HALF)
+        quantize(y_codes[1][:], y_bytes[:, HALF:], y_bf[1][:])
+        quantize(first_codes[:], v_bytes[:, SPANS[0]], v_bf[0][:])
+        turn_pairs(picked2, v_bf, 2)
         sums = [psum.tile([P, DV], F32, name="sum%d" % j, tag="rows%d" % j) for j in range(Q_TILES)]
         multiply(0, first_codes[:])
         for j in range(Q_TILES):
             mean_square(j, 0)
-        picked = pick_values(3)
-        third_codes = staged.tile([P, P], U32, name="third_codes", offset=V_AT[3], align_bytes=64)
-        quantize_late_values(2, third_codes[:])
-        turn_pairs(picked, v_bf, 3, nc.vector.tensor_copy)
+
+        picked3 = pick_values(3)
+        third_codes = place([P, P], U32, "third_codes", C_AT)
+        quantize(third_codes[:], v_bytes[:, SPANS[1]], v_bf[1][:, :P, :])
+        turn_pairs(picked3, v_bf, 3, nc.vector.tensor_copy)
         multiply(1, third_codes[:])
         for j in range(Q_TILES):
             mean_square(j, 1)
-        quantize_late_values(3, last_codes[:])
+        quantize(last_codes[:], v_bytes[:, SPANS[2]], v_bf[1][:, P:, :])
         multiply(2, last_codes[:])
         early = keep.tile([P, Q_TILES], F32, name="early")
         nc.vector.scalar_tensor_tensor(early[:], parts[0][:], EPS, parts[1][:], ALU.add, ALU.add)
 
-        by_half = out[0].rearrange("(h m j) e -> h j m e", h=2, j=2)
-        rows = [by_half[j // 2, j % 2] for j in range(Q_TILES)]
+        rows = out[0].rearrange("(h m i) e -> h i m e", h=2, i=2)
         for j in range(Q_TILES):
             mean_square(j, 2)
             gain = keep.tile([P, 1], F32, name="gain%d" % j)
             nc.scalar.activation(gain[:], parts[2][:, j:j + 1], ACT.Abs_reciprocal_sqrt, bias=early[:, j:j + 1])
             result = keep.tile([P, DV], F32, name="result%d" % j)
-            if j == 0:
-                for h in range(2):
-                    cols = slice(h * DV // 2, (h + 1) * DV // 2)
+            width = DV // 2 if j == 0 else DV
+            for first in range(0, DV, width):
+                cols = slice(first, first + width)
+                if j % 2 == 0:
                     nc.vector.tensor_scalar(result[:, cols], sums[j][:, cols], gain[:], None, ALU.mult)
-                    nc.sync.dma_start(rows[j][:, cols], result[:, cols])
-                continue
-            if j % 2 == 0:
-                nc.vector.tensor_scalar(result[:], sums[j][:], gain[:], None, ALU.mult)
-            else:
-                nc.scalar.activation(result[:], sums[j][:], ACT.Copy, scale=gain[:])
-            nc.sync.dma_start(rows[j], result[:])
+                else:
+                    nc.scalar.activation(result[:, cols], sums[j][:, cols], ACT.Copy, scale=gain[:])
+                nc.sync.dma_start(rows[j // 2, j % 2][:, cols], result[:, cols])

@@ -25,38 +25,36 @@ HALF = QUERIES // 2
 GROUPS = SLOTS // 32
 RUN = 16
 EPS = 1e-05
-C_ROW = 4
+SPREAD = 8
 WARM_PASSES = 3
 SPANS = (slice(0, 2 * P), slice(2 * P, 3 * P), slice(3 * P, 4 * P))
 
 LINK = 64
 ROW_BYTES = 4 * TOKENS
 CELL = 2048
-K_AT = 0
-COLUMN_AT = ROW_BYTES - 256
-C_AT = COLUMN_AT + 4 * P - LINK
-Q_BF1_AT = C_AT + LINK - CELL
-V0_AT = C_AT + ROW_BYTES
-Q_RAW0_AT = V0_AT + ROW_BYTES - LINK
-Q_RAW1_AT = Q_RAW0_AT + 2 * CELL - LINK
-V2_AT = Q_RAW0_AT + 2 * CELL
-K_CODES_AT = V2_AT + ROW_BYTES
-Q_BF0_AT = K_CODES_AT + CELL - LINK
-C_BYTES_AT = K_CODES_AT + CELL
-WARM_OUT_AT = C_BYTES_AT + SLOTS + LINK
-V1_AT = Q_BF0_AT + CELL - LINK
-C_SCALES_AT = V1_AT + ROW_BYTES
-K_BYTES_AT = C_SCALES_AT + TOKENS
-ROW_AT = K_BYTES_AT - LINK
-SIG_AT = K_BYTES_AT + SLOTS
-V_BF1_AT = SIG_AT + Q_TILES * CELL
-Y_BF1_AT = V_BF1_AT + CELL
-PICKED1_AT = Y_BF1_AT + CELL
-PICKED2_AT = PICKED1_AT + CELL
-WEIGHTS_AT = PICKED2_AT + CELL
-V_BF0_AT = WEIGHTS_AT + Q_TILES * CELL
+V1_AT = 0
+K_AT = V1_AT + ROW_BYTES - LINK
+C_CODES_AT = K_AT + CELL
+V2_AT = K_AT + ROW_BYTES - LINK
+COLUMN_AT = V2_AT
+C_AT = V2_AT + ROW_BYTES
+WEIGHTS0_AT = C_AT + ROW_BYTES
+Q_BF1_AT = WEIGHTS0_AT - LINK
+V0_AT = WEIGHTS0_AT + CELL
+Q_BF0_AT = V0_AT + ROW_BYTES - LINK
+WARM_AT = Q_BF0_AT + LINK
+K_CODES_AT = Q_BF0_AT + CELL - LINK
+Q_RAW_AT = K_CODES_AT + CELL
+SIG_AT = Q_RAW_AT + 4 * CELL
+Y_BF1_AT = SIG_AT + CELL
+WEIGHTS3_AT = Y_BF1_AT + CELL
+V_BF0_AT = WEIGHTS3_AT + CELL
 Y_BF0_AT = V_BF0_AT + CELL
 NEG_TH_AT = Y_BF0_AT - LINK
+BYTES_AT = Y_BF0_AT + CELL
+ROW_AT = BYTES_AT + SLOTS - LINK
+SCALES_AT = BYTES_AT + 4 * SLOTS
+Q_CODES0_AT = SCALES_AT + TOKENS - LINK
 
 FLOPS = 3 * 2 * 512 * 512 * 512
 
@@ -73,38 +71,34 @@ def tile_attend_at_residsig_topk_kernel(tc, qT, k_words, k_scales, c_words, c_sc
             return staged.tile(shape, dtype, name=name, offset=offset, align_bytes=64)
 
         offsets = keep.tile([P, SLOTS // 16], U16, name="offsets")
-        column = place([P, P], F32, "column", COLUMN_AT)
-        row = place([P, 2 * LINK // 4], F32, "row", ROW_AT)
-        nc.gpsimd.iota(column[:], pattern=[[1, P]], base=0, channel_multiplier=0, allow_small_or_imprecise_dtypes=True)
-        nc.gpsimd.iota(row[:, 0:1], pattern=[[0, 1]], base=0, channel_multiplier=1, allow_small_or_imprecise_dtypes=True)
-        k_scale_pool = keep.tile([P, TOKENS], U8, name="k_scale_pool", align_bytes=64)
+        k_scale_pool = place([P, TOKENS], U8, "k_scale_pool", SCALES_AT)
+        c_scale_pool = place([P, TOKENS], U8, "c_scale_pool", SCALES_AT + TOKENS)
         nc.vector.memset(k_scale_pool[:].bitcast(I32), 0)
-        ident = keep.tile([P, P], F32, name="ident")
-        nc.vector.tensor_scalar(ident[:], column[:], row[:, 0:1], None, ALU.is_equal)
-        c_scale_pool = place([P, TOKENS], U8, "c_scale_pool", C_SCALES_AT)
         nc.vector.memset(c_scale_pool[:].bitcast(I32), 0)
-        warm_in = place([P, 1], F32, "warm_in", C_AT)
-        warm_out = place([P, 1], F32, "warm_out", WARM_OUT_AT)
-        nc.vector.memset(warm_in[:], 0.0)
-        nc.scalar.activation(warm_out[:], warm_in[:], ACT.Sigmoid)
+        column = place([P, (ROW_BYTES + LINK) // 4], F32, "column", COLUMN_AT)
+        row = place([P, 2 * LINK // 4], F32, "row", ROW_AT)
+        nc.gpsimd.iota(column[:, 0:P], pattern=[[1, P]], base=0, channel_multiplier=0, allow_small_or_imprecise_dtypes=True)
+        nc.gpsimd.iota(row[:, 0:1], pattern=[[0, 1]], base=0, channel_multiplier=1, allow_small_or_imprecise_dtypes=True)
+        ident = keep.tile([P, P], F32, name="ident")
+        nc.vector.tensor_scalar(ident[:], column[:, 0:P], row[:, 0:1], None, ALU.is_equal)
+        warm_out = place([P, 1], F32, "warm_out", WARM_AT)
+        nc.scalar.activation(warm_out[:], ident[:, 0:1], ACT.Sigmoid)
 
         q_rows = qT[0].rearrange("(p t) q -> p t q", t=PACK)
 
         def load_queries(h):
-            raw = place([P, PACK, HALF], F32, "q_raw%d" % h, (Q_RAW0_AT, Q_RAW1_AT)[h])
+            raw = place([P, PACK, HALF], F32, "q_raw%d" % h, Q_RAW_AT + h * (2 * CELL - LINK))
             nc.sync.dma_start(raw[:], q_rows[:, :, h * HALF:(h + 1) * HALF])
             return raw
 
         q_first = load_queries(0)
         nc.sync.dma_start(offsets[:], offs)
         k_rows = k_scales[0].bitcast(I32).rearrange("(g r) n -> r g n", r=4)
-        c_rows = c_scales[0].bitcast(I32).rearrange("(g r) n -> r g n", r=4)
         for r in range(4):
             nc.sync.dma_start(k_scale_pool[r:P:32, :].bitcast(I32), k_rows[r])
+        nc.sync.dma_start(c_scale_pool[0:P:SPREAD, :].bitcast(I32), c_scales[0].bitcast(I32))
         k_pool = place([P, TOKENS], I32, "k_pool", K_AT)
         nc.sync.dma_start(k_pool[:], k_words[0].rearrange("p n t -> p (n t)").bitcast(I32))
-        for r in range(4):
-            nc.sync.dma_start(c_scale_pool[C_ROW + r:P:32, :].bitcast(I32), c_rows[r])
         c_pool = place([P, TOKENS], I32, "c_pool", C_AT)
         nc.sync.dma_start(c_pool[:], c_words[0].rearrange("p n t -> p (n t)").bitcast(I32))
         th_col = keep.tile([P, 2, 2], F32, name="th_col")
@@ -114,8 +108,7 @@ def tile_attend_at_residsig_topk_kernel(tc, qT, k_words, k_scales, c_words, c_sc
         neg_th = place([P, 2 * LINK // 4], F32, "neg_th", NEG_TH_AT)
         nc.gpsimd.tensor_scalar(neg_th[:, :Q_TILES], th_col[:].rearrange("m h i -> m (h i)"), -1.0, None, ALU.mult)
 
-        q_bf = [place([P, HALF, PACK], BF16, "q_bf%d" % h, (Q_BF0_AT, Q_BF1_AT)[h]) for h in range(2)]
-        q_codes = keep.tile([P, QUERIES], U32, name="q_codes", align_bytes=64)
+        q_bf = [place([P, HALF, PACK], BF16, "q_bf0", Q_BF0_AT)]
         q_bytes = keep.tile([P, QUERIES], U8, name="q_bytes", align_bytes=64)
 
         def cast_queries(h, raw, copy):
@@ -127,17 +120,24 @@ def tile_attend_at_residsig_topk_kernel(tc, qT, k_words, k_scales, c_words, c_sc
         cast_queries(0, q_first, nc.scalar.copy)
         q_second = load_queries(1)
 
-        k_codes = place([P, SLOTS], U32, "k_codes", K_CODES_AT)
-        k_bytes = place([P, SLOTS], U8, "k_bytes", K_BYTES_AT)
-        c_bytes = place([P, SLOTS], U8, "c_bytes", C_BYTES_AT)
-        c_codes = place([P, SLOTS], U32, "c_codes", K_AT)
+        k_bytes = place([P, SLOTS], U8, "k_bytes", BYTES_AT)
+        c_picked = place([P, SLOTS], U8, "c_picked", BYTES_AT + SLOTS)
+        c_bytes = place([P, SLOTS], U8, "c_bytes", Q_RAW_AT)
         nc.vector.tensor_copy(k_bytes[:], k_scale_pool[:].indirect(offsets[:]))
-        quantize(q_codes[:, :HALF], q_bytes[:, :HALF], q_bf[0][:])
+        nc.vector.tensor_copy(c_picked[:], c_scale_pool[:].indirect(offsets[:]))
+        nc.vector.tensor_copy(c_bytes[:].bitcast(I32), c_picked[:].bitcast(I32))
+        for r in range(1, 4):
+            nc.sync.dma_start(c_bytes[r:P:32, :].bitcast(I32), c_picked[SPREAD * r:P:32, :].bitcast(I32))
+
+        q_codes = [place([P, HALF], U32, "q_codes%d" % h, (Q_CODES0_AT, BYTES_AT + SLOTS)[h]) for h in range(2)]
+        k_codes = place([P, SLOTS], U32, "k_codes", K_CODES_AT)
+        c_codes = place([P, SLOTS], U32, "c_codes", C_CODES_AT)
+        quantize(q_codes[0][:], q_bytes[:, :HALF], q_bf[0][:])
         nc.vector.tensor_copy(k_codes[:], k_pool[:].bitcast(U32).indirect(offsets[:]))
-        nc.vector.tensor_copy(c_bytes[:], c_scale_pool[:].indirect(offsets[:]))
         nc.vector.tensor_copy(c_codes[:], c_pool[:].bitcast(U32).indirect(offsets[:]))
+        q_bf.append(place([P, HALF, PACK], BF16, "q_bf1", Q_BF1_AT))
         cast_queries(1, q_second, nc.vector.tensor_copy)
-        quantize(q_codes[:, HALF:], q_bytes[:, HALF:], q_bf[1][:])
+        quantize(q_codes[1][:], q_bytes[:, HALF:], q_bf[1][:])
 
         v_pool = [place([P, TOKENS], F32, "v_pool%d" % e, (V0_AT, V1_AT, V2_AT, C_AT)[e]) for e in range(V_TILES)]
         for e in range(V_TILES):
@@ -148,7 +148,7 @@ def tile_attend_at_residsig_topk_kernel(tc, qT, k_words, k_scales, c_words, c_sc
 
         def score_pass(j, codes, scale_rows, first):
             cols = slice(j * P, (j + 1) * P)
-            nc.tensor.matmul_mx(out=scores[j][:], lhsT=q_codes[:, cols].bitcast(FP8X4), lhsT_scale=q_bytes[:, cols],
+            nc.tensor.matmul_mx(out=scores[j][:], lhsT=q_codes[j // 2][:, (j % 2) * P:(j % 2 + 1) * P].bitcast(FP8X4), lhsT_scale=q_bytes[:, cols],
                                 rhs=codes[:].bitcast(FP8X4), rhs_scale=scale_rows, start=first, stop=not first)
 
         for t in range(PACK):
@@ -158,14 +158,14 @@ def tile_attend_at_residsig_topk_kernel(tc, qT, k_words, k_scales, c_words, c_sc
         for j in range(2):
             score_pass(j, k_codes, k_bytes[:], True)
         for j in range(2):
-            score_pass(j, c_codes, c_bytes[C_ROW:P, :], False)
+            score_pass(j, c_codes, c_bytes[:], False)
         for j in range(2, Q_TILES):
             score_pass(j, k_codes, k_bytes[:], True)
-            score_pass(j, c_codes, c_bytes[C_ROW:P, :], False)
+            score_pass(j, c_codes, c_bytes[:], False)
 
         last_codes = keep.tile([P, P], U32, name="last_codes", align_bytes=64)
         v_bytes = keep.tile([P, DV], U8, name="v_bytes", align_bytes=64)
-        v_bf = [place([P, 2 * P, PACK], BF16, "v_bf%d" % h, (V_BF0_AT, V_BF1_AT)[h]) for h in range(2)]
+        v_bf = [place([P, 2 * P, PACK], BF16, "v_bf0", V_BF0_AT), keep.tile([P, 2 * P, PACK], BF16, name="v_bf1", align_bytes=64)]
         y_bf = [place([P, 2 * P, PACK], BF16, "y_bf%d" % h, (Y_BF0_AT, Y_BF1_AT)[h]) for h in range(2)]
         y_bytes = keep.tile([P, QUERIES], U8, name="y_bytes", align_bytes=64)
 
@@ -178,14 +178,20 @@ def tile_attend_at_residsig_topk_kernel(tc, qT, k_words, k_scales, c_words, c_sc
             copy(dst.rearrange("p (c u) -> p c u", u=2), turned[:].rearrange("p u c -> p c u"))
 
         def pick_values(e):
-            picked = place([P, 2, GROUPS, RUN], BF16, "picked%d" % e, (SIG_AT, PICKED1_AT, PICKED2_AT, Y_BF1_AT)[e])
+            if e in (0, 3):
+                picked = place([P, 2, GROUPS, RUN], BF16, "picked%d" % e, SIG_AT if e == 0 else Y_BF1_AT)
+            else:
+                picked = keep.tile([P, 2, GROUPS, RUN], BF16, name="picked%d" % e, align_bytes=64)
             nc.vector.tensor_copy(picked[:].rearrange("e u g r -> e g u r"), v_pool[e][:].indirect(offsets[:]))
             return picked
 
         def weigh(j):
-            sig = place([P, SLOTS], F32, "sig%d" % j, SIG_AT + j * CELL)
+            sig = place([P, SLOTS], F32, "sig0", SIG_AT) if j == 0 else keep.tile([P, SLOTS], F32, name="sig%d" % j, align_bytes=64)
             nc.scalar.activation(sig[:], scores[j][:], ACT.Sigmoid, bias=neg_th[:, j:j + 1])
-            y = place([P, 2, GROUPS, RUN], BF16, "weights%d" % j, (Q_BF1_AT, WEIGHTS_AT + CELL, V0_AT, WEIGHTS_AT + 3 * CELL)[j])
+            if j == 1:
+                y = keep.tile([P, 2, GROUPS, RUN], BF16, name="weights1", align_bytes=64)
+            else:
+                y = place([P, 2, GROUPS, RUN], BF16, "weights%d" % j, (WEIGHTS0_AT, 0, V0_AT, WEIGHTS3_AT)[j])
             if j % 2 == 0:
                 nc.vector.tensor_tensor(y[:].rearrange("q u g (a t) -> q g u a t", t=PACK),
                                         sig[:].rearrange("q (g u a t) -> q g u a t", u=2, a=RUN // PACK, t=PACK),
@@ -217,7 +223,7 @@ def tile_attend_at_residsig_topk_kernel(tc, qT, k_words, k_scales, c_words, c_sc
         turn_pairs(weights[2], y_bf, 2)
         turn_pairs(weights[3], y_bf, 3)
         turn_pairs(pick_values(1), v_bf, 1)
-        switch_out = place([P, 1], F32, "switch_out", WEIGHTS_AT + 3 * CELL)
+        switch_out = place([P, 1], F32, "switch_out", WEIGHTS3_AT)
         nc.scalar.activation(switch_out[:], v_bf[0][:, 2 * P - 1, 0:1], ACT.Abs_reciprocal_sqrt, bias=1.0, scale=0.0)
         y_codes = [place([P, HALF], U32, "y_codes0", V1_AT)]
         quantize(y_codes[0][:], y_bytes[:, :HALF], y_bf[0][:])

@@ -43,18 +43,20 @@ Q_BF1_AT = WEIGHTS0_AT - LINK
 V0_AT = WEIGHTS0_AT + CELL
 Q_BF0_AT = V0_AT + ROW_BYTES - LINK
 WARM_AT = Q_BF0_AT + LINK
-K_CODES_AT = Q_BF0_AT + CELL - LINK
-Q_RAW_AT = K_CODES_AT + CELL
-SIG_AT = Q_RAW_AT + 4 * CELL
-Y_BF1_AT = SIG_AT + CELL
-WEIGHTS3_AT = Y_BF1_AT + CELL
-V_BF0_AT = WEIGHTS3_AT + CELL
+Q_RAW1_AT = Q_BF0_AT + CELL - LINK
+SIG_AT = Q_RAW1_AT + 2 * CELL
+WEIGHTS1_AT = SIG_AT + CELL
+Y_BF1_AT = WEIGHTS1_AT + CELL
+SWITCH_AT = Y_BF1_AT - LINK
+V_BF0_AT = Y_BF1_AT + CELL
 Y_BF0_AT = V_BF0_AT + CELL
 NEG_TH_AT = Y_BF0_AT - LINK
-BYTES_AT = Y_BF0_AT + CELL
-ROW_AT = BYTES_AT + SLOTS - LINK
-SCALES_AT = BYTES_AT + 4 * SLOTS
-Q_CODES0_AT = SCALES_AT + TOKENS - LINK
+C_PICKED_AT = Y_BF0_AT + CELL
+Q_RAW0_AT = C_PICKED_AT + CELL // 2
+C_SCALES_AT = Q_RAW0_AT + 2 * CELL
+K_BYTES_AT = C_SCALES_AT - LINK
+Q_CODES0_AT = C_SCALES_AT + CELL // 2
+K_SCALES_AT = C_SCALES_AT + TOKENS
 
 FLOPS = 3 * 2 * 512 * 512 * 512
 
@@ -71,12 +73,12 @@ def tile_attend_at_residsig_topk_kernel(tc, qT, k_words, k_scales, c_words, c_sc
             return staged.tile(shape, dtype, name=name, offset=offset, align_bytes=64)
 
         offsets = keep.tile([P, SLOTS // 16], U16, name="offsets")
-        k_scale_pool = place([P, TOKENS], U8, "k_scale_pool", SCALES_AT)
-        c_scale_pool = place([P, TOKENS], U8, "c_scale_pool", SCALES_AT + TOKENS)
-        nc.vector.memset(k_scale_pool[:].bitcast(I32), 0)
+        c_scale_pool = place([P, TOKENS], U8, "c_scale_pool", C_SCALES_AT)
+        k_scale_pool = place([P, TOKENS], U8, "k_scale_pool", K_SCALES_AT)
         nc.vector.memset(c_scale_pool[:].bitcast(I32), 0)
+        nc.vector.memset(k_scale_pool[:].bitcast(I32), 0)
         column = place([P, (ROW_BYTES + LINK) // 4], F32, "column", COLUMN_AT)
-        row = place([P, 2 * LINK // 4], F32, "row", ROW_AT)
+        row = place([P, 1], F32, "row", C_PICKED_AT)
         nc.gpsimd.iota(column[:, 0:P], pattern=[[1, P]], base=0, channel_multiplier=0, allow_small_or_imprecise_dtypes=True)
         nc.gpsimd.iota(row[:, 0:1], pattern=[[0, 1]], base=0, channel_multiplier=1, allow_small_or_imprecise_dtypes=True)
         ident = keep.tile([P, P], F32, name="ident")
@@ -87,16 +89,16 @@ def tile_attend_at_residsig_topk_kernel(tc, qT, k_words, k_scales, c_words, c_sc
         q_rows = qT[0].rearrange("(p t) q -> p t q", t=PACK)
 
         def load_queries(h):
-            raw = place([P, PACK, HALF], F32, "q_raw%d" % h, Q_RAW_AT + h * (2 * CELL - LINK))
+            raw = place([P, PACK, HALF], F32, "q_raw%d" % h, (Q_RAW0_AT, Q_RAW1_AT)[h])
             nc.sync.dma_start(raw[:], q_rows[:, :, h * HALF:(h + 1) * HALF])
             return raw
 
         q_first = load_queries(0)
         nc.sync.dma_start(offsets[:], offs)
+        nc.sync.dma_start(c_scale_pool[0:P:SPREAD, :].bitcast(I32), c_scales[0].bitcast(I32))
         k_rows = k_scales[0].bitcast(I32).rearrange("(g r) n -> r g n", r=4)
         for r in range(4):
             nc.sync.dma_start(k_scale_pool[r:P:32, :].bitcast(I32), k_rows[r])
-        nc.sync.dma_start(c_scale_pool[0:P:SPREAD, :].bitcast(I32), c_scales[0].bitcast(I32))
         k_pool = place([P, TOKENS], I32, "k_pool", K_AT)
         nc.sync.dma_start(k_pool[:], k_words[0].rearrange("p n t -> p (n t)").bitcast(I32))
         c_pool = place([P, TOKENS], I32, "c_pool", C_AT)
@@ -118,21 +120,21 @@ def tile_attend_at_residsig_topk_kernel(tc, qT, k_words, k_scales, c_words, c_sc
             nc.vector.quantize_mx(out=codes.bitcast(FP8X4), scales=scale_bytes, in_=values.rearrange("p c t -> p (c t)"))
 
         cast_queries(0, q_first, nc.scalar.copy)
-        q_second = load_queries(1)
 
-        k_bytes = place([P, SLOTS], U8, "k_bytes", BYTES_AT)
-        c_picked = place([P, SLOTS], U8, "c_picked", BYTES_AT + SLOTS)
-        c_bytes = place([P, SLOTS], U8, "c_bytes", Q_RAW_AT)
-        nc.vector.tensor_copy(k_bytes[:], k_scale_pool[:].indirect(offsets[:]))
+        c_picked = place([P, SLOTS], U8, "c_picked", C_PICKED_AT)
+        c_bytes = keep.tile([P, SLOTS], U8, name="c_bytes", align_bytes=64)
         nc.vector.tensor_copy(c_picked[:], c_scale_pool[:].indirect(offsets[:]))
         nc.vector.tensor_copy(c_bytes[:].bitcast(I32), c_picked[:].bitcast(I32))
         for r in range(1, 4):
             nc.sync.dma_start(c_bytes[r:P:32, :].bitcast(I32), c_picked[SPREAD * r:P:32, :].bitcast(I32))
 
-        q_codes = [place([P, HALF], U32, "q_codes%d" % h, (Q_CODES0_AT, BYTES_AT + SLOTS)[h]) for h in range(2)]
-        k_codes = place([P, SLOTS], U32, "k_codes", K_CODES_AT)
+        q_codes = [place([P, HALF], U32, "q_codes%d" % h, (Q_CODES0_AT, C_PICKED_AT)[h]) for h in range(2)]
+        k_codes = place([P, SLOTS], U32, "k_codes", K_SCALES_AT)
         c_codes = place([P, SLOTS], U32, "c_codes", C_CODES_AT)
         quantize(q_codes[0][:], q_bytes[:, :HALF], q_bf[0][:])
+        q_second = load_queries(1)
+        k_bytes = place([P, SLOTS], U8, "k_bytes", K_BYTES_AT)
+        nc.vector.tensor_copy(k_bytes[:], k_scale_pool[:].indirect(offsets[:]))
         nc.vector.tensor_copy(k_codes[:], k_pool[:].bitcast(U32).indirect(offsets[:]))
         nc.vector.tensor_copy(c_codes[:], c_pool[:].bitcast(U32).indirect(offsets[:]))
         q_bf.append(place([P, HALF, PACK], BF16, "q_bf1", Q_BF1_AT))
@@ -166,7 +168,7 @@ def tile_attend_at_residsig_topk_kernel(tc, qT, k_words, k_scales, c_words, c_sc
         last_codes = keep.tile([P, P], U32, name="last_codes", align_bytes=64)
         v_bytes = keep.tile([P, DV], U8, name="v_bytes", align_bytes=64)
         v_bf = [place([P, 2 * P, PACK], BF16, "v_bf0", V_BF0_AT), keep.tile([P, 2 * P, PACK], BF16, name="v_bf1", align_bytes=64)]
-        y_bf = [place([P, 2 * P, PACK], BF16, "y_bf%d" % h, (Y_BF0_AT, Y_BF1_AT)[h]) for h in range(2)]
+        y_bf = [place([P, 2 * P, PACK], BF16, "y_bf0", Y_BF0_AT)]
         y_bytes = keep.tile([P, QUERIES], U8, name="y_bytes", align_bytes=64)
 
         def turn_pairs(pairs, halves, i, copy=nc.scalar.copy):
@@ -188,11 +190,11 @@ def tile_attend_at_residsig_topk_kernel(tc, qT, k_words, k_scales, c_words, c_sc
         def weigh(j):
             sig = place([P, SLOTS], F32, "sig0", SIG_AT) if j == 0 else keep.tile([P, SLOTS], F32, name="sig%d" % j, align_bytes=64)
             nc.scalar.activation(sig[:], scores[j][:], ACT.Sigmoid, bias=neg_th[:, j:j + 1])
-            if j == 1:
-                y = keep.tile([P, 2, GROUPS, RUN], BF16, name="weights1", align_bytes=64)
+            if j < 2:
+                y = place([P, 2, GROUPS, RUN], BF16, "weights%d" % j, (WEIGHTS0_AT, WEIGHTS1_AT)[j])
             else:
-                y = place([P, 2, GROUPS, RUN], BF16, "weights%d" % j, (WEIGHTS0_AT, 0, V0_AT, WEIGHTS3_AT)[j])
-            if j % 2 == 0:
+                y = keep.tile([P, 2, GROUPS, RUN], BF16, name="weights%d" % j, align_bytes=64)
+            if j == 0:
                 nc.vector.tensor_tensor(y[:].rearrange("q u g (a t) -> q g u a t", t=PACK),
                                         sig[:].rearrange("q (g u a t) -> q g u a t", u=2, a=RUN // PACK, t=PACK),
                                         us_rows[:].rearrange("q t (g u a) -> q g u a t", u=2, a=RUN // PACK), ALU.mult)
@@ -220,11 +222,12 @@ def tile_attend_at_residsig_topk_kernel(tc, qT, k_words, k_scales, c_words, c_sc
         turn_pairs(weights[0], y_bf, 0)
         turn_pairs(weights[1], y_bf, 1)
         turn_pairs(picked0, v_bf, 0)
+        switch_out = place([P, 2 * LINK // 4], F32, "switch_out", SWITCH_AT)
+        nc.scalar.activation(switch_out[:, 0:1], v_bf[0][:, P - 1, 0:1], ACT.Abs_reciprocal_sqrt, bias=1.0, scale=0.0)
+        y_bf.append(place([P, 2 * P, PACK], BF16, "y_bf1", Y_BF1_AT))
         turn_pairs(weights[2], y_bf, 2)
-        turn_pairs(weights[3], y_bf, 3)
         turn_pairs(pick_values(1), v_bf, 1)
-        switch_out = place([P, 1], F32, "switch_out", WEIGHTS3_AT)
-        nc.scalar.activation(switch_out[:], v_bf[0][:, 2 * P - 1, 0:1], ACT.Abs_reciprocal_sqrt, bias=1.0, scale=0.0)
+        turn_pairs(weights[3], y_bf, 3)
         y_codes = [place([P, HALF], U32, "y_codes0", V1_AT)]
         quantize(y_codes[0][:], y_bytes[:, :HALF], y_bf[0][:])
         for i in range(WARM_PASSES):

@@ -52,10 +52,12 @@ V_BF0_AT = Y_BF1_AT + CELL
 Y_BF0_AT = V_BF0_AT + CELL
 NEG_TH_AT = Y_BF0_AT - LINK
 C_PICKED_AT = Y_BF0_AT + CELL
-Q_RAW0_AT = C_PICKED_AT + CELL // 2
+Q_RAW0_AT = C_PICKED_AT + CELL // 2 + 2 * LINK
 C_SCALES_AT = Q_RAW0_AT + 2 * CELL
 K_BYTES_AT = C_SCALES_AT - LINK
 Q_CODES0_AT = C_SCALES_AT + CELL // 2
+US_AT = Q_RAW0_AT - 2 * LINK
+TH_AT = US_AT + LINK
 K_SCALES_AT = C_SCALES_AT + TOKENS
 
 FLOPS = 3 * 2 * 512 * 512 * 512
@@ -75,10 +77,10 @@ def tile_attend_at_residsig_topk_kernel(tc, qT, k_words, k_scales, c_words, c_sc
         offsets = keep.tile([P, SLOTS // 16], U16, name="offsets")
         c_scale_pool = place([P, TOKENS], U8, "c_scale_pool", C_SCALES_AT)
         k_scale_pool = place([P, TOKENS], U8, "k_scale_pool", K_SCALES_AT)
-        nc.vector.memset(c_scale_pool[:].bitcast(I32), 0)
+        nc.gpsimd.memset(c_scale_pool[:].bitcast(I32), 0)
         nc.vector.memset(k_scale_pool[:].bitcast(I32), 0)
         column = place([P, (ROW_BYTES + LINK) // 4], F32, "column", COLUMN_AT)
-        row = place([P, 1], F32, "row", C_PICKED_AT)
+        row = place([P, (CELL // 2 + 2 * LINK) // 4], F32, "row", C_PICKED_AT)
         nc.gpsimd.iota(column[:, 0:P], pattern=[[1, P]], base=0, channel_multiplier=0, allow_small_or_imprecise_dtypes=True)
         nc.gpsimd.iota(row[:, 0:1], pattern=[[0, 1]], base=0, channel_multiplier=1, allow_small_or_imprecise_dtypes=True)
         ident = keep.tile([P, P], F32, name="ident")
@@ -101,12 +103,12 @@ def tile_attend_at_residsig_topk_kernel(tc, qT, k_words, k_scales, c_words, c_sc
             nc.sync.dma_start(k_scale_pool[r:P:32, :].bitcast(I32), k_rows[r])
         k_pool = place([P, TOKENS], I32, "k_pool", K_AT)
         nc.sync.dma_start(k_pool[:], k_words[0].rearrange("p n t -> p (n t)").bitcast(I32))
+        th_col = place([P, 2, 2], F32, "th_col", TH_AT)
+        us_col = place([P, PACK], F32, "us_col", US_AT)
+        nc.sync.dma_start(us_col[:], us[0].rearrange("(p t) o -> p (t o)", t=PACK))
+        nc.sync.dma_start(th_col[:], th[0, 0].rearrange("(h m i) -> m h i", h=2, i=2))
         c_pool = place([P, TOKENS], I32, "c_pool", C_AT)
         nc.sync.dma_start(c_pool[:], c_words[0].rearrange("p n t -> p (n t)").bitcast(I32))
-        th_col = keep.tile([P, 2, 2], F32, name="th_col")
-        us_col = keep.tile([P, PACK], F32, name="us_col")
-        nc.gpsimd.dma_start(us_col[:], us[0].rearrange("(p t) o -> p (t o)", t=PACK))
-        nc.gpsimd.dma_start(th_col[:], th[0, 0].rearrange("(h m i) -> m h i", h=2, i=2))
         neg_th = place([P, 2 * LINK // 4], F32, "neg_th", NEG_TH_AT)
         nc.gpsimd.tensor_scalar(neg_th[:, :Q_TILES], th_col[:].rearrange("m h i -> m (h i)"), -1.0, None, ALU.mult)
 

@@ -26,7 +26,6 @@ GROUPS = SLOTS // 32
 RUN = 16
 EPS = 1e-05
 SPREAD = 8
-WARM_PASSES = 3
 SPANS = (slice(0, 2 * P), slice(2 * P, 3 * P), slice(3 * P, 4 * P))
 
 LINK = 64
@@ -232,9 +231,6 @@ def tile_attend_at_residsig_topk_kernel(tc, qT, k_words, k_scales, c_words, c_sc
         turn_pairs(weights[3], y_bf, 3)
         y_codes = [place([P, HALF], U32, "y_codes0", V1_AT)]
         quantize(y_codes[0][:], y_bytes[:, :HALF], y_bf[0][:])
-        for i in range(WARM_PASSES):
-            nc.tensor.matmul_mx(out=us_rows[:].rearrange("q t p -> q (t p)"), lhsT=y_codes[0][:, :P].bitcast(FP8X4),
-                                lhsT_scale=y_bytes[:, :P], rhs=k_codes[:].bitcast(FP8X4), rhs_scale=k_bytes[:], start=True, stop=True)
         picked2 = pick_values(2)
         y_codes.append(place([P, HALF], U32, "y_codes1", V2_AT))
         first_codes = place([P, 2 * P], U32, "first_codes", V2_AT + 4 * HALF)

@@ -2,6 +2,7 @@ import math
 from contextlib import ExitStack
 
 import concourse.mybir as mybir
+from concourse.masks import make_identity
 
 F32 = mybir.dt.float32
 BF16 = mybir.dt.bfloat16
@@ -26,38 +27,20 @@ GROUPS = SLOTS // 32
 RUN = 16
 EPS = 1e-05
 SPREAD = 8
-SPANS = (slice(0, 2 * P), slice(2 * P, 3 * P), slice(3 * P, 4 * P))
+EARLY = slice(0, 2 * P)
+THIRD = slice(2 * P, 3 * P)
+LAST = slice(3 * P, DV)
 
 LINK = 64
 ROW_BYTES = 4 * TOKENS
 CELL = 2048
-V1_AT = 0
-K_AT = V1_AT + ROW_BYTES - LINK
-C_CODES_AT = K_AT + CELL
-V2_AT = K_AT + ROW_BYTES - LINK
-COLUMN_AT = V2_AT
-C_AT = V2_AT + ROW_BYTES
-WEIGHTS0_AT = C_AT + ROW_BYTES
-Q_BF1_AT = WEIGHTS0_AT - LINK
-V0_AT = WEIGHTS0_AT + CELL
-Q_BF0_AT = V0_AT + ROW_BYTES - LINK
-WARM_AT = Q_BF0_AT + LINK
-Q_RAW1_AT = Q_BF0_AT + CELL - LINK
-SIG_AT = Q_RAW1_AT + 2 * CELL
-WEIGHTS1_AT = SIG_AT + CELL
-Y_BF1_AT = WEIGHTS1_AT + CELL
-SWITCH_AT = Y_BF1_AT - LINK
-V_BF0_AT = Y_BF1_AT + CELL
-Y_BF0_AT = V_BF0_AT + CELL
-NEG_TH_AT = Y_BF0_AT - LINK
-C_PICKED_AT = Y_BF0_AT + CELL
-Q_RAW0_AT = C_PICKED_AT + CELL // 2 + 2 * LINK
-C_SCALES_AT = Q_RAW0_AT + 2 * CELL
-K_BYTES_AT = C_SCALES_AT - LINK
-Q_CODES0_AT = C_SCALES_AT + CELL // 2
-US_AT = Q_RAW0_AT - 2 * LINK
-TH_AT = US_AT + LINK
-K_SCALES_AT = C_SCALES_AT + TOKENS
+K_AT = 0
+C_AT = K_AT + ROW_BYTES
+V_AT = [C_AT + (1 + e) * ROW_BYTES for e in range(V_TILES)]
+Q_BF1_AT = V_AT[3] + ROW_BYTES
+Y_BF0_AT = Q_BF1_AT + CELL
+V_BF0_AT = Y_BF0_AT + CELL
+NEG_TH_AT = V_BF0_AT - LINK
 
 FLOPS = 3 * 2 * 512 * 512 * 512
 
@@ -68,33 +51,30 @@ def tile_attend_at_residsig_topk_kernel(tc, qT, k_words, k_scales, c_words, c_sc
         keep = ctx.enter_context(tc.tile_pool(name="keep", bufs=1))
         staged = ctx.enter_context(tc.tile_pool(name="staged", bufs=1))
         psum = ctx.enter_context(tc.psum_pool(name="psum", bufs=1))
-        turn = ctx.enter_context(tc.psum_pool(name="turn", bufs=3))
 
         def place(shape, dtype, name, offset):
             return staged.tile(shape, dtype, name=name, offset=offset, align_bytes=64)
 
+        def own(shape, dtype, name):
+            return keep.tile(shape, dtype, name=name, align_bytes=64)
+
         offsets = keep.tile([P, SLOTS // 16], U16, name="offsets")
-        c_scale_pool = place([P, TOKENS], U8, "c_scale_pool", C_SCALES_AT)
-        k_scale_pool = place([P, TOKENS], U8, "k_scale_pool", K_SCALES_AT)
+        c_scale_pool = place([P, TOKENS], U8, "c_scale_pool", V_AT[1] - LINK)
+        k_scale_pool = place([P, TOKENS], U8, "k_scale_pool", V_AT[3] - LINK)
+        c_bytes = own([P, SLOTS], U8, "c_bytes")
+        minus_one = own([P, 1], F32, "minus_one")
         nc.gpsimd.memset(c_scale_pool[:].bitcast(I32), 0)
         nc.vector.memset(k_scale_pool[:].bitcast(I32), 0)
-        column = place([P, (ROW_BYTES + LINK) // 4], F32, "column", COLUMN_AT)
-        row = place([P, (CELL // 2 + 2 * LINK) // 4], F32, "row", C_PICKED_AT)
-        nc.gpsimd.iota(column[:, 0:P], pattern=[[1, P]], base=0, channel_multiplier=0, allow_small_or_imprecise_dtypes=True)
-        nc.gpsimd.iota(row[:, 0:1], pattern=[[0, 1]], base=0, channel_multiplier=1, allow_small_or_imprecise_dtypes=True)
-        ident = keep.tile([P, P], F32, name="ident")
-        nc.vector.tensor_scalar(ident[:], column[:, 0:P], row[:, 0:1], None, ALU.is_equal)
-        warm_out = place([P, 1], F32, "warm_out", WARM_AT)
-        nc.scalar.activation(warm_out[:], ident[:, 0:1], ACT.Sigmoid)
+        nc.vector.memset(minus_one[:], -1.0)
+        nc.vector.memset(c_bytes[:].bitcast(I32), 0)
+        ident = own([P, P], F32, "ident")
+        make_identity(nc, ident[:])
+        warm_out = own([P, 1], F32, "warm_out")
+        nc.scalar.activation(warm_out[:], minus_one[:], ACT.Sigmoid)
 
         q_rows = qT[0].rearrange("(p t) q -> p t q", t=PACK)
-
-        def load_queries(h):
-            raw = place([P, PACK, HALF], F32, "q_raw%d" % h, (Q_RAW0_AT, Q_RAW1_AT)[h])
-            nc.sync.dma_start(raw[:], q_rows[:, :, h * HALF:(h + 1) * HALF])
-            return raw
-
-        q_first = load_queries(0)
+        q_raw = [own([P, PACK, HALF], F32, "q_raw%d" % h) for h in range(2)]
+        nc.sync.dma_start(q_raw[0][:], q_rows[:, :, :HALF])
         nc.sync.dma_start(offsets[:], offs)
         nc.sync.dma_start(c_scale_pool[0:P:SPREAD, :].bitcast(I32), c_scales[0].bitcast(I32))
         k_rows = k_scales[0].bitcast(I32).rearrange("(g r) n -> r g n", r=4)
@@ -102,168 +82,163 @@ def tile_attend_at_residsig_topk_kernel(tc, qT, k_words, k_scales, c_words, c_sc
             nc.sync.dma_start(k_scale_pool[r:P:32, :].bitcast(I32), k_rows[r])
         k_pool = place([P, TOKENS], I32, "k_pool", K_AT)
         nc.sync.dma_start(k_pool[:], k_words[0].rearrange("p n t -> p (n t)").bitcast(I32))
-        th_col = place([P, 2, 2], F32, "th_col", TH_AT)
-        us_col = place([P, PACK], F32, "us_col", US_AT)
+        us_col = own([P, PACK], F32, "us_col")
         nc.sync.dma_start(us_col[:], us[0].rearrange("(p t) o -> p (t o)", t=PACK))
-        nc.sync.dma_start(th_col[:], th[0, 0].rearrange("(h m i) -> m h i", h=2, i=2))
         c_pool = place([P, TOKENS], I32, "c_pool", C_AT)
         nc.sync.dma_start(c_pool[:], c_words[0].rearrange("p n t -> p (n t)").bitcast(I32))
-        neg_th = place([P, 2 * LINK // 4], F32, "neg_th", NEG_TH_AT)
-        nc.gpsimd.tensor_scalar(neg_th[:, :Q_TILES], th_col[:].rearrange("m h i -> m (h i)"), -1.0, None, ALU.mult)
 
-        q_bf = [place([P, HALF, PACK], BF16, "q_bf0", Q_BF0_AT)]
-        q_bytes = keep.tile([P, QUERIES], U8, name="q_bytes", align_bytes=64)
+        q_bf = [own([P, HALF, PACK], BF16, "q_bf0"), place([P, HALF, PACK], BF16, "q_bf1", Q_BF1_AT)]
+        q_bytes = own([P, QUERIES], U8, "q_bytes")
 
-        def cast_queries(h, raw, copy):
-            copy(q_bf[h][:].rearrange("p (i m n) t -> p m t n i", i=2, n=2), raw[:].rearrange("p t (m n i) -> p m t n i", n=2, i=2))
+        def cast_queries(h, copy):
+            copy(q_bf[h][:].rearrange("p (i m n) t -> p m t n i", i=2, n=2), q_raw[h][:].rearrange("p t (m n i) -> p m t n i", n=2, i=2))
+
+        cast_queries(0, nc.scalar.copy)
 
         def quantize(codes, scale_bytes, values):
             nc.vector.quantize_mx(out=codes.bitcast(FP8X4), scales=scale_bytes, in_=values.rearrange("p c t -> p (c t)"))
 
-        cast_queries(0, q_first, nc.scalar.copy)
-
-        c_picked = place([P, SLOTS], U8, "c_picked", C_PICKED_AT)
-        c_bytes = keep.tile([P, SLOTS], U8, name="c_bytes", align_bytes=64)
+        c_picked = own([P, SLOTS], U8, "c_picked")
         nc.vector.tensor_copy(c_picked[:], c_scale_pool[:].indirect(offsets[:]))
-        nc.vector.tensor_copy(c_bytes[:].bitcast(I32), c_picked[:].bitcast(I32))
-        for r in range(1, 4):
+        for r in range(4):
             nc.sync.dma_start(c_bytes[r:P:32, :].bitcast(I32), c_picked[SPREAD * r:P:32, :].bitcast(I32))
-
-        q_codes = [place([P, HALF], U32, "q_codes%d" % h, (Q_CODES0_AT, C_PICKED_AT)[h]) for h in range(2)]
-        k_codes = place([P, SLOTS], U32, "k_codes", K_SCALES_AT)
-        c_codes = place([P, SLOTS], U32, "c_codes", C_CODES_AT)
-        quantize(q_codes[0][:], q_bytes[:, :HALF], q_bf[0][:])
-        q_second = load_queries(1)
-        k_bytes = place([P, SLOTS], U8, "k_bytes", K_BYTES_AT)
-        nc.vector.tensor_copy(k_bytes[:], k_scale_pool[:].indirect(offsets[:]))
-        nc.vector.tensor_copy(k_codes[:], k_pool[:].bitcast(U32).indirect(offsets[:]))
-        nc.vector.tensor_copy(c_codes[:], c_pool[:].bitcast(U32).indirect(offsets[:]))
-        q_bf.append(place([P, HALF, PACK], BF16, "q_bf1", Q_BF1_AT))
-        cast_queries(1, q_second, nc.vector.tensor_copy)
-        quantize(q_codes[1][:], q_bytes[:, HALF:], q_bf[1][:])
-
-        v_pool = [place([P, TOKENS], F32, "v_pool%d" % e, (V0_AT, V1_AT, V2_AT, C_AT)[e]) for e in range(V_TILES)]
+        nc.sync.dma_start(q_raw[1][:], q_rows[:, :, HALF:])
+        th_col = own([P, 2, 2], F32, "th_col")
+        nc.sync.dma_start(th_col[:], th[0, 0].rearrange("(h m i) -> m h i", h=2, i=2))
+        neg_th = place([P, 2 * LINK // 4], F32, "neg_th", NEG_TH_AT)
+        nc.gpsimd.tensor_scalar(neg_th[:, :Q_TILES], th_col[:].rearrange("m h i -> m (h i)"), minus_one[:], None, ALU.mult)
+        v_pool = [place([P, TOKENS], F32, "v_pool%d" % e, V_AT[e]) for e in range(V_TILES)]
         for e in range(V_TILES):
             nc.sync.dma_start(v_pool[e][:], vT[e * P:(e + 1) * P, :])
 
+        k_bytes = own([P, SLOTS], U8, "k_bytes")
+        k_codes = [own([P, SLOTS // 2], U32, "k_codes%d" % s) for s in range(2)]
+        nc.vector.tensor_copy(k_bytes[:], k_scale_pool[:].indirect(offsets[:]))
         us_rows = psum.tile([P, PACK, P], F32, name="us_rows")
-        scores = [psum.tile([P, SLOTS], F32, name="score%d" % j, tag="rows%d" % j) for j in range(Q_TILES)]
-
-        def score_pass(j, codes, scale_rows, first):
-            cols = slice(j * P, (j + 1) * P)
-            nc.tensor.matmul_mx(out=scores[j][:], lhsT=q_codes[j // 2][:, (j % 2) * P:(j % 2 + 1) * P].bitcast(FP8X4), lhsT_scale=q_bytes[:, cols],
-                                rhs=codes[:].bitcast(FP8X4), rhs_scale=scale_rows, start=first, stop=not first)
-
         for t in range(PACK):
             nc.tensor.transpose(us_rows[:, t, :], us_col[:, t:t + 1].to_broadcast([P, P]), ident[:])
-        us_copy = keep.tile([P, SLOTS], F32, name="us_copy")
+        q_codes = [own([P, HALF], U32, "q_codes0")]
+        quantize(q_codes[0][:], q_bytes[:, :HALF], q_bf[0][:])
+        for s in range(2):
+            nc.vector.tensor_copy(k_codes[s][:], k_pool[:].bitcast(U32).indirect(offsets[:, s * 16:(s + 1) * 16]))
+        c_codes = own([P, SLOTS], U32, "c_codes")
+        nc.vector.tensor_copy(c_codes[:], c_pool[:].bitcast(U32).indirect(offsets[:]))
+        cast_queries(1, nc.vector.tensor_copy)
+        q_codes.append(own([P, HALF], U32, "q_codes1"))
+        quantize(q_codes[1][:], q_bytes[:, HALF:], q_bf[1][:])
+
+        scores = [psum.tile([P, SLOTS], F32, name="score%d" % j, tag="rows%d" % j) for j in range(Q_TILES)]
+        us_copy = own([P, SLOTS], F32, "us_copy")
         nc.scalar.copy(us_copy[:].rearrange("q (p t) -> q p t", t=PACK), us_rows[:].rearrange("q t p -> q p t"))
-        for j in range(2):
-            score_pass(j, k_codes, k_bytes[:], True)
-        for j in range(2):
-            score_pass(j, c_codes, c_bytes[:], False)
-        for j in range(2, Q_TILES):
-            score_pass(j, k_codes, k_bytes[:], True)
-            score_pass(j, c_codes, c_bytes[:], False)
 
-        last_codes = keep.tile([P, P], U32, name="last_codes", align_bytes=64)
-        v_bytes = keep.tile([P, DV], U8, name="v_bytes", align_bytes=64)
-        v_bf = [place([P, 2 * P, PACK], BF16, "v_bf0", V_BF0_AT), keep.tile([P, 2 * P, PACK], BF16, name="v_bf1", align_bytes=64)]
-        y_bf = [place([P, 2 * P, PACK], BF16, "y_bf0", Y_BF0_AT)]
-        y_bytes = keep.tile([P, QUERIES], U8, name="y_bytes", align_bytes=64)
+        def score_pass(j, codes, scale_rows, cols, first, last):
+            nc.tensor.matmul_mx(out=scores[j][:, cols], lhsT=q_codes[j // 2][:, (j % 2) * P:(j % 2 + 1) * P].bitcast(FP8X4),
+                                lhsT_scale=q_bytes[:, j * P:(j + 1) * P], rhs=codes[:].bitcast(FP8X4), rhs_scale=scale_rows[:, cols],
+                                start=first, stop=last)
 
-        def turn_pairs(pairs, halves, i, copy=nc.scalar.copy):
-            words = pairs[:].rearrange("c u g r -> c (u g r)").bitcast(F32)
-            turned = turn.tile([P, 2, P], F32, name="turned")
-            for u in range(2):
-                nc.tensor.transpose(turned[:, u, :], words[:, u * P:(u + 1) * P], ident[:])
-            dst = halves[i // 2][:, (i % 2) * P:(i % 2 + 1) * P, :].rearrange("p c t -> p (c t)").bitcast(F32)
-            copy(dst.rearrange("p (c u) -> p c u", u=2), turned[:].rearrange("p u c -> p c u"))
+        for s in range(2):
+            for j in range(2):
+                score_pass(j, k_codes[s], k_bytes, slice(s * HALF, (s + 1) * HALF), s == 0, False)
+        for j in range(Q_TILES):
+            for s in range(2 * (j // 2)):
+                score_pass(j, k_codes[s], k_bytes, slice(s * HALF, (s + 1) * HALF), s == 0, False)
+            score_pass(j, c_codes, c_bytes, slice(0, SLOTS), False, True)
+
+        def turn_pairs(tiles, dst, bank, copy):
+            turned = psum.tile([P, len(tiles), 2, P], F32, name="turned", tag=bank)
+            for i, pairs in enumerate(tiles):
+                words = pairs[:].rearrange("c u g r -> c (u g r)").bitcast(F32)
+                for u in range(2):
+                    nc.tensor.transpose(turned[:, i, u, :], words[:, u * P:(u + 1) * P], ident[:])
+            dst_words = dst.rearrange("p c t -> p (c t)").bitcast(F32)
+            copy(dst_words.rearrange("p (i c u) -> p i c u", i=len(tiles), u=2), turned[:].rearrange("p i u c -> p i c u"))
 
         def pick_values(e):
-            if e in (0, 3):
-                picked = place([P, 2, GROUPS, RUN], BF16, "picked%d" % e, SIG_AT if e == 0 else Y_BF1_AT)
-            else:
-                picked = keep.tile([P, 2, GROUPS, RUN], BF16, name="picked%d" % e, align_bytes=64)
+            picked = own([P, 2, GROUPS, RUN], BF16, "picked%d" % e)
             nc.vector.tensor_copy(picked[:].rearrange("e u g r -> e g u r"), v_pool[e][:].indirect(offsets[:]))
             return picked
 
+        sig = [own([P, SLOTS], F32, "sig%d" % j) for j in range(Q_TILES)]
+        for j in range(Q_TILES):
+            nc.scalar.activation(sig[j][:], scores[j][:], ACT.Sigmoid, bias=neg_th[:, j:j + 1])
+
         def weigh(j):
-            sig = place([P, SLOTS], F32, "sig0", SIG_AT) if j == 0 else keep.tile([P, SLOTS], F32, name="sig%d" % j, align_bytes=64)
-            nc.scalar.activation(sig[:], scores[j][:], ACT.Sigmoid, bias=neg_th[:, j:j + 1])
-            if j < 2:
-                y = place([P, 2, GROUPS, RUN], BF16, "weights%d" % j, (WEIGHTS0_AT, WEIGHTS1_AT)[j])
-            else:
-                y = keep.tile([P, 2, GROUPS, RUN], BF16, name="weights%d" % j, align_bytes=64)
-            if j == 0:
+            if j % 2 == 0:
+                y = place([P, 2, GROUPS, RUN], BF16, "weights%d" % j, (Q_BF1_AT, V_AT[0])[j // 2])
                 nc.vector.tensor_tensor(y[:].rearrange("q u g (a t) -> q g u a t", t=PACK),
-                                        sig[:].rearrange("q (g u a t) -> q g u a t", u=2, a=RUN // PACK, t=PACK),
+                                        sig[j][:].rearrange("q (g u a t) -> q g u a t", u=2, a=RUN // PACK, t=PACK),
                                         us_rows[:].rearrange("q t (g u a) -> q g u a t", u=2, a=RUN // PACK), ALU.mult)
             else:
-                nc.gpsimd.tensor_tensor(y[:].rearrange("q u g r -> q g u r"), sig[:].rearrange("q (g u r) -> q g u r", u=2, r=RUN),
+                y = own([P, 2, GROUPS, RUN], BF16, "weights%d" % j)
+                nc.gpsimd.tensor_tensor(y[:].rearrange("q u g r -> q g u r"), sig[j][:].rearrange("q (g u r) -> q g u r", u=2, r=RUN),
                                         us_copy[:].rearrange("q (g u r) -> q g u r", u=2, r=RUN), ALU.mult)
             return y
-
-        squares = keep.tile([P, Q_TILES, DV], F32, name="squares")
-        parts = [keep.tile([P, Q_TILES], F32, name="part%d" % s) for s in range(len(SPANS))]
-
-        def multiply(s, v_codes):
-            for j in range(Q_TILES):
-                nc.tensor.matmul_mx(out=sums[j][:, SPANS[s]], lhsT=y_codes[j // 2][:, (j % 2) * P:(j % 2 + 1) * P].bitcast(FP8X4),
-                                    lhsT_scale=y_bytes[:, j * P:(j + 1) * P], rhs=v_codes.bitcast(FP8X4),
-                                    rhs_scale=v_bytes[:, SPANS[s]], start=True, stop=True)
-
-        def mean_square(j, s):
-            nc.scalar.activation(squares[:, j, SPANS[s]], sums[j][:, SPANS[s]], ACT.Square, scale=1.0 / math.sqrt(DV),
-                                 accum_out=parts[s][:, j:j + 1])
 
         weights = [weigh(j) for j in range(2)]
         picked0 = pick_values(0)
         weights = weights + [weigh(j) for j in range(2, Q_TILES)]
-        turn_pairs(weights[0], y_bf, 0)
-        turn_pairs(weights[1], y_bf, 1)
-        turn_pairs(picked0, v_bf, 0)
-        switch_out = place([P, 2 * LINK // 4], F32, "switch_out", SWITCH_AT)
-        nc.scalar.activation(switch_out[:, 0:1], v_bf[0][:, P - 1, 0:1], ACT.Abs_reciprocal_sqrt, bias=1.0, scale=0.0)
-        y_bf.append(place([P, 2 * P, PACK], BF16, "y_bf1", Y_BF1_AT))
-        turn_pairs(weights[2], y_bf, 2)
-        turn_pairs(pick_values(1), v_bf, 1)
-        turn_pairs(weights[3], y_bf, 3)
-        y_codes = [place([P, HALF], U32, "y_codes0", V1_AT)]
+        switch_out = own([P, 1], F32, "switch_out")
+        nc.scalar.activation(switch_out[:], sig[Q_TILES - 1][:, SLOTS - 1:], ACT.Abs_reciprocal_sqrt, bias=1.0, scale=0.0)
+        picked1 = pick_values(1)
+        v_early = place([P, 2 * P, PACK], BF16, "v_early", V_AT[1] + 2 * CELL)
+        y_bf = [place([P, 2 * P, PACK], BF16, "y_bf0", Y_BF0_AT), own([P, 2 * P, PACK], BF16, "y_bf1")]
+        turn_pairs(weights[:2], y_bf[0][:], "rows2", nc.scalar.copy)
+        turn_pairs([picked0], v_early[:, :P, :], "turn0", nc.vector.tensor_copy)
+        turn_pairs(weights[2:], y_bf[1][:], "rows3", nc.scalar.copy)
+        y_bytes = own([P, QUERIES], U8, "y_bytes")
+        v_bytes = own([P, DV], U8, "v_bytes")
+        y_codes = [place([P, HALF], U32, "y_codes%d" % h, V_AT[1] + h * CELL) for h in range(2)]
+        early_codes = own([P, 2 * P], U32, "early_codes")
         quantize(y_codes[0][:], y_bytes[:, :HALF], y_bf[0][:])
-        picked2 = pick_values(2)
-        y_codes.append(place([P, HALF], U32, "y_codes1", V2_AT))
-        first_codes = place([P, 2 * P], U32, "first_codes", V2_AT + 4 * HALF)
+        turn_pairs([picked1], v_early[:, P:, :], "turn1", nc.scalar.copy)
         quantize(y_codes[1][:], y_bytes[:, HALF:], y_bf[1][:])
-        quantize(first_codes[:], v_bytes[:, SPANS[0]], v_bf[0][:])
-        turn_pairs(picked2, v_bf, 2)
+        quantize(early_codes[:], v_bytes[:, EARLY], v_early[:])
+        picked2 = pick_values(2)
+        v_late = [own([P, P, PACK], BF16, "v_late%d" % e) for e in range(2)]
+
         sums = [psum.tile([P, DV], F32, name="sum%d" % j, tag="rows%d" % j) for j in range(Q_TILES)]
-        multiply(0, first_codes[:])
+        squares = own([P, Q_TILES, DV], F32, "squares")
+        parts = [own([P, Q_TILES], F32, "part%d" % s) for s in range(3)]
+
+        def multiply(cols, v_codes):
+            for j in range(Q_TILES):
+                nc.tensor.matmul_mx(out=sums[j][:, cols], lhsT=y_codes[j // 2][:, (j % 2) * P:(j % 2 + 1) * P].bitcast(FP8X4),
+                                    lhsT_scale=y_bytes[:, j * P:(j + 1) * P], rhs=v_codes.bitcast(FP8X4),
+                                    rhs_scale=v_bytes[:, cols], start=True, stop=True)
+
+        def mean_square(j, s, cols):
+            nc.scalar.activation(squares[:, j, cols], sums[j][:, cols], ACT.Square, scale=1.0 / math.sqrt(DV),
+                                 accum_out=parts[s][:, j:j + 1])
+
+        multiply(EARLY, early_codes[:])
         for j in range(Q_TILES):
-            mean_square(j, 0)
+            mean_square(j, 0, EARLY)
+        turn_pairs([picked2], v_late[0][:], "turn2", nc.scalar.copy)
 
         picked3 = pick_values(3)
-        third_codes = place([P, P], U32, "third_codes", C_AT)
-        quantize(third_codes[:], v_bytes[:, SPANS[1]], v_bf[1][:, :P, :])
-        turn_pairs(picked3, v_bf, 3, nc.vector.tensor_copy)
-        multiply(1, third_codes[:])
-        for j in range(Q_TILES):
-            mean_square(j, 1)
-        quantize(last_codes[:], v_bytes[:, SPANS[2]], v_bf[1][:, P:, :])
-        multiply(2, last_codes[:])
-        early = keep.tile([P, Q_TILES], F32, name="early")
-        nc.vector.scalar_tensor_tensor(early[:], parts[0][:], EPS, parts[1][:], ALU.add, ALU.add)
+        third_codes = place([P, P], U32, "third_codes", V_AT[3])
+        quantize(third_codes[:], v_bytes[:, 2 * P:3 * P], v_late[0][:])
+        turn_pairs([picked3], v_late[1][:], "turn0", nc.vector.tensor_copy)
+        multiply(THIRD, third_codes[:])
+        for j in range(2):
+            mean_square(j, 1, THIRD)
+        last_codes = own([P, P], U32, "last_codes")
+        quantize(last_codes[:], v_bytes[:, 3 * P:], v_late[1][:])
+        multiply(LAST, last_codes[:])
+        early = [own([P, 2], F32, "early%d" % h) for h in range(2)]
+        nc.vector.scalar_tensor_tensor(early[0][:], parts[0][:, :2], EPS, parts[1][:, :2], ALU.add, ALU.add)
+        nc.gpsimd.tensor_scalar(early[1][:], parts[0][:, 2:], EPS, None, ALU.add)
 
         rows = out[0].rearrange("(h m i) e -> h i m e", h=2, i=2)
         for j in range(Q_TILES):
-            mean_square(j, 2)
-            gain = keep.tile([P, 1], F32, name="gain%d" % j)
-            nc.scalar.activation(gain[:], parts[2][:, j:j + 1], ACT.Abs_reciprocal_sqrt, bias=early[:, j:j + 1])
-            result = keep.tile([P, DV], F32, name="result%d" % j)
+            mean_square(j, 2, LAST if j < 2 else slice(2 * P, DV))
+            gain = own([P, 1], F32, "gain%d" % j)
+            nc.scalar.activation(gain[:], parts[2][:, j:j + 1], ACT.Abs_reciprocal_sqrt, bias=early[j // 2][:, j % 2:j % 2 + 1])
+            result = own([P, DV], F32, "result%d" % j)
             width = DV // 2 if j == 0 else DV
             for first in range(0, DV, width):
                 cols = slice(first, first + width)
-                if j % 2 == 0:
+                if j < Q_TILES - 1:
                     nc.vector.tensor_scalar(result[:, cols], sums[j][:, cols], gain[:], None, ALU.mult)
                 else:
                     nc.scalar.activation(result[:, cols], sums[j][:, cols], ACT.Copy, scale=gain[:])

@@ -58,6 +58,8 @@ def tile_attend_at_residsig_topk_kernel(tc, qT, k_words, k_scales, c_words, c_sc
         def own(shape, dtype, name):
             return keep.tile(shape, dtype, name=name, align_bytes=64)
 
+        us_col = own([P, PACK], F32, "us_col")
+        nc.sync.dma_start(us_col[:], us[0].rearrange("(p t) o -> p (t o)", t=PACK))
         offsets = keep.tile([P, SLOTS // 16], U16, name="offsets")
         c_scale_pool = place([P, TOKENS], U8, "c_scale_pool", V_AT[1] - LINK)
         k_scale_pool = place([P, TOKENS], U8, "k_scale_pool", V_AT[3] - LINK)
@@ -72,9 +74,8 @@ def tile_attend_at_residsig_topk_kernel(tc, qT, k_words, k_scales, c_words, c_sc
         warm_out = own([P, 1], F32, "warm_out")
         nc.scalar.activation(warm_out[:], minus_one[:], ACT.Sigmoid)
 
-        q_rows = qT[0].rearrange("(p t) q -> p t q", t=PACK)
-        q_raw = [own([P, PACK, HALF], F32, "q_raw%d" % h) for h in range(2)]
-        nc.sync.dma_start(q_raw[0][:], q_rows[:, :, :HALF])
+        q_raw = own([P, PACK, QUERIES], F32, "q_raw")
+        nc.sync.dma_start(q_raw[:], qT[0].rearrange("(p t) q -> p t q", t=PACK))
         nc.sync.dma_start(offsets[:], offs)
         nc.sync.dma_start(c_scale_pool[0:P:SPREAD, :].bitcast(I32), c_scales[0].bitcast(I32))
         k_rows = k_scales[0].bitcast(I32).rearrange("(g r) n -> r g n", r=4)
@@ -82,18 +83,18 @@ def tile_attend_at_residsig_topk_kernel(tc, qT, k_words, k_scales, c_words, c_sc
             nc.sync.dma_start(k_scale_pool[r:P:32, :].bitcast(I32), k_rows[r])
         k_pool = place([P, TOKENS], I32, "k_pool", K_AT)
         nc.sync.dma_start(k_pool[:], k_words[0].rearrange("p n t -> p (n t)").bitcast(I32))
-        us_col = own([P, PACK], F32, "us_col")
-        nc.sync.dma_start(us_col[:], us[0].rearrange("(p t) o -> p (t o)", t=PACK))
         c_pool = place([P, TOKENS], I32, "c_pool", C_AT)
         nc.sync.dma_start(c_pool[:], c_words[0].rearrange("p n t -> p (n t)").bitcast(I32))
+        th_col = own([P, 2, 2], F32, "th_col")
+        nc.sync.dma_start(th_col[:], th[0, 0].rearrange("(h m i) -> m h i", h=2, i=2))
+        neg_th = place([P, 2 * LINK // 4], F32, "neg_th", NEG_TH_AT)
+        nc.gpsimd.tensor_scalar(neg_th[:, :Q_TILES], th_col[:].rearrange("m h i -> m (h i)"), minus_one[:], None, ALU.mult)
 
         q_bf = [own([P, HALF, PACK], BF16, "q_bf0"), place([P, HALF, PACK], BF16, "q_bf1", Q_BF1_AT)]
         q_bytes = own([P, QUERIES], U8, "q_bytes")
-
-        def cast_queries(h, copy):
-            copy(q_bf[h][:].rearrange("p (i m n) t -> p m t n i", i=2, n=2), q_raw[h][:].rearrange("p t (m n i) -> p m t n i", n=2, i=2))
-
-        cast_queries(0, nc.scalar.copy)
+        for h in range(2):
+            nc.scalar.copy(q_bf[h][:].rearrange("p (i m n) t -> p m t n i", i=2, n=2),
+                           q_raw[:, :, h * HALF:(h + 1) * HALF].rearrange("p t (m n i) -> p m t n i", n=2, i=2))
 
         def quantize(codes, scale_bytes, values):
             nc.vector.quantize_mx(out=codes.bitcast(FP8X4), scales=scale_bytes, in_=values.rearrange("p c t -> p (c t)"))
@@ -102,11 +103,6 @@ def tile_attend_at_residsig_topk_kernel(tc, qT, k_words, k_scales, c_words, c_sc
         nc.vector.tensor_copy(c_picked[:], c_scale_pool[:].indirect(offsets[:]))
         for r in range(4):
             nc.sync.dma_start(c_bytes[r:P:32, :].bitcast(I32), c_picked[SPREAD * r:P:32, :].bitcast(I32))
-        nc.sync.dma_start(q_raw[1][:], q_rows[:, :, HALF:])
-        th_col = own([P, 2, 2], F32, "th_col")
-        nc.sync.dma_start(th_col[:], th[0, 0].rearrange("(h m i) -> m h i", h=2, i=2))
-        neg_th = place([P, 2 * LINK // 4], F32, "neg_th", NEG_TH_AT)
-        nc.gpsimd.tensor_scalar(neg_th[:, :Q_TILES], th_col[:].rearrange("m h i -> m (h i)"), minus_one[:], None, ALU.mult)
         v_pool = [place([P, TOKENS], F32, "v_pool%d" % e, V_AT[e]) for e in range(V_TILES)]
         for e in range(V_TILES):
             nc.sync.dma_start(v_pool[e][:], vT[e * P:(e + 1) * P, :])
@@ -121,11 +117,10 @@ def tile_attend_at_residsig_topk_kernel(tc, qT, k_words, k_scales, c_words, c_sc
         quantize(q_codes[0][:], q_bytes[:, :HALF], q_bf[0][:])
         for s in range(2):
             nc.vector.tensor_copy(k_codes[s][:], k_pool[:].bitcast(U32).indirect(offsets[:, s * 16:(s + 1) * 16]))
-        c_codes = own([P, SLOTS], U32, "c_codes")
-        nc.vector.tensor_copy(c_codes[:], c_pool[:].bitcast(U32).indirect(offsets[:]))
-        cast_queries(1, nc.vector.tensor_copy)
-        q_codes.append(own([P, HALF], U32, "q_codes1"))
+        q_codes.append(place([P, HALF], U32, "q_codes1", K_AT))
         quantize(q_codes[1][:], q_bytes[:, HALF:], q_bf[1][:])
+        c_codes = place([P, SLOTS], U32, "c_codes", Q_BF1_AT)
+        nc.vector.tensor_copy(c_codes[:], c_pool[:].bitcast(U32).indirect(offsets[:]))
 
         scores = [psum.tile([P, SLOTS], F32, name="score%d" % j, tag="rows%d" % j) for j in range(Q_TILES)]
         us_copy = own([P, SLOTS], F32, "us_copy")
@@ -136,12 +131,11 @@ def tile_attend_at_residsig_topk_kernel(tc, qT, k_words, k_scales, c_words, c_sc
                                 lhsT_scale=q_bytes[:, j * P:(j + 1) * P], rhs=codes[:].bitcast(FP8X4), rhs_scale=scale_rows[:, cols],
                                 start=first, stop=last)
 
-        for s in range(2):
-            for j in range(2):
-                score_pass(j, k_codes[s], k_bytes, slice(s * HALF, (s + 1) * HALF), s == 0, False)
+        for h in range(2):
+            for s in range(2):
+                for j in (2 * h, 2 * h + 1):
+                    score_pass(j, k_codes[s], k_bytes, slice(s * HALF, (s + 1) * HALF), s == 0, False)
         for j in range(Q_TILES):
-            for s in range(2 * (j // 2)):
-                score_pass(j, k_codes[s], k_bytes, slice(s * HALF, (s + 1) * HALF), s == 0, False)
             score_pass(j, c_codes, c_bytes, slice(0, SLOTS), False, True)
 
         def turn_pairs(tiles, dst, bank, copy):
@@ -163,8 +157,8 @@ def tile_attend_at_residsig_topk_kernel(tc, qT, k_words, k_scales, c_words, c_sc
             nc.scalar.activation(sig[j][:], scores[j][:], ACT.Sigmoid, bias=neg_th[:, j:j + 1])
 
         def weigh(j):
-            if j % 2 == 0:
-                y = place([P, 2, GROUPS, RUN], BF16, "weights%d" % j, (Q_BF1_AT, V_AT[0])[j // 2])
+            if j % 2 == 1:
+                y = place([P, 2, GROUPS, RUN], BF16, "weights%d" % j, V_AT[j // 2])
                 nc.vector.tensor_tensor(y[:].rearrange("q u g (a t) -> q g u a t", t=PACK),
                                         sig[j][:].rearrange("q (g u a t) -> q g u a t", u=2, a=RUN // PACK, t=PACK),
                                         us_rows[:].rearrange("q t (g u a) -> q g u a t", u=2, a=RUN // PACK), ALU.mult)
@@ -174,31 +168,31 @@ def tile_attend_at_residsig_topk_kernel(tc, qT, k_words, k_scales, c_words, c_sc
                                         us_copy[:].rearrange("q (g u r) -> q g u r", u=2, r=RUN), ALU.mult)
             return y
 
-        weights = [weigh(j) for j in range(2)]
         picked0 = pick_values(0)
-        weights = weights + [weigh(j) for j in range(2, Q_TILES)]
+        weights = [weigh(j) for j in range(3)]
         switch_out = own([P, 1], F32, "switch_out")
         nc.scalar.activation(switch_out[:], sig[Q_TILES - 1][:, SLOTS - 1:], ACT.Abs_reciprocal_sqrt, bias=1.0, scale=0.0)
         picked1 = pick_values(1)
-        v_early = place([P, 2 * P, PACK], BF16, "v_early", V_AT[1] + 2 * CELL)
+        weights.append(weigh(3))
+        picked2 = pick_values(2)
+        v_early = own([P, 2 * P, PACK], BF16, "v_early")
         y_bf = [place([P, 2 * P, PACK], BF16, "y_bf0", Y_BF0_AT), own([P, 2 * P, PACK], BF16, "y_bf1")]
-        turn_pairs(weights[:2], y_bf[0][:], "rows2", nc.scalar.copy)
-        turn_pairs([picked0], v_early[:, :P, :], "turn0", nc.vector.tensor_copy)
+        v_late = [own([P, P, PACK], BF16, "v_late%d" % e) for e in range(2)]
+        turn_pairs(weights[:2], y_bf[0][:], "turn0", nc.scalar.copy)
+        turn_pairs([picked0, picked1], v_early[:], "turn1", nc.scalar.copy)
         turn_pairs(weights[2:], y_bf[1][:], "rows3", nc.scalar.copy)
+        turn_pairs([picked2], v_late[0][:], "turn2", nc.scalar.copy)
         y_bytes = own([P, QUERIES], U8, "y_bytes")
         v_bytes = own([P, DV], U8, "v_bytes")
-        y_codes = [place([P, HALF], U32, "y_codes%d" % h, V_AT[1] + h * CELL) for h in range(2)]
-        early_codes = own([P, 2 * P], U32, "early_codes")
+        y_codes = [place([P, HALF], U32, "y_codes%d" % h, V_AT[2] + h * CELL) for h in range(2)]
+        early_codes = place([P, 2 * P], U32, "early_codes", V_AT[2] + 2 * CELL)
         quantize(y_codes[0][:], y_bytes[:, :HALF], y_bf[0][:])
-        turn_pairs([picked1], v_early[:, P:, :], "turn1", nc.scalar.copy)
-        quantize(y_codes[1][:], y_bytes[:, HALF:], y_bf[1][:])
         quantize(early_codes[:], v_bytes[:, EARLY], v_early[:])
-        picked2 = pick_values(2)
-        v_late = [own([P, P, PACK], BF16, "v_late%d" % e) for e in range(2)]
+        quantize(y_codes[1][:], y_bytes[:, HALF:], y_bf[1][:])
 
         sums = [psum.tile([P, DV], F32, name="sum%d" % j, tag="rows%d" % j) for j in range(Q_TILES)]
         squares = own([P, Q_TILES, DV], F32, "squares")
-        parts = [own([P, Q_TILES], F32, "part%d" % s) for s in range(3)]
+        parts = [own([P, Q_TILES], F32, "part%d" % s) for s in range(2)]
 
         def multiply(cols, v_codes):
             for j in range(Q_TILES):
@@ -213,27 +207,23 @@ def tile_attend_at_residsig_topk_kernel(tc, qT, k_words, k_scales, c_words, c_sc
         multiply(EARLY, early_codes[:])
         for j in range(Q_TILES):
             mean_square(j, 0, EARLY)
-        turn_pairs([picked2], v_late[0][:], "turn2", nc.scalar.copy)
 
         picked3 = pick_values(3)
         third_codes = place([P, P], U32, "third_codes", V_AT[3])
         quantize(third_codes[:], v_bytes[:, 2 * P:3 * P], v_late[0][:])
         turn_pairs([picked3], v_late[1][:], "turn0", nc.vector.tensor_copy)
         multiply(THIRD, third_codes[:])
-        for j in range(2):
-            mean_square(j, 1, THIRD)
         last_codes = own([P, P], U32, "last_codes")
         quantize(last_codes[:], v_bytes[:, 3 * P:], v_late[1][:])
         multiply(LAST, last_codes[:])
-        early = [own([P, 2], F32, "early%d" % h) for h in range(2)]
-        nc.vector.scalar_tensor_tensor(early[0][:], parts[0][:, :2], EPS, parts[1][:, :2], ALU.add, ALU.add)
-        nc.gpsimd.tensor_scalar(early[1][:], parts[0][:, 2:], EPS, None, ALU.add)
+        early = own([P, Q_TILES], F32, "early")
+        nc.gpsimd.tensor_scalar(early[:], parts[0][:], EPS, None, ALU.add)
 
         rows = out[0].rearrange("(h m i) e -> h i m e", h=2, i=2)
         for j in range(Q_TILES):
-            mean_square(j, 2, LAST if j < 2 else slice(2 * P, DV))
+            mean_square(j, 1, slice(2 * P, DV))
             gain = own([P, 1], F32, "gain%d" % j)
-            nc.scalar.activation(gain[:], parts[2][:, j:j + 1], ACT.Abs_reciprocal_sqrt, bias=early[j // 2][:, j % 2:j % 2 + 1])
+            nc.scalar.activation(gain[:], parts[1][:, j:j + 1], ACT.Abs_reciprocal_sqrt, bias=early[:, j:j + 1])
             result = own([P, DV], F32, "result%d" % j)
             width = DV // 2 if j == 0 else DV
             for first in range(0, DV, width):

@@ -2,7 +2,6 @@ import math
 from contextlib import ExitStack
 
 import concourse.mybir as mybir
-from concourse.masks import make_identity
 
 F32 = mybir.dt.float32
 BF16 = mybir.dt.bfloat16
@@ -40,6 +39,7 @@ V_AT = [C_AT + (1 + e) * ROW_BYTES for e in range(V_TILES)]
 Q_BF1_AT = V_AT[3] + ROW_BYTES
 Y_BF0_AT = Q_BF1_AT + CELL
 V_BF0_AT = Y_BF0_AT + CELL
+WEIGHTS0_AT = V_BF0_AT + LINK
 NEG_TH_AT = V_BF0_AT - LINK
 
 FLOPS = 3 * 2 * 512 * 512 * 512
@@ -70,7 +70,9 @@ def tile_attend_at_residsig_topk_kernel(tc, qT, k_words, k_scales, c_words, c_sc
         nc.vector.memset(minus_one[:], -1.0)
         nc.vector.memset(c_bytes[:].bitcast(I32), 0)
         ident = own([P, P], F32, "ident")
-        make_identity(nc, ident[:])
+        diagonal = own([P, P], F32, "diagonal")
+        nc.gpsimd.iota(diagonal[:], pattern=[[1, P]], base=0, channel_multiplier=-1, allow_small_or_imprecise_dtypes=True)
+        nc.gpsimd.tensor_scalar(ident[:], diagonal[:], 0.0, None, ALU.is_equal)
         warm_out = own([P, 1], F32, "warm_out")
         nc.scalar.activation(warm_out[:], minus_one[:], ACT.Sigmoid)
 
@@ -163,67 +165,71 @@ def tile_attend_at_residsig_topk_kernel(tc, qT, k_words, k_scales, c_words, c_sc
                                         sig[j][:].rearrange("q (g u a t) -> q g u a t", u=2, a=RUN // PACK, t=PACK),
                                         us_rows[:].rearrange("q t (g u a) -> q g u a t", u=2, a=RUN // PACK), ALU.mult)
             else:
-                y = own([P, 2, GROUPS, RUN], BF16, "weights%d" % j)
+                y = own([P, 2, GROUPS, RUN], BF16, "weights2") if j else place([P, 2, GROUPS, RUN], BF16, "weights0", WEIGHTS0_AT)
                 nc.gpsimd.tensor_tensor(y[:].rearrange("q u g r -> q g u r"), sig[j][:].rearrange("q (g u r) -> q g u r", u=2, r=RUN),
                                         us_copy[:].rearrange("q (g u r) -> q g u r", u=2, r=RUN), ALU.mult)
             return y
 
         picked0 = pick_values(0)
         weights = [weigh(j) for j in range(3)]
-        switch_out = own([P, 1], F32, "switch_out")
-        nc.scalar.activation(switch_out[:], sig[Q_TILES - 1][:, SLOTS - 1:], ACT.Abs_reciprocal_sqrt, bias=1.0, scale=0.0)
         picked1 = pick_values(1)
         weights.append(weigh(3))
-        picked2 = pick_values(2)
-        v_early = own([P, 2 * P, PACK], BF16, "v_early")
+        v_early = place([P, 2 * P, PACK], BF16, "v_early", WEIGHTS0_AT)
         y_bf = [place([P, 2 * P, PACK], BF16, "y_bf0", Y_BF0_AT), own([P, 2 * P, PACK], BF16, "y_bf1")]
-        v_late = [own([P, P, PACK], BF16, "v_late%d" % e) for e in range(2)]
         turn_pairs(weights[:2], y_bf[0][:], "turn0", nc.scalar.copy)
         turn_pairs([picked0, picked1], v_early[:], "turn1", nc.scalar.copy)
-        turn_pairs(weights[2:], y_bf[1][:], "rows3", nc.scalar.copy)
-        turn_pairs([picked2], v_late[0][:], "turn2", nc.scalar.copy)
+        switch_out = own([P, 1], F32, "switch_out")
+        nc.scalar.activation(switch_out[:], v_early[:, 2 * P - 1, 0:1], ACT.Abs_reciprocal_sqrt, bias=1.0, scale=0.0)
+        turn_pairs(weights[2:], y_bf[1][:], "turn1", nc.scalar.copy)
         y_bytes = own([P, QUERIES], U8, "y_bytes")
         v_bytes = own([P, DV], U8, "v_bytes")
-        y_codes = [place([P, HALF], U32, "y_codes%d" % h, V_AT[2] + h * CELL) for h in range(2)]
-        early_codes = place([P, 2 * P], U32, "early_codes", V_AT[2] + 2 * CELL)
+        y_codes = [place([P, HALF], U32, "y_codes0", V_AT[1] + CELL)]
+        v_codes = own([P, DV], U32, "v_codes")
         quantize(y_codes[0][:], y_bytes[:, :HALF], y_bf[0][:])
-        quantize(early_codes[:], v_bytes[:, EARLY], v_early[:])
-        quantize(y_codes[1][:], y_bytes[:, HALF:], y_bf[1][:])
+        quantize(v_codes[:, EARLY], v_bytes[:, EARLY], v_early[:])
+        picked2 = pick_values(2)
 
         sums = [psum.tile([P, DV], F32, name="sum%d" % j, tag="rows%d" % j) for j in range(Q_TILES)]
         squares = own([P, Q_TILES, DV], F32, "squares")
         parts = [own([P, Q_TILES], F32, "part%d" % s) for s in range(2)]
 
-        def multiply(cols, v_codes):
-            for j in range(Q_TILES):
-                nc.tensor.matmul_mx(out=sums[j][:, cols], lhsT=y_codes[j // 2][:, (j % 2) * P:(j % 2 + 1) * P].bitcast(FP8X4),
-                                    lhsT_scale=y_bytes[:, j * P:(j + 1) * P], rhs=v_codes.bitcast(FP8X4),
-                                    rhs_scale=v_bytes[:, cols], start=True, stop=True)
+        def multiply(j, cols):
+            nc.tensor.matmul_mx(out=sums[j][:, cols], lhsT=y_codes[j // 2][:, (j % 2) * P:(j % 2 + 1) * P].bitcast(FP8X4),
+                                lhsT_scale=y_bytes[:, j * P:(j + 1) * P], rhs=v_codes[:, cols].bitcast(FP8X4),
+                                rhs_scale=v_bytes[:, cols], start=True, stop=True)
 
         def mean_square(j, s, cols):
             nc.scalar.activation(squares[:, j, cols], sums[j][:, cols], ACT.Square, scale=1.0 / math.sqrt(DV),
                                  accum_out=parts[s][:, j:j + 1])
 
-        multiply(EARLY, early_codes[:])
-        for j in range(Q_TILES):
+        for j in range(2):
+            multiply(j, EARLY)
             mean_square(j, 0, EARLY)
+        early = [own([P, 2], F32, "early")]
+        nc.gpsimd.tensor_scalar(early[0][:], parts[0][:, :2], EPS, None, ALU.add)
 
         picked3 = pick_values(3)
-        third_codes = place([P, P], U32, "third_codes", V_AT[3])
-        quantize(third_codes[:], v_bytes[:, 2 * P:3 * P], v_late[0][:])
+        y_codes.append(place([P, HALF], U32, "y_codes1", V_AT[3]))
+        quantize(y_codes[1][:], y_bytes[:, HALF:], y_bf[1][:])
+        multiply(2, EARLY)
+        v_late = [place([P, P, PACK], BF16, "v_late0", V_AT[3] + CELL), own([P, P, PACK], BF16, "v_late1")]
+        turn_pairs([picked2], v_late[0][:], "turn2", nc.scalar.copy)
         turn_pairs([picked3], v_late[1][:], "turn0", nc.vector.tensor_copy)
-        multiply(THIRD, third_codes[:])
-        last_codes = own([P, P], U32, "last_codes")
-        quantize(last_codes[:], v_bytes[:, 3 * P:], v_late[1][:])
-        multiply(LAST, last_codes[:])
-        early = own([P, Q_TILES], F32, "early")
-        nc.gpsimd.tensor_scalar(early[:], parts[0][:], EPS, None, ALU.add)
+        mean_square(2, 0, EARLY)
+        early.append(own([P, 1], F32, "early_third"))
+        nc.gpsimd.tensor_scalar(early[1][:], parts[0][:, 2:3], EPS, None, ALU.add)
+        for e, cols in enumerate((THIRD, LAST)):
+            quantize(v_codes[:, cols], v_bytes[:, cols], v_late[e][:])
+            for j in range(2):
+                multiply(j, cols)
+        multiply(2, slice(2 * P, DV))
+        multiply(3, slice(0, DV))
 
         rows = out[0].rearrange("(h m i) e -> h i m e", h=2, i=2)
         for j in range(Q_TILES):
-            mean_square(j, 1, slice(2 * P, DV))
+            mean_square(j, 1, slice(2 * P if j < 3 else 0, DV))
             gain = own([P, 1], F32, "gain%d" % j)
-            nc.scalar.activation(gain[:], parts[1][:, j:j + 1], ACT.Abs_reciprocal_sqrt, bias=early[:, j:j + 1])
+            nc.scalar.activation(gain[:], parts[1][:, j:j + 1], ACT.Abs_reciprocal_sqrt, bias=early[j // 2][:, j % 2:j % 2 + 1] if j < 3 else EPS)
             result = own([P, DV], F32, "result%d" % j)
             width = DV // 2 if j == 0 else DV
             for first in range(0, DV, width):

@@ -40,6 +40,9 @@ Q_BF1_AT = V_AT[3] + ROW_BYTES
 Y_BF0_AT = Q_BF1_AT + CELL
 V_BF0_AT = Y_BF0_AT + CELL
 WEIGHTS0_AT = V_BF0_AT + LINK
+Q_BF0_AT = V_BF0_AT + 6 * CELL
+Q_CODES_AT = Q_BF0_AT + CELL
+US_AT = Q_CODES_AT + CELL // 2 - LINK
 NEG_TH_AT = V_BF0_AT - LINK
 
 FLOPS = 3 * 2 * 512 * 512 * 512
@@ -58,8 +61,6 @@ def tile_attend_at_residsig_topk_kernel(tc, qT, k_words, k_scales, c_words, c_sc
         def own(shape, dtype, name):
             return keep.tile(shape, dtype, name=name, align_bytes=64)
 
-        us_col = own([P, PACK], F32, "us_col")
-        nc.sync.dma_start(us_col[:], us[0].rearrange("(p t) o -> p (t o)", t=PACK))
         offsets = keep.tile([P, SLOTS // 16], U16, name="offsets")
         c_scale_pool = place([P, TOKENS], U8, "c_scale_pool", V_AT[1] - LINK)
         k_scale_pool = place([P, TOKENS], U8, "k_scale_pool", V_AT[3] - LINK)
@@ -85,6 +86,8 @@ def tile_attend_at_residsig_topk_kernel(tc, qT, k_words, k_scales, c_words, c_sc
             nc.sync.dma_start(k_scale_pool[r:P:32, :].bitcast(I32), k_rows[r])
         k_pool = place([P, TOKENS], I32, "k_pool", K_AT)
         nc.sync.dma_start(k_pool[:], k_words[0].rearrange("p n t -> p (n t)").bitcast(I32))
+        us_col = place([P, 2 * LINK // 4], F32, "us_col", US_AT)
+        nc.sync.dma_start(us_col[:, :PACK], us[0].rearrange("(p t) o -> p (t o)", t=PACK))
         c_pool = place([P, TOKENS], I32, "c_pool", C_AT)
         nc.sync.dma_start(c_pool[:], c_words[0].rearrange("p n t -> p (n t)").bitcast(I32))
         th_col = own([P, 2, 2], F32, "th_col")
@@ -92,7 +95,7 @@ def tile_attend_at_residsig_topk_kernel(tc, qT, k_words, k_scales, c_words, c_sc
         neg_th = place([P, 2 * LINK // 4], F32, "neg_th", NEG_TH_AT)
         nc.gpsimd.tensor_scalar(neg_th[:, :Q_TILES], th_col[:].rearrange("m h i -> m (h i)"), minus_one[:], None, ALU.mult)
 
-        q_bf = [own([P, HALF, PACK], BF16, "q_bf0"), place([P, HALF, PACK], BF16, "q_bf1", Q_BF1_AT)]
+        q_bf = [place([P, HALF, PACK], BF16, "q_bf0", Q_BF0_AT), place([P, HALF, PACK], BF16, "q_bf1", Q_BF1_AT)]
         q_bytes = own([P, QUERIES], U8, "q_bytes")
         for h in range(2):
             nc.scalar.copy(q_bf[h][:].rearrange("p (i m n) t -> p m t n i", i=2, n=2),
@@ -110,17 +113,17 @@ def tile_attend_at_residsig_topk_kernel(tc, qT, k_words, k_scales, c_words, c_sc
             nc.sync.dma_start(v_pool[e][:], vT[e * P:(e + 1) * P, :])
 
         k_bytes = own([P, SLOTS], U8, "k_bytes")
-        k_codes = [own([P, SLOTS // 2], U32, "k_codes%d" % s) for s in range(2)]
+        k_codes = [own([P, SLOTS // 2], U32, "k_codes0")]
         nc.vector.tensor_copy(k_bytes[:], k_scale_pool[:].indirect(offsets[:]))
         us_rows = psum.tile([P, PACK, P], F32, name="us_rows")
         for t in range(PACK):
             nc.tensor.transpose(us_rows[:, t, :], us_col[:, t:t + 1].to_broadcast([P, P]), ident[:])
-        q_codes = [own([P, HALF], U32, "q_codes0")]
-        quantize(q_codes[0][:], q_bytes[:, :HALF], q_bf[0][:])
-        for s in range(2):
-            nc.vector.tensor_copy(k_codes[s][:], k_pool[:].bitcast(U32).indirect(offsets[:, s * 16:(s + 1) * 16]))
-        q_codes.append(place([P, HALF], U32, "q_codes1", K_AT))
-        quantize(q_codes[1][:], q_bytes[:, HALF:], q_bf[1][:])
+        nc.vector.tensor_copy(k_codes[0][:], k_pool[:].bitcast(U32).indirect(offsets[:, :16]))
+        q_codes = [place([P, HALF], U32, "q_codes%d" % h, Q_CODES_AT + h * CELL // 2) for h in range(2)]
+        for h in range(2):
+            quantize(q_codes[h][:], q_bytes[:, h * HALF:(h + 1) * HALF], q_bf[h][:])
+        k_codes.append(place([P, SLOTS // 2], U32, "k_codes1", Q_BF0_AT))
+        nc.vector.tensor_copy(k_codes[1][:], k_pool[:].bitcast(U32).indirect(offsets[:, 16:]))
         c_codes = place([P, SLOTS], U32, "c_codes", Q_BF1_AT)
         nc.vector.tensor_copy(c_codes[:], c_pool[:].bitcast(U32).indirect(offsets[:]))
 
@@ -133,10 +136,9 @@ def tile_attend_at_residsig_topk_kernel(tc, qT, k_words, k_scales, c_words, c_sc
                                 lhsT_scale=q_bytes[:, j * P:(j + 1) * P], rhs=codes[:].bitcast(FP8X4), rhs_scale=scale_rows[:, cols],
                                 start=first, stop=last)
 
-        for h in range(2):
-            for s in range(2):
-                for j in (2 * h, 2 * h + 1):
-                    score_pass(j, k_codes[s], k_bytes, slice(s * HALF, (s + 1) * HALF), s == 0, False)
+        for s in range(2):
+            for j in range(Q_TILES):
+                score_pass(j, k_codes[s], k_bytes, slice(s * HALF, (s + 1) * HALF), s == 0, False)
         for j in range(Q_TILES):
             score_pass(j, c_codes, c_bytes, slice(0, SLOTS), False, True)
 
@@ -202,28 +204,33 @@ def tile_attend_at_residsig_topk_kernel(tc, qT, k_words, k_scales, c_words, c_sc
             nc.scalar.activation(squares[:, j, cols], sums[j][:, cols], ACT.Square, scale=1.0 / math.sqrt(DV),
                                  accum_out=parts[s][:, j:j + 1])
 
+        kept = [own([P, 2 * P], F32, "kept%d" % j) for j in range(3)]
         for j in range(2):
             multiply(j, EARLY)
-            mean_square(j, 0, EARLY)
-        early = [own([P, 2], F32, "early")]
-        nc.gpsimd.tensor_scalar(early[0][:], parts[0][:, :2], EPS, None, ALU.add)
+            nc.scalar.copy(kept[j][:], sums[j][:, EARLY])
 
         picked3 = pick_values(3)
         y_codes.append(place([P, HALF], U32, "y_codes1", V_AT[3]))
         quantize(y_codes[1][:], y_bytes[:, HALF:], y_bf[1][:])
         multiply(2, EARLY)
-        v_late = [place([P, P, PACK], BF16, "v_late0", V_AT[3] + CELL), own([P, P, PACK], BF16, "v_late1")]
+        v_late = [place([P, P, PACK], BF16, "v_late0", V_AT[3] + CELL), place([P, P, PACK], BF16, "v_late1", C_AT)]
         turn_pairs([picked2], v_late[0][:], "turn2", nc.scalar.copy)
         turn_pairs([picked3], v_late[1][:], "turn0", nc.vector.tensor_copy)
-        mean_square(2, 0, EARLY)
-        early.append(own([P, 1], F32, "early_third"))
-        nc.gpsimd.tensor_scalar(early[1][:], parts[0][:, 2:3], EPS, None, ALU.add)
+        kept_squares = place([P, 2, 2 * P], BF16, "kept_squares", V_AT[3] + 2 * CELL)
+        for j in range(2):
+            nc.scalar.activation(kept_squares[:, j, :], kept[j][:], ACT.Square, scale=1.0 / math.sqrt(DV), accum_out=parts[0][:, j:j + 1])
+        nc.scalar.copy(kept[2][:], sums[2][:, EARLY])
         for e, cols in enumerate((THIRD, LAST)):
             quantize(v_codes[:, cols], v_bytes[:, cols], v_late[e][:])
             for j in range(2):
                 multiply(j, cols)
         multiply(2, slice(2 * P, DV))
         multiply(3, slice(0, DV))
+        early = [place([P, 2], F32, "early", C_AT), own([P, 1], F32, "early_third")]
+        nc.vector.tensor_scalar(early[0][:], parts[0][:, :2], EPS, None, ALU.add)
+        third_squares = own([P, 2 * P], F32, "third_squares")
+        nc.vector.scalar_tensor_tensor(third_squares[:], kept[2][:], 1.0 / DV, kept[2][:], ALU.mult, ALU.mult, accum_out=parts[0][:, 2:3])
+        nc.vector.tensor_scalar(early[1][:], parts[0][:, 2:3], EPS, None, ALU.add)
 
         rows = out[0].rearrange("(h m i) e -> h i m e", h=2, i=2)
         for j in range(Q_TILES):
@@ -231,11 +238,12 @@ def tile_attend_at_residsig_topk_kernel(tc, qT, k_words, k_scales, c_words, c_sc
             gain = own([P, 1], F32, "gain%d" % j)
             nc.scalar.activation(gain[:], parts[1][:, j:j + 1], ACT.Abs_reciprocal_sqrt, bias=early[j // 2][:, j % 2:j % 2 + 1] if j < 3 else EPS)
             result = own([P, DV], F32, "result%d" % j)
-            width = DV // 2 if j == 0 else DV
-            for first in range(0, DV, width):
-                cols = slice(first, first + width)
-                if j < Q_TILES - 1:
-                    nc.vector.tensor_scalar(result[:, cols], sums[j][:, cols], gain[:], None, ALU.mult)
-                else:
-                    nc.scalar.activation(result[:, cols], sums[j][:, cols], ACT.Copy, scale=gain[:])
-                nc.sync.dma_start(rows[j // 2, j % 2][:, cols], result[:, cols])
+            if j < Q_TILES - 1:
+                for cols, source in ((EARLY, kept[j][:]), (slice(2 * P, DV), sums[j][:, 2 * P:])):
+                    nc.vector.tensor_scalar(result[:, cols], source, gain[:], None, ALU.mult)
+                    if j == 0:
+                        nc.sync.dma_start(rows[0, 0][:, cols], result[:, cols])
+            else:
+                nc.scalar.activation(result[:], sums[j][:], ACT.Copy, scale=gain[:])
+            if j > 0:
+                nc.sync.dma_start(rows[j // 2, j % 2], result[:])

@@ -152,7 +152,7 @@ def tile_attend_at_residsig_topk_kernel(tc, qT, k_words, k_scales, c_words, c_sc
             copy(dst_words.rearrange("p (i c u) -> p i c u", i=len(tiles), u=2), turned[:].rearrange("p i u c -> p i c u"))
 
         def pick_values(e):
-            picked = own([P, 2, GROUPS, RUN], BF16, "picked%d" % e)
+            picked = place([P, 2, GROUPS, RUN], BF16, "picked3", K_AT + CELL) if e == 3 else own([P, 2, GROUPS, RUN], BF16, "picked%d" % e)
             nc.vector.tensor_copy(picked[:].rearrange("e u g r -> e g u r"), v_pool[e][:].indirect(offsets[:]))
             return picked
 
@@ -204,7 +204,7 @@ def tile_attend_at_residsig_topk_kernel(tc, qT, k_words, k_scales, c_words, c_sc
             nc.scalar.activation(squares[:, j, cols], sums[j][:, cols], ACT.Square, scale=1.0 / math.sqrt(DV),
                                  accum_out=parts[s][:, j:j + 1])
 
-        kept = [own([P, 2 * P], F32, "kept%d" % j) for j in range(3)]
+        kept = [own([P, 2 * P], F32, "kept%d" % j) for j in range(2)]
         for j in range(2):
             multiply(j, EARLY)
             nc.scalar.copy(kept[j][:], sums[j][:, EARLY])
@@ -215,17 +215,18 @@ def tile_attend_at_residsig_topk_kernel(tc, qT, k_words, k_scales, c_words, c_sc
         multiply(2, EARLY)
         v_late = [place([P, P, PACK], BF16, "v_late0", V_AT[3] + CELL), place([P, P, PACK], BF16, "v_late1", C_AT)]
         turn_pairs([picked2], v_late[0][:], "turn2", nc.scalar.copy)
-        turn_pairs([picked3], v_late[1][:], "turn0", nc.vector.tensor_copy)
-        kept_squares = place([P, 2, 2 * P], BF16, "kept_squares", V_AT[3] + 2 * CELL)
+        turn_pairs([picked3], v_late[1][:], "turn0", nc.scalar.copy)
+        kept_squares = place([P, 2, 2 * P], BF16, "kept_squares", K_AT + CELL)
         for j in range(2):
             nc.scalar.activation(kept_squares[:, j, :], kept[j][:], ACT.Square, scale=1.0 / math.sqrt(DV), accum_out=parts[0][:, j:j + 1])
-        nc.scalar.copy(kept[2][:], sums[2][:, EARLY])
         for e, cols in enumerate((THIRD, LAST)):
             quantize(v_codes[:, cols], v_bytes[:, cols], v_late[e][:])
             for j in range(2):
                 multiply(j, cols)
-        multiply(2, slice(2 * P, DV))
+        kept.append(place([P, 2 * P], F32, "kept2", C_AT + LINK))
+        nc.vector.tensor_copy(kept[2][:], sums[2][:, EARLY])
         multiply(3, slice(0, DV))
+        multiply(2, slice(2 * P, DV))
         early = [place([P, 2], F32, "early", C_AT), own([P, 1], F32, "early_third")]
         nc.vector.tensor_scalar(early[0][:], parts[0][:, :2], EPS, None, ALU.add)
         third_squares = own([P, 2 * P], F32, "third_squares")

@@ -115,7 +115,7 @@ def tile_attend_at_residsig_topk_kernel(tc, qT, k_words, k_scales, c_words, c_sc
         k_bytes = own([P, SLOTS], U8, "k_bytes")
         k_codes = [own([P, SLOTS // 2], U32, "k_codes0")]
         nc.vector.tensor_copy(k_bytes[:], k_scale_pool[:].indirect(offsets[:]))
-        us_rows = psum.tile([P, PACK, P], F32, name="us_rows")
+        us_rows = psum.tile([P, PACK, P], F32, name="us_rows", tag="us_rows")
         for t in range(PACK):
             nc.tensor.transpose(us_rows[:, t, :], us_col[:, t:t + 1].to_broadcast([P, P]), ident[:])
         nc.vector.tensor_copy(k_codes[0][:], k_pool[:].bitcast(U32).indirect(offsets[:, :16]))
@@ -208,6 +208,12 @@ def tile_attend_at_residsig_topk_kernel(tc, qT, k_words, k_scales, c_words, c_sc
         for j in range(2):
             multiply(j, EARLY)
             nc.scalar.copy(kept[j][:], sums[j][:, EARLY])
+
+        warm_sums = psum.tile([P, 2, 2 * P], F32, name="warm_sums", tag="us_rows")
+        for i in range(2):
+            nc.tensor.matmul_mx(out=warm_sums[:, i, :], lhsT=y_codes[0][:, i * P:(i + 1) * P].bitcast(FP8X4),
+                                lhsT_scale=y_bytes[:, i * P:(i + 1) * P], rhs=v_codes[:, EARLY].bitcast(FP8X4),
+                                rhs_scale=v_bytes[:, EARLY], start=True, stop=True)
 
         picked3 = pick_values(3)
         y_codes.append(place([P, HALF], U32, "y_codes1", V_AT[3]))

import math
from contextlib import ExitStack

import concourse.mybir as mybir

F32 = mybir.dt.float32
BF16 = mybir.dt.bfloat16
I32 = mybir.dt.int32
U32 = mybir.dt.uint32
U16 = mybir.dt.uint16
U8 = mybir.dt.uint8
FP8X4 = mybir.dt.float8_e4m3fn_x4
ACT = mybir.ActivationFunctionType
ALU = mybir.AluOpType

P = 128
PACK = 4
SLOTS = 512
TOKENS = 2048
QUERIES = 512
DV = 512
Q_TILES = QUERIES // P
V_TILES = DV // P
HALF = QUERIES // 2
GROUPS = SLOTS // 32
RUN = 16
EPS = 1e-05
SPREAD = 8
EARLY = slice(0, 2 * P)
THIRD = slice(2 * P, 3 * P)
LAST = slice(3 * P, DV)

LINK = 64
ROW_BYTES = 4 * TOKENS
CELL = 2048
K_AT = 0
C_AT = K_AT + ROW_BYTES
V_AT = [C_AT + (1 + e) * ROW_BYTES for e in range(V_TILES)]
Q_BF1_AT = V_AT[3] + ROW_BYTES
Y_BF0_AT = Q_BF1_AT + CELL
V_BF0_AT = Y_BF0_AT + CELL
WEIGHTS0_AT = V_BF0_AT + LINK
Q_BF0_AT = V_BF0_AT + 6 * CELL
Q_CODES_AT = Q_BF0_AT + CELL
US_AT = Q_CODES_AT + CELL // 2 - LINK
NEG_TH_AT = V_BF0_AT - LINK

FLOPS = 3 * 2 * 512 * 512 * 512


def tile_attend_at_residsig_topk_kernel(tc, qT, k_words, k_scales, c_words, c_scales, vT, th, us, offs, out):
    nc = tc.nc
    with ExitStack() as ctx:
        keep = ctx.enter_context(tc.tile_pool(name="keep", bufs=1))
        staged = ctx.enter_context(tc.tile_pool(name="staged", bufs=1))
        psum = ctx.enter_context(tc.psum_pool(name="psum", bufs=1))

        def place(shape, dtype, name, offset):
            return staged.tile(shape, dtype, name=name, offset=offset, align_bytes=64)

        def own(shape, dtype, name):
            return keep.tile(shape, dtype, name=name, align_bytes=64)

        offsets = keep.tile([P, SLOTS // 16], U16, name="offsets")
        c_scale_pool = place([P, TOKENS], U8, "c_scale_pool", V_AT[1] - LINK)
        k_scale_pool = place([P, TOKENS], U8, "k_scale_pool", V_AT[3] - LINK)
        c_bytes = own([P, SLOTS], U8, "c_bytes")
        minus_one = own([P, 1], F32, "minus_one")
        nc.gpsimd.memset(c_scale_pool[:].bitcast(I32), 0)
        nc.vector.memset(k_scale_pool[:].bitcast(I32), 0)
        nc.vector.memset(minus_one[:], -1.0)
        nc.vector.memset(c_bytes[:].bitcast(I32), 0)
        ident = own([P, P], F32, "ident")
        diagonal = own([P, P], F32, "diagonal")
        nc.gpsimd.iota(diagonal[:], pattern=[[1, P]], base=0, channel_multiplier=-1, allow_small_or_imprecise_dtypes=True)
        nc.gpsimd.tensor_scalar(ident[:], diagonal[:], 0.0, None, ALU.is_equal)
        warm_out = own([P, 1], F32, "warm_out")
        nc.scalar.activation(warm_out[:], minus_one[:], ACT.Sigmoid)

        q_raw = own([P, PACK, QUERIES], F32, "q_raw")
        nc.sync.dma_start(q_raw[:], qT[0].rearrange("(p t) q -> p t q", t=PACK))
        nc.sync.dma_start(offsets[:], offs)
        nc.sync.dma_start(c_scale_pool[0:P:SPREAD, :].bitcast(I32), c_scales[0].bitcast(I32))
        k_rows = k_scales[0].bitcast(I32).rearrange("(g r) n -> r g n", r=4)
        for r in range(4):
            nc.sync.dma_start(k_scale_pool[r:P:32, :].bitcast(I32), k_rows[r])
        k_pool = place([P, TOKENS], I32, "k_pool", K_AT)
        nc.sync.dma_start(k_pool[:], k_words[0].rearrange("p n t -> p (n t)").bitcast(I32))
        us_col = place([P, 2 * LINK // 4], F32, "us_col", US_AT)
        nc.sync.dma_start(us_col[:, :PACK], us[0].rearrange("(p t) o -> p (t o)", t=PACK))
        c_pool = place([P, TOKENS], I32, "c_pool", C_AT)
        nc.sync.dma_start(c_pool[:], c_words[0].rearrange("p n t -> p (n t)").bitcast(I32))
        th_col = own([P, 2, 2], F32, "th_col")
        nc.sync.dma_start(th_col[:], th[0, 0].rearrange("(h m i) -> m h i", h=2, i=2))
        neg_th = place([P, 2 * LINK // 4], F32, "neg_th", NEG_TH_AT)
        nc.gpsimd.tensor_scalar(neg_th[:, :Q_TILES], th_col[:].rearrange("m h i -> m (h i)"), minus_one[:], None, ALU.mult)

        q_bf = [place([P, HALF, PACK], BF16, "q_bf0", Q_BF0_AT), place([P, HALF, PACK], BF16, "q_bf1", Q_BF1_AT)]
        q_bytes = own([P, QUERIES], U8, "q_bytes")
        for h in range(2):
            nc.scalar.copy(q_bf[h][:].rearrange("p (i m n) t -> p m t n i", i=2, n=2),
                           q_raw[:, :, h * HALF:(h + 1) * HALF].rearrange("p t (m n i) -> p m t n i", n=2, i=2))

        def quantize(codes, scale_bytes, values):
            nc.vector.quantize_mx(out=codes.bitcast(FP8X4), scales=scale_bytes, in_=values.rearrange("p c t -> p (c t)"))

        c_picked = own([P, SLOTS], U8, "c_picked")
        nc.vector.tensor_copy(c_picked[:], c_scale_pool[:].indirect(offsets[:]))
        for r in range(4):
            nc.sync.dma_start(c_bytes[r:P:32, :].bitcast(I32), c_picked[SPREAD * r:P:32, :].bitcast(I32))
        v_pool = [place([P, TOKENS], F32, "v_pool%d" % e, V_AT[e]) for e in range(V_TILES)]
        for e in range(V_TILES):
            nc.sync.dma_start(v_pool[e][:], vT[e * P:(e + 1) * P, :])

        k_bytes = own([P, SLOTS], U8, "k_bytes")
        k_codes = [own([P, SLOTS // 2], U32, "k_codes0")]
        nc.vector.tensor_copy(k_bytes[:], k_scale_pool[:].indirect(offsets[:]))
        us_rows = psum.tile([P, PACK, P], F32, name="us_rows", tag="us_rows")
        for t in range(PACK):
            nc.tensor.transpose(us_rows[:, t, :], us_col[:, t:t + 1].to_broadcast([P, P]), ident[:])
        nc.vector.tensor_copy(k_codes[0][:], k_pool[:].bitcast(U32).indirect(offsets[:, :16]))
        q_codes = [place([P, HALF], U32, "q_codes%d" % h, Q_CODES_AT + h * CELL // 2) for h in range(2)]
        for h in range(2):
            quantize(q_codes[h][:], q_bytes[:, h * HALF:(h + 1) * HALF], q_bf[h][:])
        k_codes.append(place([P, SLOTS // 2], U32, "k_codes1", Q_BF0_AT))
        nc.vector.tensor_copy(k_codes[1][:], k_pool[:].bitcast(U32).indirect(offsets[:, 16:]))
        c_codes = place([P, SLOTS], U32, "c_codes", Q_BF1_AT)
        nc.vector.tensor_copy(c_codes[:], c_pool[:].bitcast(U32).indirect(offsets[:]))

        scores = [psum.tile([P, SLOTS], F32, name="score%d" % j, tag="rows%d" % j) for j in range(Q_TILES)]
        us_copy = own([P, SLOTS], F32, "us_copy")
        nc.scalar.copy(us_copy[:].rearrange("q (p t) -> q p t", t=PACK), us_rows[:].rearrange("q t p -> q p t"))

        def score_pass(j, codes, scale_rows, cols, first, last):
            nc.tensor.matmul_mx(out=scores[j][:, cols], lhsT=q_codes[j // 2][:, (j % 2) * P:(j % 2 + 1) * P].bitcast(FP8X4),
                                lhsT_scale=q_bytes[:, j * P:(j + 1) * P], rhs=codes[:].bitcast(FP8X4), rhs_scale=scale_rows[:, cols],
                                start=first, stop=last)

        for s in range(2):
            for j in range(Q_TILES):
                score_pass(j, k_codes[s], k_bytes, slice(s * HALF, (s + 1) * HALF), s == 0, False)
        for j in range(Q_TILES):
            score_pass(j, c_codes, c_bytes, slice(0, SLOTS), False, True)

        def turn_pairs(tiles, dst, bank, copy):
            turned = psum.tile([P, len(tiles), 2, P], F32, name="turned", tag=bank)
            for i, pairs in enumerate(tiles):
                words = pairs[:].rearrange("c u g r -> c (u g r)").bitcast(F32)
                for u in range(2):
                    nc.tensor.transpose(turned[:, i, u, :], words[:, u * P:(u + 1) * P], ident[:])
            dst_words = dst.rearrange("p c t -> p (c t)").bitcast(F32)
            copy(dst_words.rearrange("p (i c u) -> p i c u", i=len(tiles), u=2), turned[:].rearrange("p i u c -> p i c u"))

        def pick_values(e):
            picked = place([P, 2, GROUPS, RUN], BF16, "picked3", K_AT + CELL) if e == 3 else own([P, 2, GROUPS, RUN], BF16, "picked%d" % e)
            nc.vector.tensor_copy(picked[:].rearrange("e u g r -> e g u r"), v_pool[e][:].indirect(offsets[:]))
            return picked

        sig = [own([P, SLOTS], F32, "sig%d" % j) for j in range(Q_TILES)]
        for j in range(Q_TILES):
            nc.scalar.activation(sig[j][:], scores[j][:], ACT.Sigmoid, bias=neg_th[:, j:j + 1])

        def weigh(j):
            if j % 2 == 1:
                y = place([P, 2, GROUPS, RUN], BF16, "weights%d" % j, V_AT[j // 2])
                nc.vector.tensor_tensor(y[:].rearrange("q u g (a t) -> q g u a t", t=PACK),
                                        sig[j][:].rearrange("q (g u a t) -> q g u a t", u=2, a=RUN // PACK, t=PACK),
                                        us_rows[:].rearrange("q t (g u a) -> q g u a t", u=2, a=RUN // PACK), ALU.mult)
            else:
                y = own([P, 2, GROUPS, RUN], BF16, "weights2") if j else place([P, 2, GROUPS, RUN], BF16, "weights0", WEIGHTS0_AT)
                nc.gpsimd.tensor_tensor(y[:].rearrange("q u g r -> q g u r"), sig[j][:].rearrange("q (g u r) -> q g u r", u=2, r=RUN),
                                        us_copy[:].rearrange("q (g u r) -> q g u r", u=2, r=RUN), ALU.mult)
            return y

        picked0 = pick_values(0)
        weights = [weigh(j) for j in range(3)]
        picked1 = pick_values(1)
        weights.append(weigh(3))
        v_early = place([P, 2 * P, PACK], BF16, "v_early", WEIGHTS0_AT)
        y_bf = [place([P, 2 * P, PACK], BF16, "y_bf0", Y_BF0_AT), own([P, 2 * P, PACK], BF16, "y_bf1")]
        turn_pairs(weights[:2], y_bf[0][:], "turn0", nc.scalar.copy)
        turn_pairs([picked0, picked1], v_early[:], "turn1", nc.scalar.copy)
        switch_out = own([P, 1], F32, "switch_out")
        nc.scalar.activation(switch_out[:], v_early[:, 2 * P - 1, 0:1], ACT.Abs_reciprocal_sqrt, bias=1.0, scale=0.0)
        turn_pairs(weights[2:], y_bf[1][:], "turn1", nc.scalar.copy)
        y_bytes = own([P, QUERIES], U8, "y_bytes")
        v_bytes = own([P, DV], U8, "v_bytes")
        y_codes = [place([P, HALF], U32, "y_codes0", V_AT[1] + CELL)]
        v_codes = own([P, DV], U32, "v_codes")
        quantize(y_codes[0][:], y_bytes[:, :HALF], y_bf[0][:])
        quantize(v_codes[:, EARLY], v_bytes[:, EARLY], v_early[:])
        picked2 = pick_values(2)

        sums = [psum.tile([P, DV], F32, name="sum%d" % j, tag="rows%d" % j) for j in range(Q_TILES)]
        squares = own([P, Q_TILES, DV], F32, "squares")
        parts = [own([P, Q_TILES], F32, "part%d" % s) for s in range(2)]

        def multiply(j, cols):
            nc.tensor.matmul_mx(out=sums[j][:, cols], lhsT=y_codes[j // 2][:, (j % 2) * P:(j % 2 + 1) * P].bitcast(FP8X4),
                                lhsT_scale=y_bytes[:, j * P:(j + 1) * P], rhs=v_codes[:, cols].bitcast(FP8X4),
                                rhs_scale=v_bytes[:, cols], start=True, stop=True)

        def mean_square(j, s, cols):
            nc.scalar.activation(squares[:, j, cols], sums[j][:, cols], ACT.Square, scale=1.0 / math.sqrt(DV),
                                 accum_out=parts[s][:, j:j + 1])

        kept = [own([P, 2 * P], F32, "kept%d" % j) for j in range(2)]
        for j in range(2):
            multiply(j, EARLY)
            nc.scalar.copy(kept[j][:], sums[j][:, EARLY])

        warm_sums = psum.tile([P, 2, 2 * P], F32, name="warm_sums", tag="us_rows")
        for i in range(2):
            nc.tensor.matmul_mx(out=warm_sums[:, i, :], lhsT=y_codes[0][:, i * P:(i + 1) * P].bitcast(FP8X4),
                                lhsT_scale=y_bytes[:, i * P:(i + 1) * P], rhs=v_codes[:, EARLY].bitcast(FP8X4),
                                rhs_scale=v_bytes[:, EARLY], start=True, stop=True)

        picked3 = pick_values(3)
        y_codes.append(place([P, HALF], U32, "y_codes1", V_AT[3]))
        quantize(y_codes[1][:], y_bytes[:, HALF:], y_bf[1][:])
        multiply(2, EARLY)
        v_late = [place([P, P, PACK], BF16, "v_late0", V_AT[3] + CELL), place([P, P, PACK], BF16, "v_late1", C_AT)]
        turn_pairs([picked2], v_late[0][:], "turn2", nc.scalar.copy)
        turn_pairs([picked3], v_late[1][:], "turn0", nc.scalar.copy)
        kept_squares = place([P, 2, 2 * P], BF16, "kept_squares", K_AT + CELL)
        for j in range(2):
            nc.scalar.activation(kept_squares[:, j, :], kept[j][:], ACT.Square, scale=1.0 / math.sqrt(DV), accum_out=parts[0][:, j:j + 1])
        for e, cols in enumerate((THIRD, LAST)):
            quantize(v_codes[:, cols], v_bytes[:, cols], v_late[e][:])
            for j in range(2):
                multiply(j, cols)
        kept.append(place([P, 2 * P], F32, "kept2", C_AT + LINK))
        nc.vector.tensor_copy(kept[2][:], sums[2][:, EARLY])
        multiply(3, slice(0, DV))
        multiply(2, slice(2 * P, DV))
        early = [place([P, 2], F32, "early", C_AT), own([P, 1], F32, "early_third")]
        nc.vector.tensor_scalar(early[0][:], parts[0][:, :2], EPS, None, ALU.add)
        third_squares = own([P, 2 * P], F32, "third_squares")
        nc.vector.scalar_tensor_tensor(third_squares[:], kept[2][:], 1.0 / DV, kept[2][:], ALU.mult, ALU.mult, accum_out=parts[0][:, 2:3])
        nc.vector.tensor_scalar(early[1][:], parts[0][:, 2:3], EPS, None, ALU.add)

        rows = out[0].rearrange("(h m i) e -> h i m e", h=2, i=2)
        for j in range(Q_TILES):
            mean_square(j, 1, slice(2 * P if j < 3 else 0, DV))
            gain = own([P, 1], F32, "gain%d" % j)
            nc.scalar.activation(gain[:], parts[1][:, j:j + 1], ACT.Abs_reciprocal_sqrt, bias=early[j // 2][:, j % 2:j % 2 + 1] if j < 3 else EPS)
            result = own([P, DV], F32, "result%d" % j)
            if j < Q_TILES - 1:
                for cols, source in ((EARLY, kept[j][:]), (slice(2 * P, DV), sums[j][:, 2 * P:])):
                    nc.vector.tensor_scalar(result[:, cols], source, gain[:], None, ALU.mult)
                    if j == 0:
                        nc.sync.dma_start(rows[0, 0][:, cols], result[:, cols])
            else:
                nc.scalar.activation(result[:], sums[j][:], ACT.Copy, scale=gain[:])
            if j > 0:
                nc.sync.dma_start(rows[j // 2, j % 2], result[:])
